import numpy as np
import ml_dtypes


def mxq(x, axis, fmt="e4m3"):
    dtype, down = {"e4m3": (ml_dtypes.float8_e4m3fn, 7), "e5m2": (ml_dtypes.float8_e5m2, 14)}[fmt]
    v = np.moveaxis(np.asarray(x, np.float32).astype(ml_dtypes.bfloat16).astype(np.float64), axis, -1)
    blocks = v.reshape(v.shape[:-1] + (-1, 32))
    amax = np.abs(blocks).max(-1, keepdims=True)
    byte = np.maximum(np.where(amax > 0, np.frexp(amax)[1] - 1 + 127, 0) - down, 1)
    scale = np.exp2(byte - 127.0)
    codes = (blocks / scale).astype(np.float32).astype(dtype).astype(np.float64)
    return np.moveaxis((codes * scale).reshape(v.shape), -1, axis)


WIDE = False


def mx_kscale(k):
    if not WIDE:
        return np.ones(k)
    levels = np.array([10, -10, 5, -5, 0])
    if k % 512:
        return np.exp2(np.random.permutation(np.resize(levels, k // 32))).repeat(32)
    a = np.empty((k // 512, 16))
    for p in range(k // 512):
        a[p, :8] = np.random.permutation(np.resize(levels, 8))
        for g in range(8):
            far = levels[np.abs(levels - a[p, g]) >= 10]
            a[p, g + 8] = far[np.random.randint(len(far))]
    return np.exp2(a.ravel()).repeat(32)


def f64(x):
    return np.asarray(x).astype(np.float64)


def striped(idx):
    return np.tile(idx.reshape(-1, 16).T, (8, 1)).astype(np.uint16)


def unstriped(offs):
    return offs[:16].T.reshape(-1).astype(np.int64)


E2M1 = np.array([0.0, 0.5, 1.0, 1.5, 2.0, 3.0, 4.0, 6.0, -0.0, -0.5, -1.0, -1.5, -2.0, -3.0, -4.0, -6.0])


def pack_weight(w, fmt):
    k, n = w.shape
    w = f64(np.asarray(w, np.float32).astype(ml_dtypes.bfloat16)).reshape(k // 32, 32, n)
    amax = np.abs(w).max(1)
    if fmt == "e4m3":
        byte = np.frexp(amax)[1] - 1 + 127 - 7
    else:
        mant, ex = np.frexp(amax / 6.0)
        byte = np.where(mant > 0.5, ex, ex - 1) + 127
    byte = np.clip(np.where(amax > 0, byte, 1), 1, 254)
    scaled = (w * np.exp2(127.0 - byte)[:, None, :]).reshape(k, n).astype(np.float32)
    by_word = np.ascontiguousarray(scaled.reshape(k // 512, 128, 4, n).transpose(0, 1, 3, 2))
    if fmt == "e4m3":
        words = by_word.astype(ml_dtypes.float8_e4m3fn).view(np.uint8)
    else:
        c = by_word.astype(ml_dtypes.float4_e2m1fn).view(np.uint8) & 0xF
        words = (c[..., 0::2] | (c[..., 1::2] << 4)).reshape(k // 512, 128, 2 * n)
    return np.ascontiguousarray(words), np.ascontiguousarray(byte.astype(np.uint8).reshape(k // 512, 16, n))


def unpack_weight(words, scales, fmt):
    g, _, n = scales.shape
    words = np.ascontiguousarray(words).reshape(g, 128, n, -1)
    if fmt == "e4m3":
        vals = words.view(ml_dtypes.float8_e4m3fn).astype(np.float64)
    else:
        nib = np.empty((g, 128, n, 4), np.uint8)
        nib[..., 0::2] = words & 0xF
        nib[..., 1::2] = words >> 4
        vals = E2M1[nib]
    vals = vals * np.repeat(np.exp2(scales.astype(np.float64) - 127.0), 8, axis=1)[..., None]
    return vals.transpose(0, 1, 3, 2).reshape(g * 512, n)


def gelu(v):
    return 0.5 * v * (1.0 + np.tanh(np.sqrt(2.0 / np.pi) * (v + 0.044715 * v**3)))


K, T, S, H, N = 1024, 4096, 1024, 512, 256

def setup_inputs():
    n = np.random.standard_normal
    s = mx_kscale(K)[:, None]
    u = mx_kscale(H)[:, None]
    root = np.sqrt(u).T
    tab_words, tab_scales = pack_weight(n((K, T)) * s, "e4m3")
    wu = n((K, H)) / np.sqrt(K) / s * root
    wi_words, wi_scales = pack_weight(n((K, H)) / np.sqrt(K) / s * root, "e4m3")
    wc_words, wc_scales = pack_weight(n((K, H)) / np.sqrt(K) / s * root, "e2m1")
    wr = n((H, N)) / np.sqrt(H) / u
    return {"tab_words": tab_words, "tab_scales": tab_scales,
            "offs": striped(np.random.permutation(T)[:S]),
            "offs2": striped(np.random.permutation(T)[:S]),
            "offs3": striped(np.random.permutation(T)[:S]),
            "wu": wu.astype(np.float32),
            "wi_words": wi_words, "wi_scales": wi_scales,
            "wc_words": wc_words, "wc_scales": wc_scales,
            "wr": wr.astype(np.float32), "bias": n(N).astype(np.float32)}

def reference(tab_words, tab_scales, offs, offs2, offs3, wu, wi_words, wi_scales, wc_words, wc_scales, wr, bias):
    vu = unpack_weight(tab_words, tab_scales, "e4m3")[:, unstriped(offs)]
    vi = unpack_weight(tab_words, tab_scales, "e4m3")[:, unstriped(offs2)]
    vc = unpack_weight(tab_words, tab_scales, "e4m3")[:, unstriped(offs3)]
    wi = unpack_weight(wi_words, wi_scales, "e4m3")
    wc = unpack_weight(wc_words, wc_scales, "e2m1")
    a = mxq(f64(wu), 0, "e4m3").T @ vu
    b = wi.T @ vi
    c = wc.T @ vc
    h = a * (b + c) + b * c
    y = mxq(f64(wr), 0, "e4m3").T @ mxq(h, 0, "e4m3")
    return y + f64(bias)[:, None]

@@ -1,0 +1,253 @@
+from contextlib import ExitStack
+
+import concourse.mybir as mybir
+from concourse.masks import make_identity
+
+K, T, S, H, N = 1024, 4096, 1024, 512, 256
+FLOPS = 2 * (3 * K * H * S + H * N * S)
+
+F32 = mybir.dt.float32
+BF16 = mybir.dt.bfloat16
+I32 = mybir.dt.int32
+U32 = mybir.dt.uint32
+U16 = mybir.dt.uint16
+U8 = mybir.dt.uint8
+FP8X4 = mybir.dt.float8_e4m3fn_x4
+FP4X4 = mybir.dt.float4_e2m1fn_x4
+ADD = mybir.AluOpType.add
+MULT = mybir.AluOpType.mult
+IDENT = mybir.ActivationFunctionType.Identity
+
+P = 128
+PASSES = K // 512
+CHUNK = 512
+CHUNKS = S // CHUNK
+TILES = S // P
+TPC = CHUNK // P
+LOADS = "lc lb la t0 t1 t2 t3 W0 W1 s wi wc wu0 wu1 wu2 wu3 wr"
+ORDER = "Sc Sb Sa Wa00 Wb00 i3 Wb10 Wc01 Wc10 Wc00 B0 Wb01 B1 i1 i0 U1 B2 i2 U2 Wb11 B3 Wc11 ir U0 U3 Wa10 A0 T0 A1 A2 A3 T1 Wa01 B4 T2 T3 Wa11 B5 A4 A5 B6 Ur B7 T4 T5 Y01 A6 T6 A7 Y45 Y23 T7 Y6 Y7"
+TIE = {"0":0,"1":1,"2":2,"r":3}
+IL_POOL = []
+GP = []
+GS = []
+NPROD, NH, NY = 5, 2, 1
+
+
+def tile_list_fm_rating_kernel(
+    tc, tab_words, tab_scales, offs, offs2, offs3, wu, wi_words, wi_scales, wc_words, wc_scales, wr, bias, out
+):
+    nc = tc.nc
+    with ExitStack() as ctx:
+        keep = ctx.enter_context(tc.tile_pool(name="keep", bufs=1))
+        psum = ctx.enter_context(tc.psum_pool(name="psum", bufs=1))
+
+        lists = {}
+        for name in ("c", "b", "a"):
+            lists[name] = keep.tile([P, S // 16], U16, name="list_" + name)
+        tab_sc = keep.tile([P, T], U8, align_bytes=64)
+        w_sc = keep.tile([P, 3, H], U8, align_bytes=64)
+        c1_sc = keep.tile([P, S], U8, align_bytes=64)
+        nc.vector.memset(tab_sc[:].bitcast(I32), 0)
+        nc.vector.memset(w_sc[:].rearrange("p a e -> p (a e)").bitcast(I32), 0)
+        nc.vector.memset(c1_sc[:].bitcast(I32), 0)
+
+        tab_w = [keep.tile([P, T], I32, name="tab_w%d" % a) for a in range(PASSES)]
+        wi_w = keep.tile([P, PASSES, H], I32, align_bytes=64)
+        wc_w = keep.tile([P, PASSES, 2 * H], U8, align_bytes=64)
+        bias_sb = keep.tile([P, 2], F32)
+        wr_raw = keep.tile([P, 4, N], F32)
+        HALF = H // 2
+        wu_raw = [keep.tile([P, 4, HALF], F32, name="wu_raw%d" % u) for u in range(4)]
+        srcs = {"a": offs, "b": offs2, "c": offs3}
+        for x in LOADS.split():
+            if x[0] == "l":
+                nc.sync.dma_start(lists[x[1]][:], srcs[x[1]])
+            elif x[0] == "t":
+                q = int(x[1])
+                nc.sync.dma_start(
+                    tab_sc[32 * q : 32 * q + 8, :].bitcast(I32), tab_scales[:, 4 * q : 4 * q + 4, :].bitcast(I32)
+                )
+            elif x[0] == "r":
+                a, r = int(x[1]), int(x[2])
+                nc.sync.dma_start(tab_sc[4 * a + r : P : 32, :].bitcast(I32), tab_scales[a, r:16:4, :].bitcast(I32))
+            elif x[0] == "W":
+                a = int(x[1])
+                nc.sync.dma_start(tab_w[a][:], tab_words[a].rearrange("p t i -> p (t i)").bitcast(I32))
+            elif x == "wi":
+                nc.sync.dma_start(wi_w[:], wi_words.rearrange("a p e i -> p a (e i)").bitcast(I32))
+            elif x == "wc":
+                nc.sync.dma_start(wc_w[:].bitcast(I32), wc_words.rearrange("a p e -> p a e").bitcast(I32))
+            elif x == "s":
+                for q in range(4):
+                    nc.sync.dma_start(
+                        w_sc[32 * q : 32 * q + 8, 0, :].bitcast(I32), wi_scales[:, 4 * q : 4 * q + 4, :].bitcast(I32)
+                    )
+            elif x == "wr":
+                nc.sync.dma_start(wr_raw[:], wr.rearrange("(p j) n -> p j n", j=4))
+            else:
+                u = int(x[2])
+                a, c0 = u // 2, HALF * (u % 2)
+                nc.sync.dma_start(
+                    wu_raw[u][:], wu[512 * a : 512 * (a + 1), c0 : c0 + HALF].rearrange("(p j) e -> p j e", j=4)
+                )
+        for q in range(4):
+            nc.gpsimd.dma_start(
+                w_sc[32 * q : 32 * q + 4, 1:3, :].bitcast(I32),
+                wc_scales[:, 4 * q : 4 * q + 4, :].rearrange("a r e -> r a e").bitcast(I32),
+            )
+        with nc.allow_non_contiguous_dma(reason="one bias value a partition"):
+            nc.sync.dma_start(bias_sb[:], bias.rearrange("(h p) -> p h", p=P))
+
+        ident = keep.tile([P, P], F32)
+        make_identity(nc, ident[:])
+        warm = keep.tile([P, 1], F32)
+        nc.scalar.activation(warm[:], ident[:, 0:1], IDENT)
+
+        sc = {}
+        for name in ("c", "b", "a"):
+            sc[name] = keep.tile([P, S], U8, name="sc_" + name, align_bytes=64)
+        words = {}
+
+        def gather_scales(name):
+            nc.vector.tensor_copy(sc[name][:], tab_sc[:].indirect(lists[name][:]))
+
+        def gather_words(name, a, ch):
+            words[name, a, ch] = keep.tile([P, CHUNK], U32, name="w_%s%d%d" % (name, a, ch), align_bytes=64)
+            cols = CHUNK // 16
+            nc.vector.tensor_copy(
+                words[name, a, ch][:], tab_w[a][:].bitcast(U32).indirect(lists[name][:, cols * ch : cols * (ch + 1)])
+            )
+
+        wu_w = keep.tile([P, PASSES, H], U32, align_bytes=64)
+        wu_sc = keep.tile([P, PASSES, H], U8, align_bytes=64)
+        wr_w = keep.tile([P, N], U32, align_bytes=64)
+        wr_sc = keep.tile([P, N], U8, align_bytes=64)
+        w_bf = {}
+
+        def interleave(u):
+            src = wr_raw if u == "r" else wu_raw[int(u)]
+            tag = "b_sb%d" % TIE[u] if u in TIE else "w_bf" + u
+            w_bf[u] = keep.tile([P, HALF, 4], BF16, name="w_bf" + u, tag=tag, align_bytes=64)
+            dst_v = w_bf[u][:].rearrange("p (c i) t -> p c t i", i=4)
+            src_v = src[:].rearrange("p t (c i) -> p c t i", i=4)
+            if u in IL_POOL:
+                nc.gpsimd.tensor_scalar(dst_v, src_v, 1.0, 0.0, MULT, ADD)
+            else:
+                nc.scalar.copy(dst_v, src_v)
+
+        def quantize_weight(u):
+            src = w_bf[u][:].rearrange("p e t -> p (e t)")
+            if u == "r":
+                nc.vector.quantize_mx(wr_w[:].bitcast(FP8X4), wr_sc[:], src)
+            else:
+                a, c0 = int(u) // 2, HALF * (int(u) % 2)
+                nc.vector.quantize_mx(wu_w[:, a, c0 : c0 + HALF].bitcast(FP8X4), wu_sc[:, a, c0 : c0 + HALF], src)
+
+        def project(name, j):
+            ch, c0 = j // TPC, (j % TPC) * P
+            bank = psum.tile([P, H], F32, tag="prod", bufs=NPROD, name="bank")
+            cols = slice(j * P, (j + 1) * P)
+            for a in range(PASSES):
+                if name == "a":
+                    rhs, rhs_sc, lhs_sc = wu_w[:, a, :].bitcast(FP8X4), wu_sc[:, a, :], sc[name][4 * a :, cols]
+                elif name == "b":
+                    rhs, rhs_sc, lhs_sc = wi_w[:, a, :].bitcast(FP8X4), w_sc[4 * a :, 0, :], sc[name][4 * a :, cols]
+                else:
+                    rhs, rhs_sc = wc_w[:, a, :].bitcast(FP4X4), w_sc[:, 1 + a, :]
+                    lhs_sc = (sc["c"], c1_sc)[a][:, cols]
+                nc.tensor.matmul_mx(
+                    bank[:],
+                    lhsT=words[name, a, ch][:, c0 : c0 + P].bitcast(FP8X4),
+                    lhsT_scale=lhs_sc,
+                    rhs=rhs,
+                    rhs_scale=rhs_sc,
+                    start=(a == 0),
+                    stop=(a == PASSES - 1),
+                )
+            return bank[:].rearrange("p (m t) -> p t m", t=4)
+
+        s_sb, p_sb, q_sb, h_bf = {}, {}, {}, {}
+
+        def pair_bc(j):
+            b_ps = project("b", j)
+            c_ps = project("c", j)
+            b_sb = keep.tile([P, 4, P], F32, name="b_sb", tag="b_sb%d" % j, align_bytes=64)
+            nc.scalar.copy(b_sb[:], b_ps)
+            s_sb[j] = keep.tile([P, 4, P], F32, name="s%d" % j)
+            p_sb[j] = keep.tile([P, 4, P], F32, name="p%d" % j)
+            if j in GP:
+                c_sb = keep.tile([P, 4, P], F32, name="c_sb%d" % j)
+                nc.scalar.copy(c_sb[:], c_ps)
+                if j in GS:
+                    nc.gpsimd.tensor_tensor(s_sb[j][:], c_sb[:], b_sb[:], ADD)
+                else:
+                    nc.vector.tensor_tensor(s_sb[j][:], c_ps, b_sb[:], ADD)
+                nc.gpsimd.tensor_tensor(p_sb[j][:], c_sb[:], b_sb[:], MULT)
+            else:
+                nc.vector.tensor_tensor(s_sb[j][:], c_ps, b_sb[:], ADD)
+                nc.vector.tensor_tensor(p_sb[j][:], c_ps, b_sb[:], MULT)
+
+        out_v = out.rearrange("(h p) j -> p h j", p=P)
+
+        def times_a(j):
+            a_ps = project("a", j)
+            q_sb[j] = keep.tile([P, 4, P], F32, name="q%d" % j)
+            nc.vector.tensor_tensor(q_sb[j][:], a_ps, s_sb[j][:], MULT)
+
+        group_of = {}
+        for x in ORDER.split():
+            if x[0] == "Y":
+                for z in x[1:]:
+                    group_of[int(z)] = x[1:]
+
+        def turn(j):
+            h_ps = psum.tile([P, 4, P], F32, tag="h", bufs=NH, name="h_ps")
+            for t in range(4):
+                nc.tensor.matmul(h_ps[:, t, :], p_sb[j][:, t, :], ident[:], start=True, stop=False, is_transpose=True)
+                nc.tensor.matmul(h_ps[:, t, :], q_sb[j][:, t, :], ident[:], start=False, stop=True, is_transpose=True)
+            g = group_of[j]
+            if g not in h_bf:
+                h_bf[g] = keep.tile([P, len(g) * P, 4], BF16, name="h_bf" + g, align_bytes=64)
+            c0 = (j - int(g[0])) * P
+            nc.scalar.copy(h_bf[g][:, c0 : c0 + P, :], h_ps[:].rearrange("p t j -> p j t"))
+
+        def rate(g):
+            w, j0 = len(g) * P, int(g[0]) * P
+            h_w = keep.tile([P, w], U32, name="h_w" + g, align_bytes=64)
+            h_sc = keep.tile([P, w], U8, name="h_sc" + g, align_bytes=64)
+            nc.vector.quantize_mx(h_w[:].bitcast(FP8X4), h_sc[:], h_bf[g][:].rearrange("p j t -> p (j t)"))
+            y_ps = psum.tile([P, 2, w], F32, tag="y", bufs=NY, name="y_ps")
+            y_sb = keep.tile([P, 2, w], F32, name="y_sb" + g)
+            for h in range(2):
+                nc.tensor.matmul_mx(
+                    y_ps[:, h, :],
+                    lhsT=wr_w[:, h * P : (h + 1) * P].bitcast(FP8X4),
+                    lhsT_scale=wr_sc[:, h * P : (h + 1) * P],
+                    rhs=h_w[:].bitcast(FP8X4),
+                    rhs_scale=h_sc[:],
+                    start=True,
+                    stop=True,
+                )
+            for h in range(2):
+                nc.scalar.activation(y_sb[:, h, :], y_ps[:, h, :], IDENT, bias=bias_sb[:, h : h + 1])
+            nc.sync.dma_start(out_v[:, :, j0 : j0 + w], y_sb[:])
+
+        for x in ORDER.split():
+            if x[0] == "S":
+                gather_scales(x[1])
+                if x[1] == "c":
+                    nc.gpsimd.dma_start(c1_sc[0:100, :].bitcast(I32), sc["c"][4:104, :].bitcast(I32))
+            elif x[0] == "W":
+                gather_words(x[1], int(x[2]), int(x[3]))
+            elif x[0] == "i":
+                interleave(x[1])
+            elif x[0] == "U":
+                quantize_weight(x[1])
+            elif x[0] == "B":
+                pair_bc(int(x[1]))
+            elif x[0] == "A":
+                times_a(int(x[1]))
+            elif x[0] == "T":
+                turn(int(x[1]))
+            else:
+                rate(x[1:])

@@ -24,13 +24,13 @@ CHUNK = 512
 CHUNKS = S // CHUNK
 TILES = S // P
 TPC = CHUNK // P
-LOADS = "lc lb la t0 t1 t2 t3 W0 W1 s wi wc wu0 wu1 wu2 wu3 wr"
-ORDER = "Sc Sb Sa Wa00 Wb00 i3 Wb10 Wc01 Wc10 Wc00 B0 Wb01 B1 i1 i0 U1 B2 i2 U2 Wb11 B3 Wc11 ir U0 U3 Wa10 A0 T0 A1 A2 A3 T1 Wa01 B4 T2 T3 Wa11 B5 A4 A5 B6 Ur B7 T4 T5 Y01 A6 T6 A7 Y45 Y23 T7 Y6 Y7"
-TIE = {"0":0,"1":1,"2":2,"r":3}
+LOADS = "lc t0 t1 t2 t3 lb la W0 W1a s0 s1 s2 s3 s4 W1b s5 s6 s7 wi wc wu0 wu1 wu2 wu3 wr"
+ORDER = "Sc Sb Sa Wc00 Wb00 Wb01 i0 Wb11 Wb10 Wc10 B0 i1 i3 Wa00 i2 U1 Wa10 U0 U2 B1 U3 B2 A0 Wc11 A1 A2 Wc01 B3 Wa01 ir A3 B4 T0 T1 Wa11 Ur T2 B5 T3 A4 A5 B6 B7 Y01 T4 Y23 A6 T5 A7 T6 T7 Y45 Y6 Y7"
+TIE = {"1":0,"2":0,"3":0,"r":1}
 IL_POOL = []
 GP = []
 GS = []
-NPROD, NH, NY = 5, 2, 1
+NPROD, NH, NY = 4, 2, 2
 
 
 def tile_list_fm_rating_kernel(
@@ -72,15 +72,22 @@ def tile_list_fm_rating_kernel(
                 nc.sync.dma_start(tab_sc[4 * a + r : P : 32, :].bitcast(I32), tab_scales[a, r:16:4, :].bitcast(I32))
             elif x[0] == "W":
                 a = int(x[1])
-                nc.sync.dma_start(tab_w[a][:], tab_words[a].rearrange("p t i -> p (t i)").bitcast(I32))
+                cols = {"": slice(0, T), "a": slice(0, T // 2), "b": slice(T // 2, T)}[x[2:]]
+                nc.sync.dma_start(tab_w[a][:, cols], tab_words[a].rearrange("p t i -> p (t i)").bitcast(I32)[:, cols])
             elif x == "wi":
                 nc.sync.dma_start(wi_w[:], wi_words.rearrange("a p e i -> p a (e i)").bitcast(I32))
             elif x == "wc":
                 nc.sync.dma_start(wc_w[:].bitcast(I32), wc_words.rearrange("a p e -> p a e").bitcast(I32))
-            elif x == "s":
-                for q in range(4):
+            elif x[0] == "s":
+                q = int(x[1]) % 4
+                if int(x[1]) < 4:
                     nc.sync.dma_start(
                         w_sc[32 * q : 32 * q + 8, 0, :].bitcast(I32), wi_scales[:, 4 * q : 4 * q + 4, :].bitcast(I32)
+                    )
+                else:
+                    nc.sync.dma_start(
+                        w_sc[32 * q : 32 * q + 4, 1:3, :].bitcast(I32),
+                        wc_scales[:, 4 * q : 4 * q + 4, :].rearrange("a r e -> r a e").bitcast(I32),
                     )
             elif x == "wr":
                 nc.sync.dma_start(wr_raw[:], wr.rearrange("(p j) n -> p j n", j=4))
@@ -90,11 +97,6 @@ def tile_list_fm_rating_kernel(
                 nc.sync.dma_start(
                     wu_raw[u][:], wu[512 * a : 512 * (a + 1), c0 : c0 + HALF].rearrange("(p j) e -> p j e", j=4)
                 )
-        for q in range(4):
-            nc.gpsimd.dma_start(
-                w_sc[32 * q : 32 * q + 4, 1:3, :].bitcast(I32),
-                wc_scales[:, 4 * q : 4 * q + 4, :].rearrange("a r e -> r a e").bitcast(I32),
-            )
         with nc.allow_non_contiguous_dma(reason="one bias value a partition"):
             nc.sync.dma_start(bias_sb[:], bias.rearrange("(h p) -> p h", p=P))
 
@@ -126,9 +128,13 @@ def tile_list_fm_rating_kernel(
 
         def interleave(u):
             src = wr_raw if u == "r" else wu_raw[int(u)]
-            tag = "b_sb%d" % TIE[u] if u in TIE else "w_bf" + u
-            w_bf[u] = keep.tile([P, HALF, 4], BF16, name="w_bf" + u, tag=tag, align_bytes=64)
-            dst_v = w_bf[u][:].rearrange("p (c i) t -> p c t i", i=4)
+            if u not in w_bf:
+                mates = [v for v in TIE if TIE[v] == TIE[u]] if u in TIE else [u]
+                tag = "b_sb%d" % TIE[u] if u in TIE else "w_bf" + u
+                held = keep.tile([P, len(mates), HALF, 4], BF16, name="w_bf" + u, tag=tag, align_bytes=64)
+                for n, v in enumerate(mates):
+                    w_bf[v] = held[:, n, :, :]
+            dst_v = w_bf[u].rearrange("p (c i) t -> p c t i", i=4)
             src_v = src[:].rearrange("p t (c i) -> p c t i", i=4)
             if u in IL_POOL:
                 nc.gpsimd.tensor_scalar(dst_v, src_v, 1.0, 0.0, MULT, ADD)
@@ -136,7 +142,7 @@ def tile_list_fm_rating_kernel(
                 nc.scalar.copy(dst_v, src_v)
 
         def quantize_weight(u):
-            src = w_bf[u][:].rearrange("p e t -> p (e t)")
+            src = w_bf[u].rearrange("p e t -> p (e t)")
             if u == "r":
                 nc.vector.quantize_mx(wr_w[:].bitcast(FP8X4), wr_sc[:], src)
             else:
@@ -236,7 +242,7 @@ def tile_list_fm_rating_kernel(
             if x[0] == "S":
                 gather_scales(x[1])
                 if x[1] == "c":
-                    nc.gpsimd.dma_start(c1_sc[0:100, :].bitcast(I32), sc["c"][4:104, :].bitcast(I32))
+                    nc.scalar.dma_start(c1_sc[0:100, :].bitcast(I32), sc["c"][4:104, :].bitcast(I32))
             elif x[0] == "W":
                 gather_words(x[1], int(x[2]), int(x[3]))
             elif x[0] == "i":

@@ -24,12 +24,10 @@ CHUNK = 512
 CHUNKS = S // CHUNK
 TILES = S // P
 TPC = CHUNK // P
-LOADS = "lc t0 t1 t2 t3 lb la W0 W1a s0 s1 s2 s3 s4 W1b s5 s6 s7 wi wc wu0 wu1 wu2 wu3 wr"
-ORDER = "Sc Sb Sa Wc00 Wb00 Wb01 i0 Wb11 Wb10 Wc10 B0 i1 i3 Wa00 i2 U1 Wa10 U0 U2 B1 U3 B2 A0 Wc11 A1 A2 Wc01 B3 Wa01 ir A3 B4 T0 T1 Wa11 Ur T2 B5 T3 A4 A5 B6 B7 Y01 T4 Y23 A6 T5 A7 T6 T7 Y45 Y6 Y7"
-TIE = {"1":0,"2":0,"3":0,"r":1}
-IL_POOL = []
-GP = []
-GS = []
+LOADS = "lc t0 t1 t2 t3 lb la W0 W1a s0 s1 s2 s3 s4 W1b s5 s6 s7 wi wc"
+ORDER = "Sc Sb Sa Wc00 Wb10 i0 Wb00 i3 i1 Wc11 Wc10 Wa10 B0 Wa00 B1 U0 i2 B2 U3 U2 U1 A0 B3 A1 T0 A2 Wb01 Wb11 Wc01 ir Wa11 T1 A3 Wa01 Ur B4 T2 B5 T3 A4 A5 B6 T4 A6 B7 T5 A7 Y01 Y23 T6 T7 Y45 Y6 Y7"
+TIE = {"Wc01":"p1","Wb01":"p2","Wb11":"q1","ir":"p3","Wa01":"q3","Wa11":"q2"}
+LATE = "wu0 wu1 wu2 wu3 wr"
 NPROD, NH, NY = 4, 2, 2
 
 
@@ -44,7 +42,7 @@ def tile_list_fm_rating_kernel(
         lists = {}
         for name in ("c", "b", "a"):
             lists[name] = keep.tile([P, S // 16], U16, name="list_" + name)
-        tab_sc = keep.tile([P, T], U8, align_bytes=64)
+        tab_sc = keep.tile([P, T], U8, tag="tab_sc", align_bytes=64)
         w_sc = keep.tile([P, 3, H], U8, align_bytes=64)
         c1_sc = keep.tile([P, S], U8, align_bytes=64)
         nc.vector.memset(tab_sc[:].bitcast(I32), 0)
@@ -54,10 +52,31 @@ def tile_list_fm_rating_kernel(
         tab_w = [keep.tile([P, T], I32, name="tab_w%d" % a) for a in range(PASSES)]
         wi_w = keep.tile([P, PASSES, H], I32, align_bytes=64)
         wc_w = keep.tile([P, PASSES, 2 * H], U8, align_bytes=64)
-        bias_sb = keep.tile([P, 2], F32)
-        wr_raw = keep.tile([P, 4, N], F32)
         HALF = H // 2
-        wu_raw = [keep.tile([P, 4, HALF], F32, name="wu_raw%d" % u) for u in range(4)]
+        raw = {}
+
+        def tag_of(key):
+            tie = TIE.get(key)
+            if tie is None:
+                return "own_" + key
+            return ("b_sb" if tie[0] == "p" else "s_sb") + tie[1]
+
+        def late_loads():
+            held = keep.tile([P, 5 * 4 * HALF + 8], F32, name="raw", tag="tab_sc", align_bytes=64)
+            for n, u in enumerate("0123r"):
+                raw[u] = held[:, n * 4 * HALF : (n + 1) * 4 * HALF].rearrange("p (j e) -> p j e", j=4)
+            raw["bias"] = held[:, 5 * 4 * HALF : 5 * 4 * HALF + 2]
+            for u in range(4):
+                a, c0 = u // 2, HALF * (u % 2)
+                nc.sync.dma_start(
+                    raw[str(u)], wu[512 * a : 512 * (a + 1), c0 : c0 + HALF].rearrange("(p j) e -> p j e", j=4)
+                )
+            wr_v = wr.rearrange("(q t i) n -> t q i n", t=4, i=8)
+            for t in range(4):
+                nc.sync.dma_start(raw["r"][:, t, :], wr_v[t])
+            with nc.allow_non_contiguous_dma(reason="one bias value a partition"):
+                nc.sync.dma_start(raw["bias"], bias.rearrange("(h p) -> p h", p=P))
+
         srcs = {"a": offs, "b": offs2, "c": offs3}
         for x in LOADS.split():
             if x[0] == "l":
@@ -89,16 +108,6 @@ def tile_list_fm_rating_kernel(
                         w_sc[32 * q : 32 * q + 4, 1:3, :].bitcast(I32),
                         wc_scales[:, 4 * q : 4 * q + 4, :].rearrange("a r e -> r a e").bitcast(I32),
                     )
-            elif x == "wr":
-                nc.sync.dma_start(wr_raw[:], wr.rearrange("(p j) n -> p j n", j=4))
-            else:
-                u = int(x[2])
-                a, c0 = u // 2, HALF * (u % 2)
-                nc.sync.dma_start(
-                    wu_raw[u][:], wu[512 * a : 512 * (a + 1), c0 : c0 + HALF].rearrange("(p j) e -> p j e", j=4)
-                )
-        with nc.allow_non_contiguous_dma(reason="one bias value a partition"):
-            nc.sync.dma_start(bias_sb[:], bias.rearrange("(h p) -> p h", p=P))
 
         ident = keep.tile([P, P], F32)
         make_identity(nc, ident[:])
@@ -114,40 +123,37 @@ def tile_list_fm_rating_kernel(
             nc.vector.tensor_copy(sc[name][:], tab_sc[:].indirect(lists[name][:]))
 
         def gather_words(name, a, ch):
-            words[name, a, ch] = keep.tile([P, CHUNK], U32, name="w_%s%d%d" % (name, a, ch), align_bytes=64)
+            words[name, a, ch] = keep.tile([P, CHUNK], U32, name="w_%s%d%d" % (name, a, ch), tag=tag_of("W%s%d%d" % (name, a, ch)), align_bytes=64)
             cols = CHUNK // 16
             nc.vector.tensor_copy(
                 words[name, a, ch][:], tab_w[a][:].bitcast(U32).indirect(lists[name][:, cols * ch : cols * (ch + 1)])
             )
 
         wu_w = keep.tile([P, PASSES, H], U32, align_bytes=64)
-        wu_sc = keep.tile([P, PASSES, H], U8, align_bytes=64)
         wr_w = keep.tile([P, N], U32, align_bytes=64)
         wr_sc = keep.tile([P, N], U8, align_bytes=64)
-        w_bf = {}
+        w_bf, wu_sc = {}, []
 
         def interleave(u):
-            src = wr_raw if u == "r" else wu_raw[int(u)]
             if u not in w_bf:
-                mates = [v for v in TIE if TIE[v] == TIE[u]] if u in TIE else [u]
-                tag = "b_sb%d" % TIE[u] if u in TIE else "w_bf" + u
-                held = keep.tile([P, len(mates), HALF, 4], BF16, name="w_bf" + u, tag=tag, align_bytes=64)
+                mates = "123" if u in "123" else u
+                key = "ix" if u in "123" else "i" + u
+                held = keep.tile([P, len(mates), HALF, 4], BF16, name="w_bf" + u, tag=tag_of(key), align_bytes=64)
                 for n, v in enumerate(mates):
                     w_bf[v] = held[:, n, :, :]
-            dst_v = w_bf[u].rearrange("p (c i) t -> p c t i", i=4)
-            src_v = src[:].rearrange("p t (c i) -> p c t i", i=4)
-            if u in IL_POOL:
-                nc.gpsimd.tensor_scalar(dst_v, src_v, 1.0, 0.0, MULT, ADD)
-            else:
-                nc.scalar.copy(dst_v, src_v)
+            nc.scalar.copy(
+                w_bf[u].rearrange("p (c i) t -> p c t i", i=4), raw[u].rearrange("p t (c i) -> p c t i", i=4)
+            )
 
         def quantize_weight(u):
             src = w_bf[u].rearrange("p e t -> p (e t)")
             if u == "r":
                 nc.vector.quantize_mx(wr_w[:].bitcast(FP8X4), wr_sc[:], src)
             else:
+                if not wu_sc:
+                    wu_sc.append(keep.tile([P, PASSES, H], U8, name="wu_sc", tag=tag_of("U"), align_bytes=64))
                 a, c0 = int(u) // 2, HALF * (int(u) % 2)
-                nc.vector.quantize_mx(wu_w[:, a, c0 : c0 + HALF].bitcast(FP8X4), wu_sc[:, a, c0 : c0 + HALF], src)
+                nc.vector.quantize_mx(wu_w[:, a, c0 : c0 + HALF].bitcast(FP8X4), wu_sc[0][:, a, c0 : c0 + HALF], src)
 
         def project(name, j):
             ch, c0 = j // TPC, (j % TPC) * P
@@ -155,7 +161,7 @@ def tile_list_fm_rating_kernel(
             cols = slice(j * P, (j + 1) * P)
             for a in range(PASSES):
                 if name == "a":
-                    rhs, rhs_sc, lhs_sc = wu_w[:, a, :].bitcast(FP8X4), wu_sc[:, a, :], sc[name][4 * a :, cols]
+                    rhs, rhs_sc, lhs_sc = wu_w[:, a, :].bitcast(FP8X4), wu_sc[0][:, a, :], sc[name][4 * a :, cols]
                 elif name == "b":
                     rhs, rhs_sc, lhs_sc = wi_w[:, a, :].bitcast(FP8X4), w_sc[4 * a :, 0, :], sc[name][4 * a :, cols]
                 else:
@@ -170,35 +176,29 @@ def tile_list_fm_rating_kernel(
                     start=(a == 0),
                     stop=(a == PASSES - 1),
                 )
-            return bank[:].rearrange("p (m t) -> p t m", t=4)
+            return bank[:].rearrange("p (q t i) -> p t q i", t=4, i=8)
 
         s_sb, p_sb, q_sb, h_bf = {}, {}, {}, {}
+
+        def runs(tile):
+            return tile[:].rearrange("p t (q i) -> p t q i", i=8)
 
         def pair_bc(j):
             b_ps = project("b", j)
             c_ps = project("c", j)
             b_sb = keep.tile([P, 4, P], F32, name="b_sb", tag="b_sb%d" % j, align_bytes=64)
-            nc.scalar.copy(b_sb[:], b_ps)
-            s_sb[j] = keep.tile([P, 4, P], F32, name="s%d" % j)
+            nc.scalar.copy(runs(b_sb), b_ps)
+            s_sb[j] = keep.tile([P, 4, P], F32, name="s%d" % j, tag="s_sb%d" % j, align_bytes=64)
             p_sb[j] = keep.tile([P, 4, P], F32, name="p%d" % j)
-            if j in GP:
-                c_sb = keep.tile([P, 4, P], F32, name="c_sb%d" % j)
-                nc.scalar.copy(c_sb[:], c_ps)
-                if j in GS:
-                    nc.gpsimd.tensor_tensor(s_sb[j][:], c_sb[:], b_sb[:], ADD)
-                else:
-                    nc.vector.tensor_tensor(s_sb[j][:], c_ps, b_sb[:], ADD)
-                nc.gpsimd.tensor_tensor(p_sb[j][:], c_sb[:], b_sb[:], MULT)
-            else:
-                nc.vector.tensor_tensor(s_sb[j][:], c_ps, b_sb[:], ADD)
-                nc.vector.tensor_tensor(p_sb[j][:], c_ps, b_sb[:], MULT)
+            nc.vector.tensor_tensor(runs(s_sb[j]), c_ps, runs(b_sb), ADD)
+            nc.vector.tensor_tensor(runs(p_sb[j]), c_ps, runs(b_sb), MULT)
 
         out_v = out.rearrange("(h p) j -> p h j", p=P)
 
         def times_a(j):
             a_ps = project("a", j)
             q_sb[j] = keep.tile([P, 4, P], F32, name="q%d" % j)
-            nc.vector.tensor_tensor(q_sb[j][:], a_ps, s_sb[j][:], MULT)
+            nc.vector.tensor_tensor(runs(q_sb[j]), a_ps, runs(s_sb[j]), MULT)
 
         group_of = {}
         for x in ORDER.split():
@@ -235,12 +235,14 @@ def tile_list_fm_rating_kernel(
                     stop=True,
                 )
             for h in range(2):
-                nc.scalar.activation(y_sb[:, h, :], y_ps[:, h, :], IDENT, bias=bias_sb[:, h : h + 1])
+                nc.scalar.activation(y_sb[:, h, :], y_ps[:, h, :], IDENT, bias=raw["bias"][:, h : h + 1])
             nc.sync.dma_start(out_v[:, :, j0 : j0 + w], y_sb[:])
 
         for x in ORDER.split():
             if x[0] == "S":
                 gather_scales(x[1])
+                if x[1] == "a":
+                    late_loads()
                 if x[1] == "c":
                     nc.scalar.dma_start(c1_sc[0:100, :].bitcast(I32), sc["c"][4:104, :].bitcast(I32))
             elif x[0] == "W":

@@ -24,10 +24,10 @@ CHUNK = 512
 CHUNKS = S // CHUNK
 TILES = S // P
 TPC = CHUNK // P
-LOADS = "lc t0 t1 t2 t3 lb la W0 W1a s0 s1 s2 s3 s4 W1b s5 s6 s7 wi wc"
-ORDER = "Sc Sb Sa Wc00 Wb10 i0 Wb00 i3 i1 Wc11 Wc10 Wa10 B0 Wa00 B1 U0 i2 B2 U3 U2 U1 A0 B3 A1 T0 A2 Wb01 Wb11 Wc01 ir Wa11 T1 A3 Wa01 Ur B4 T2 B5 T3 A4 A5 B6 T4 A6 B7 T5 A7 Y01 Y23 T6 T7 Y45 Y6 Y7"
-TIE = {"Wc01":"p1","Wb01":"p2","Wb11":"q1","ir":"p3","Wa01":"q3","Wa11":"q2"}
-LATE = "wu0 wu1 wu2 wu3 wr"
+LOADS = "lc t0 t1 t2 t3 lb la W0 wu0 s0 s1 s2 s3 wu1 W1a s4 s5 s6 s7 W1b wi wc"
+ORDER = "Sc Sb Sa i2 Wb00 Wb01 Wa00 U2 Wc00 i1 i0 Wb10 U1 Wc10 B0 U0 B1 i3 Wa10 B2 U3 Wc11 A0 A1 T0 A2 Wc01 Wb11 B3 A3 T1 T2 B4 B5 Wa01 ir B6 T3 Wa11 Ur A4 Y01 A5 B7 A6 T4 T5 A7 Y23 T6 T7 Y45 Y6 Y7"
+TIE = {"Wc01":"q0","Wb11":"q2","ir":"p4","Wa01":"p3","Wa11":"q3"}
+LATE = "wu2 wu3 wr"
 NPROD, NH, NY = 4, 2, 2
 
 
@@ -61,16 +61,19 @@ def tile_list_fm_rating_kernel(
                 return "own_" + key
             return ("b_sb" if tie[0] == "p" else "s_sb") + tie[1]
 
+        def load_wu(u):
+            a, c0 = u // 2, HALF * (u % 2)
+            nc.sync.dma_start(
+                raw[str(u)], wu[512 * a : 512 * (a + 1), c0 : c0 + HALF].rearrange("(p j) e -> p j e", j=4)
+            )
+
         def late_loads():
-            held = keep.tile([P, 5 * 4 * HALF + 8], F32, name="raw", tag="tab_sc", align_bytes=64)
-            for n, u in enumerate("0123r"):
+            held = keep.tile([P, 3 * 4 * HALF + 8], F32, name="raw", tag="tab_sc", align_bytes=64)
+            for n, u in enumerate("23r"):
                 raw[u] = held[:, n * 4 * HALF : (n + 1) * 4 * HALF].rearrange("p (j e) -> p j e", j=4)
-            raw["bias"] = held[:, 5 * 4 * HALF : 5 * 4 * HALF + 2]
-            for u in range(4):
-                a, c0 = u // 2, HALF * (u % 2)
-                nc.sync.dma_start(
-                    raw[str(u)], wu[512 * a : 512 * (a + 1), c0 : c0 + HALF].rearrange("(p j) e -> p j e", j=4)
-                )
+            raw["bias"] = held[:, 3 * 4 * HALF : 3 * 4 * HALF + 2]
+            for u in range(2, 4):
+                load_wu(u)
             wr_v = wr.rearrange("(q t i) n -> t q i n", t=4, i=8)
             for t in range(4):
                 nc.sync.dma_start(raw["r"][:, t, :], wr_v[t])
@@ -93,6 +96,10 @@ def tile_list_fm_rating_kernel(
                 a = int(x[1])
                 cols = {"": slice(0, T), "a": slice(0, T // 2), "b": slice(T // 2, T)}[x[2:]]
                 nc.sync.dma_start(tab_w[a][:, cols], tab_words[a].rearrange("p t i -> p (t i)").bitcast(I32)[:, cols])
+            elif x[1] == "u":
+                early = keep.tile([P, 4, HALF], F32, name="raw" + x[2])
+                raw[x[2]] = early[:]
+                load_wu(int(x[2]))
             elif x == "wi":
                 nc.sync.dma_start(wi_w[:], wi_words.rearrange("a p e i -> p a (e i)").bitcast(I32))
             elif x == "wc":

@@ -25,9 +25,10 @@ CHUNKS = S // CHUNK
 TILES = S // P
 TPC = CHUNK // P
 LOADS = "lc t0 t1 t2 t3 lb la W0 wu0 s0 s1 s2 s3 wu1 W1a s4 s5 s6 s7 W1b wi wc"
-ORDER = "Sc Sb Sa i2 Wb00 Wb01 Wa00 U2 Wc00 i1 i0 Wb10 U1 Wc10 B0 U0 B1 i3 Wa10 B2 U3 Wc11 A0 A1 T0 A2 Wc01 Wb11 B3 A3 T1 T2 B4 B5 Wa01 ir B6 T3 Wa11 Ur A4 Y01 A5 B7 A6 T4 T5 A7 Y23 T6 T7 Y45 Y6 Y7"
-TIE = {"Wc01":"q0","Wb11":"q2","ir":"p4","Wa01":"p3","Wa11":"q3"}
+ORDER = "Sc Sb Sa i2 i1 Wb10 Wb00 i0 U2 Wc00 U1 U0 Wc10 Wa10 Wa00 i3 B0 B1 U3 B2 A0 B3 Wb11 Wc11 A1 Wc01 T0 A2 A3 T1 Wb01 B4 T2 Wa01 B5 Wa11 B6 A4 T3 A5 A6 B7 ir A7 T4 T5 Ur Y23 Y01 T6 T7 Y45 Y6 Y7"
+TIE = {"Wb11":"p0","ir":"q4","Wa11":"q1","Wb01":"q0","Wc01":"p1"}
 LATE = "wu2 wu3 wr"
+GP = [0,1,2,3]
 NPROD, NH, NY = 4, 2, 2
 
 
@@ -197,8 +198,14 @@ def tile_list_fm_rating_kernel(
             nc.scalar.copy(runs(b_sb), b_ps)
             s_sb[j] = keep.tile([P, 4, P], F32, name="s%d" % j, tag="s_sb%d" % j, align_bytes=64)
             p_sb[j] = keep.tile([P, 4, P], F32, name="p%d" % j)
+            if j in GP:
+                c_sb = keep.tile([P, 4, P], F32, name="c%d" % j)
+                nc.scalar.copy(runs(c_sb), c_ps)
             nc.vector.tensor_tensor(runs(s_sb[j]), c_ps, runs(b_sb), ADD)
-            nc.vector.tensor_tensor(runs(p_sb[j]), c_ps, runs(b_sb), MULT)
+            if j in GP:
+                nc.gpsimd.tensor_tensor(p_sb[j][:], c_sb[:], b_sb[:], MULT)
+            else:
+                nc.vector.tensor_tensor(runs(p_sb[j]), c_ps, runs(b_sb), MULT)
 
         out_v = out.rearrange("(h p) j -> p h j", p=P)
 

@@ -24,12 +24,14 @@ CHUNK = 512
 CHUNKS = S // CHUNK
 TILES = S // P
 TPC = CHUNK // P
-LOADS = "lc t0 t1 t2 t3 lb la W0 wu0 s0 s1 s2 s3 wu1 W1a s4 s5 s6 s7 W1b wi wc"
-ORDER = "Sc Sb Sa i2 i1 Wb10 Wb00 i0 U2 Wc00 U1 U0 Wc10 Wa10 Wa00 i3 B0 B1 U3 B2 A0 B3 Wb11 Wc11 A1 Wc01 T0 A2 A3 T1 Wb01 B4 T2 Wa01 B5 Wa11 B6 A4 T3 A5 A6 B7 ir A7 T4 T5 Ur Y23 Y01 T6 T7 Y45 Y6 Y7"
-TIE = {"Wb11":"p0","ir":"q4","Wa11":"q1","Wb01":"q0","Wc01":"p1"}
-LATE = "wu2 wu3 wr"
-GP = [0,1,2,3]
-NPROD, NH, NY = 4, 2, 2
+HALF = H // 2
+VECTOR_TILES = (4, 5)
+BC_ORDER = (0, 1, 2, 3, 6, 7, 4, 5)
+GROUPS = ((0, 1), (2, 3), (4, 5), (6,), (7,))
+BANKS = {"a0": 1, "a1": 2, "a2": 4, "a3": 1, "a4": 2, "a5": 4, "a6": 3, "a7": 0}
+REUSE = {"s4": "s0", "p4": "s1", "s5": "s2", "p5": "q0", "h0": "p2", "h2": "s1"}
+Y_BANKS = {0: "prod1", 2: "prod2", 4: "prod4", 6: "prod3", 7: "prod0"}
+NPROD, NH = 5, 3
 
 
 def tile_list_fm_rating_kernel(
@@ -43,79 +45,55 @@ def tile_list_fm_rating_kernel(
         lists = {}
         for name in ("c", "b", "a"):
             lists[name] = keep.tile([P, S // 16], U16, name="list_" + name)
-        tab_sc = keep.tile([P, T], U8, tag="tab_sc", align_bytes=64)
-        w_sc = keep.tile([P, 3, H], U8, align_bytes=64)
+        tab_sc = keep.tile([P, T], U8, align_bytes=64)
+        wi_sc = keep.tile([P, H], U8, align_bytes=64)
+        wc_sc = keep.tile([P, PASSES, H], U8, align_bytes=64)
         c1_sc = keep.tile([P, S], U8, align_bytes=64)
         nc.vector.memset(tab_sc[:].bitcast(I32), 0)
-        nc.vector.memset(w_sc[:].rearrange("p a e -> p (a e)").bitcast(I32), 0)
+        nc.vector.memset(wi_sc[:].bitcast(I32), 0)
+        nc.vector.memset(wc_sc[:].rearrange("p a e -> p (a e)").bitcast(I32), 0)
         nc.vector.memset(c1_sc[:].bitcast(I32), 0)
 
         tab_w = [keep.tile([P, T], I32, name="tab_w%d" % a) for a in range(PASSES)]
         wi_w = keep.tile([P, PASSES, H], I32, align_bytes=64)
         wc_w = keep.tile([P, PASSES, 2 * H], U8, align_bytes=64)
-        HALF = H // 2
-        raw = {}
+        raw = [keep.tile([P, 4, w], F32, name="raw%d" % u) for u, w in enumerate((HALF, HALF, H, N))]
+        bias_sb = keep.tile([P, 2], F32)
 
-        def tag_of(key):
-            tie = TIE.get(key)
-            if tie is None:
-                return "own_" + key
-            return ("b_sb" if tie[0] == "p" else "s_sb") + tie[1]
+        def load_table(a, half):
+            cols = slice(half * T // 2, (half + 1) * T // 2)
+            nc.sync.dma_start(tab_w[a][:, cols], tab_words[a].rearrange("p t i -> p (t i)").bitcast(I32)[:, cols])
 
-        def load_wu(u):
-            a, c0 = u // 2, HALF * (u % 2)
+        nc.sync.dma_start(lists["c"][:], offs3)
+        for q in range(4):
             nc.sync.dma_start(
-                raw[str(u)], wu[512 * a : 512 * (a + 1), c0 : c0 + HALF].rearrange("(p j) e -> p j e", j=4)
+                tab_sc[32 * q : 32 * q + 8, :].bitcast(I32), tab_scales[:, 4 * q : 4 * q + 4, :].bitcast(I32)
             )
-
-        def late_loads():
-            held = keep.tile([P, 3 * 4 * HALF + 8], F32, name="raw", tag="tab_sc", align_bytes=64)
-            for n, u in enumerate("23r"):
-                raw[u] = held[:, n * 4 * HALF : (n + 1) * 4 * HALF].rearrange("p (j e) -> p j e", j=4)
-            raw["bias"] = held[:, 3 * 4 * HALF : 3 * 4 * HALF + 2]
-            for u in range(2, 4):
-                load_wu(u)
-            wr_v = wr.rearrange("(q t i) n -> t q i n", t=4, i=8)
-            for t in range(4):
-                nc.sync.dma_start(raw["r"][:, t, :], wr_v[t])
-            with nc.allow_non_contiguous_dma(reason="one bias value a partition"):
-                nc.sync.dma_start(raw["bias"], bias.rearrange("(h p) -> p h", p=P))
-
-        srcs = {"a": offs, "b": offs2, "c": offs3}
-        for x in LOADS.split():
-            if x[0] == "l":
-                nc.sync.dma_start(lists[x[1]][:], srcs[x[1]])
-            elif x[0] == "t":
-                q = int(x[1])
-                nc.sync.dma_start(
-                    tab_sc[32 * q : 32 * q + 8, :].bitcast(I32), tab_scales[:, 4 * q : 4 * q + 4, :].bitcast(I32)
-                )
-            elif x[0] == "r":
-                a, r = int(x[1]), int(x[2])
-                nc.sync.dma_start(tab_sc[4 * a + r : P : 32, :].bitcast(I32), tab_scales[a, r:16:4, :].bitcast(I32))
-            elif x[0] == "W":
-                a = int(x[1])
-                cols = {"": slice(0, T), "a": slice(0, T // 2), "b": slice(T // 2, T)}[x[2:]]
-                nc.sync.dma_start(tab_w[a][:, cols], tab_words[a].rearrange("p t i -> p (t i)").bitcast(I32)[:, cols])
-            elif x[1] == "u":
-                early = keep.tile([P, 4, HALF], F32, name="raw" + x[2])
-                raw[x[2]] = early[:]
-                load_wu(int(x[2]))
-            elif x == "wi":
-                nc.sync.dma_start(wi_w[:], wi_words.rearrange("a p e i -> p a (e i)").bitcast(I32))
-            elif x == "wc":
-                nc.sync.dma_start(wc_w[:].bitcast(I32), wc_words.rearrange("a p e -> p a e").bitcast(I32))
-            elif x[0] == "s":
-                q = int(x[1]) % 4
-                if int(x[1]) < 4:
-                    nc.sync.dma_start(
-                        w_sc[32 * q : 32 * q + 8, 0, :].bitcast(I32), wi_scales[:, 4 * q : 4 * q + 4, :].bitcast(I32)
-                    )
-                else:
-                    nc.sync.dma_start(
-                        w_sc[32 * q : 32 * q + 4, 1:3, :].bitcast(I32),
-                        wc_scales[:, 4 * q : 4 * q + 4, :].rearrange("a r e -> r a e").bitcast(I32),
-                    )
+        nc.sync.dma_start(lists["b"][:], offs2)
+        with nc.allow_non_contiguous_dma(reason="one bias value a partition"):
+            nc.sync.dma_start(bias_sb[:], bias.rearrange("(h p) -> p h", p=P))
+        load_table(0, 0)
+        for q in range(4):
+            nc.sync.dma_start(
+                wi_sc[32 * q : 32 * q + 8, :].bitcast(I32), wi_scales[:, 4 * q : 4 * q + 4, :].bitcast(I32)
+            )
+        load_table(0, 1)
+        for q in range(4):
+            nc.sync.dma_start(
+                wc_sc[32 * q : 32 * q + 4, :, :].bitcast(I32),
+                wc_scales[:, 4 * q : 4 * q + 4, :].rearrange("a r e -> r a e").bitcast(I32),
+            )
+        load_table(1, 0)
+        load_table(1, 1)
+        nc.sync.dma_start(wi_w[:], wi_words.rearrange("a p e i -> p a (e i)").bitcast(I32))
+        nc.sync.dma_start(wc_w[:].bitcast(I32), wc_words.rearrange("a p e -> p a e").bitcast(I32))
+        nc.sync.dma_start(lists["a"][:], offs)
+        for u in range(2):
+            nc.sync.dma_start(raw[u][:], wu[0:512, HALF * u : HALF * (u + 1)].rearrange("(p j) e -> p j e", j=4))
+        nc.sync.dma_start(raw[2][:], wu[512:1024, :].rearrange("(p j) e -> p j e", j=4))
+        wr_v = wr.rearrange("(q t i) n -> t q i n", t=4, i=8)
+        for t in range(4):
+            nc.sync.dma_start(raw[3][:, t, :], wr_v[t])
 
         ident = keep.tile([P, P], F32)
         make_identity(nc, ident[:])
@@ -123,57 +101,51 @@ def tile_list_fm_rating_kernel(
         nc.scalar.activation(warm[:], ident[:, 0:1], IDENT)
 
         sc = {}
-        for name in ("c", "b", "a"):
-            sc[name] = keep.tile([P, S], U8, name="sc_" + name, align_bytes=64)
         words = {}
 
         def gather_scales(name):
+            sc[name] = keep.tile([P, S], U8, name="sc_" + name, align_bytes=64)
             nc.vector.tensor_copy(sc[name][:], tab_sc[:].indirect(lists[name][:]))
 
-        def gather_words(name, a, ch):
-            words[name, a, ch] = keep.tile([P, CHUNK], U32, name="w_%s%d%d" % (name, a, ch), tag=tag_of("W%s%d%d" % (name, a, ch)), align_bytes=64)
-            cols = CHUNK // 16
-            nc.vector.tensor_copy(
-                words[name, a, ch][:], tab_w[a][:].bitcast(U32).indirect(lists[name][:, cols * ch : cols * (ch + 1)])
-            )
+        def gather_words(name, a, chunks, tile=None):
+            width = CHUNK * len(chunks)
+            if tile is None:
+                own = keep.tile([P, width], U32, name="w_%s%d%d" % (name, a, chunks[0]), align_bytes=64)
+                tile = own[:]
+            for n, ch in enumerate(chunks):
+                words[name, a, ch] = tile[:, n * CHUNK : (n + 1) * CHUNK]
+            c0 = CHUNK // 16 * chunks[0]
+            nc.vector.tensor_copy(tile, tab_w[a][:].bitcast(U32).indirect(lists[name][:, c0 : c0 + width // 16]))
 
         wu_w = keep.tile([P, PASSES, H], U32, align_bytes=64)
+        wu_sc = keep.tile([P, PASSES, H], U8, align_bytes=64)
         wr_w = keep.tile([P, N], U32, align_bytes=64)
         wr_sc = keep.tile([P, N], U8, align_bytes=64)
-        w_bf, wu_sc = {}, []
 
-        def interleave(u):
-            if u not in w_bf:
-                mates = "123" if u in "123" else u
-                key = "ix" if u in "123" else "i" + u
-                held = keep.tile([P, len(mates), HALF, 4], BF16, name="w_bf" + u, tag=tag_of(key), align_bytes=64)
-                for n, v in enumerate(mates):
-                    w_bf[v] = held[:, n, :, :]
-            nc.scalar.copy(
-                w_bf[u].rearrange("p (c i) t -> p c t i", i=4), raw[u].rearrange("p t (c i) -> p c t i", i=4)
-            )
+        wu_bf = keep.tile([P, PASSES * H, 4], BF16, tag="wu_bf", align_bytes=64)
+        wr_bf = keep.tile([P, N, 4], BF16, align_bytes=64)
 
-        def quantize_weight(u):
-            src = w_bf[u].rearrange("p e t -> p (e t)")
-            if u == "r":
-                nc.vector.quantize_mx(wr_w[:].bitcast(FP8X4), wr_sc[:], src)
-            else:
-                if not wu_sc:
-                    wu_sc.append(keep.tile([P, PASSES, H], U8, name="wu_sc", tag=tag_of("U"), align_bytes=64))
-                a, c0 = int(u) // 2, HALF * (int(u) % 2)
-                nc.vector.quantize_mx(wu_w[:, a, c0 : c0 + HALF].bitcast(FP8X4), wu_sc[0][:, a, c0 : c0 + HALF], src)
+        def cast_weight(copy, dst, rows):
+            copy(dst.rearrange("p (c i) t -> p c t i", i=4), rows.rearrange("p t (c i) -> p c t i", i=4))
+
+        def quantize(words, scales, values):
+            nc.vector.quantize_mx(words.bitcast(FP8X4), scales, values.rearrange("p e t -> p (e t)"))
 
         def project(name, j):
             ch, c0 = j // TPC, (j % TPC) * P
-            bank = psum.tile([P, H], F32, tag="prod", bufs=NPROD, name="bank")
+            if name == "a":
+                slot = BANKS["a%d" % j]
+            else:
+                slot = (2 * BC_ORDER.index(j) + (name == "c")) % NPROD
+            bank = psum.tile([P, H], F32, tag="prod%d" % slot, name="bank")
             cols = slice(j * P, (j + 1) * P)
             for a in range(PASSES):
                 if name == "a":
-                    rhs, rhs_sc, lhs_sc = wu_w[:, a, :].bitcast(FP8X4), wu_sc[0][:, a, :], sc[name][4 * a :, cols]
+                    rhs, rhs_sc, lhs_sc = wu_w[:, a, :].bitcast(FP8X4), wu_sc[:, a, :], sc[name][4 * a :, cols]
                 elif name == "b":
-                    rhs, rhs_sc, lhs_sc = wi_w[:, a, :].bitcast(FP8X4), w_sc[4 * a :, 0, :], sc[name][4 * a :, cols]
+                    rhs, rhs_sc, lhs_sc = wi_w[:, a, :].bitcast(FP8X4), wi_sc[4 * a :, :], sc[name][4 * a :, cols]
                 else:
-                    rhs, rhs_sc = wc_w[:, a, :].bitcast(FP4X4), w_sc[:, 1 + a, :]
+                    rhs, rhs_sc = wc_w[:, a, :].bitcast(FP4X4), wc_sc[:, a, :]
                     lhs_sc = (sc["c"], c1_sc)[a][:, cols]
                 nc.tensor.matmul_mx(
                     bank[:],
@@ -186,58 +158,62 @@ def tile_list_fm_rating_kernel(
                 )
             return bank[:].rearrange("p (q t i) -> p t q i", t=4, i=8)
 
-        s_sb, p_sb, q_sb, h_bf = {}, {}, {}, {}
+        s_sb, p_sb, q_sb, h_bf, pooled = {}, {}, {}, {}, {}
+
+        def tag_of(key):
+            return REUSE.get(key, key)
 
         def runs(tile):
             return tile[:].rearrange("p t (q i) -> p t q i", i=8)
 
-        def pair_bc(j):
+        def project_bc(j):
             b_ps = project("b", j)
             c_ps = project("c", j)
-            b_sb = keep.tile([P, 4, P], F32, name="b_sb", tag="b_sb%d" % j, align_bytes=64)
+            b_sb = keep.tile([P, 4, P], F32, name="b%d" % j)
             nc.scalar.copy(runs(b_sb), b_ps)
-            s_sb[j] = keep.tile([P, 4, P], F32, name="s%d" % j, tag="s_sb%d" % j, align_bytes=64)
-            p_sb[j] = keep.tile([P, 4, P], F32, name="p%d" % j)
-            if j in GP:
-                c_sb = keep.tile([P, 4, P], F32, name="c%d" % j)
-                nc.scalar.copy(runs(c_sb), c_ps)
+            return b_sb, c_ps
+
+        def sum_and_product_tiles(j):
+            s_sb[j] = keep.tile([P, 4, P], F32, name="s%d" % j, tag=tag_of("s%d" % j), align_bytes=64)
+            p_sb[j] = keep.tile([P, 4, P], F32, name="p%d" % j, tag=tag_of("p%d" % j), align_bytes=64)
+
+        def pair_bc(j):
+            b_sb, c_ps = project_bc(j)
+            c_sb = keep.tile([P, 4, P], F32, name="c%d" % j)
+            nc.scalar.copy(runs(c_sb), c_ps)
+            sum_and_product_tiles(j)
+            nc.gpsimd.tensor_tensor(s_sb[j][:], c_sb[:], b_sb[:], ADD)
+            pooled[j] = b_sb, c_sb
+
+        def combine_on_vector(j, b_sb, c_ps):
+            sum_and_product_tiles(j)
             nc.vector.tensor_tensor(runs(s_sb[j]), c_ps, runs(b_sb), ADD)
-            if j in GP:
-                nc.gpsimd.tensor_tensor(p_sb[j][:], c_sb[:], b_sb[:], MULT)
-            else:
-                nc.vector.tensor_tensor(runs(p_sb[j]), c_ps, runs(b_sb), MULT)
+            nc.vector.tensor_tensor(runs(p_sb[j]), c_ps, runs(b_sb), MULT)
 
         out_v = out.rearrange("(h p) j -> p h j", p=P)
 
         def times_a(j):
             a_ps = project("a", j)
-            q_sb[j] = keep.tile([P, 4, P], F32, name="q%d" % j)
+            q_sb[j] = keep.tile([P, 4, P], F32, name="q%d" % j, tag=tag_of("q%d" % j), align_bytes=64)
             nc.vector.tensor_tensor(runs(q_sb[j]), a_ps, runs(s_sb[j]), MULT)
 
-        group_of = {}
-        for x in ORDER.split():
-            if x[0] == "Y":
-                for z in x[1:]:
-                    group_of[int(z)] = x[1:]
-
-        def turn(j):
+        def turn(j, g):
             h_ps = psum.tile([P, 4, P], F32, tag="h", bufs=NH, name="h_ps")
             for t in range(4):
                 nc.tensor.matmul(h_ps[:, t, :], p_sb[j][:, t, :], ident[:], start=True, stop=False, is_transpose=True)
                 nc.tensor.matmul(h_ps[:, t, :], q_sb[j][:, t, :], ident[:], start=False, stop=True, is_transpose=True)
-            g = group_of[j]
             if g not in h_bf:
-                h_bf[g] = keep.tile([P, len(g) * P, 4], BF16, name="h_bf" + g, align_bytes=64)
-            c0 = (j - int(g[0])) * P
+                h_bf[g] = keep.tile([P, len(g) * P, 4], BF16, name="h_bf%d" % g[0], align_bytes=64)
+            c0 = (j - g[0]) * P
             nc.scalar.copy(h_bf[g][:, c0 : c0 + P, :], h_ps[:].rearrange("p t j -> p j t"))
 
         def rate(g):
-            w, j0 = len(g) * P, int(g[0]) * P
-            h_w = keep.tile([P, w], U32, name="h_w" + g, align_bytes=64)
-            h_sc = keep.tile([P, w], U8, name="h_sc" + g, align_bytes=64)
+            w, j0 = len(g) * P, g[0] * P
+            h_w = keep.tile([P, w], U32, name="h_w%d" % g[0], tag=tag_of("h%d" % g[0]), align_bytes=64)
+            h_sc = keep.tile([P, w], U8, name="h_sc%d" % g[0], align_bytes=64)
             nc.vector.quantize_mx(h_w[:].bitcast(FP8X4), h_sc[:], h_bf[g][:].rearrange("p j t -> p (j t)"))
-            y_ps = psum.tile([P, 2, w], F32, tag="y", bufs=NY, name="y_ps")
-            y_sb = keep.tile([P, 2, w], F32, name="y_sb" + g)
+            y_ps = psum.tile([P, 2, w], F32, tag=Y_BANKS[g[0]], name="y_ps")
+            y_sb = keep.tile([P, 2, w], F32, name="y_sb%d" % g[0])
             for h in range(2):
                 nc.tensor.matmul_mx(
                     y_ps[:, h, :],
@@ -249,27 +225,45 @@ def tile_list_fm_rating_kernel(
                     stop=True,
                 )
             for h in range(2):
-                nc.scalar.activation(y_sb[:, h, :], y_ps[:, h, :], IDENT, bias=raw["bias"][:, h : h + 1])
+                nc.scalar.activation(y_sb[:, h, :], y_ps[:, h, :], IDENT, bias=bias_sb[:, h : h + 1])
             nc.sync.dma_start(out_v[:, :, j0 : j0 + w], y_sb[:])
 
-        for x in ORDER.split():
-            if x[0] == "S":
-                gather_scales(x[1])
-                if x[1] == "a":
-                    late_loads()
-                if x[1] == "c":
-                    nc.scalar.dma_start(c1_sc[0:100, :].bitcast(I32), sc["c"][4:104, :].bitcast(I32))
-            elif x[0] == "W":
-                gather_words(x[1], int(x[2]), int(x[3]))
-            elif x[0] == "i":
-                interleave(x[1])
-            elif x[0] == "U":
-                quantize_weight(x[1])
-            elif x[0] == "B":
-                pair_bc(int(x[1]))
-            elif x[0] == "A":
-                times_a(int(x[1]))
-            elif x[0] == "T":
-                turn(int(x[1]))
-            else:
-                rate(x[1:])
+        gather_scales("c")
+        nc.gpsimd.dma_start(c1_sc[0:100, :].bitcast(I32), sc["c"][4:104, :].bitcast(I32))
+        gather_scales("b")
+        gather_words("b", 0, (0, 1))
+        gather_words("c", 0, (0, 1))
+        for ch in range(CHUNKS):
+            gather_words("b", 1, (ch,))
+            gather_words("c", 1, (ch,))
+        gather_scales("a")
+        gather_words("a", 0, (0,))
+        gather_words("a", 1, (0,))
+        for j in BC_ORDER[:2]:
+            pair_bc(j)
+        for u in range(2):
+            cast_weight(nc.scalar.copy, wu_bf[:, HALF * u : HALF * (u + 1), :], raw[u][:])
+        cast_weight(nc.vector.tensor_copy, wu_bf[:, H:, :], raw[2][:])
+        quantize(wu_w[:].rearrange("p a e -> p (a e)"), wu_sc[:].rearrange("p a e -> p (a e)"), wu_bf[:])
+        late = keep.tile([P, PASSES, CHUNK], U32, tag="wu_bf", align_bytes=64)
+        for a in range(PASSES):
+            gather_words("a", a, (1,), late[:, a, :])
+        for j in BC_ORDER[2:6]:
+            pair_bc(j)
+        held = {j: project_bc(j) for j in VECTOR_TILES}
+        for j in BC_ORDER[:6]:
+            nc.gpsimd.tensor_tensor(p_sb[j][:], pooled[j][1][:], pooled[j][0][:], MULT)
+        cast_weight(nc.scalar.copy, wr_bf[:], raw[3][:])
+        quantize(wr_w[:], wr_sc[:], wr_bf[:])
+        for j in range(3):
+            times_a(j)
+        turn(0, GROUPS[0])
+        for j in VECTOR_TILES:
+            combine_on_vector(j, *held[j])
+        for j in range(3, TILES):
+            times_a(j)
+        for g in GROUPS:
+            for j in g:
+                if j > 0:
+                    turn(j, g)
+            rate(g)

@@ -25,13 +25,8 @@ CHUNKS = S // CHUNK
 TILES = S // P
 TPC = CHUNK // P
 HALF = H // 2
-VECTOR_TILES = (4, 5)
-BC_ORDER = (0, 1, 2, 3, 6, 7, 4, 5)
-GROUPS = ((0, 1), (2, 3), (4, 5), (6,), (7,))
-BANKS = {"a0": 1, "a1": 2, "a2": 4, "a3": 1, "a4": 2, "a5": 4, "a6": 3, "a7": 0}
-REUSE = {"s4": "s0", "p4": "s1", "s5": "s2", "p5": "q0", "h0": "p2", "h2": "s1"}
-Y_BANKS = {0: "prod1", 2: "prod2", 4: "prod4", 6: "prod3", 7: "prod0"}
-NPROD, NH = 5, 3
+GROUPS = ((0, 1, 2, 3), (4, 5), (6,), (7,))
+BANKS = 8
 
 
 def tile_list_fm_rating_kernel(
@@ -54,10 +49,10 @@ def tile_list_fm_rating_kernel(
         nc.vector.memset(wc_sc[:].rearrange("p a e -> p (a e)").bitcast(I32), 0)
         nc.vector.memset(c1_sc[:].bitcast(I32), 0)
 
-        tab_w = [keep.tile([P, T], I32, name="tab_w%d" % a) for a in range(PASSES)]
+        tab_w = [keep.tile([P, T], I32, name="tab_w%d" % a, tag="tab_w%d" % a) for a in range(PASSES)]
         wi_w = keep.tile([P, PASSES, H], I32, align_bytes=64)
         wc_w = keep.tile([P, PASSES, 2 * H], U8, align_bytes=64)
-        raw = [keep.tile([P, 4, w], F32, name="raw%d" % u) for u, w in enumerate((HALF, HALF, H, N))]
+        raw = [keep.tile([P, 4, w], F32, name="raw%d" % u, tag="raw%d" % u) for u, w in enumerate((HALF, HALF, H))]
         bias_sb = keep.tile([P, 2], F32)
 
         def load_table(a, half):
@@ -85,15 +80,17 @@ def tile_list_fm_rating_kernel(
             )
         load_table(1, 0)
         load_table(1, 1)
+        nc.sync.dma_start(lists["a"][:], offs)
         nc.sync.dma_start(wi_w[:], wi_words.rearrange("a p e i -> p a (e i)").bitcast(I32))
         nc.sync.dma_start(wc_w[:].bitcast(I32), wc_words.rearrange("a p e -> p a e").bitcast(I32))
-        nc.sync.dma_start(lists["a"][:], offs)
         for u in range(2):
             nc.sync.dma_start(raw[u][:], wu[0:512, HALF * u : HALF * (u + 1)].rearrange("(p j) e -> p j e", j=4))
         nc.sync.dma_start(raw[2][:], wu[512:1024, :].rearrange("(p j) e -> p j e", j=4))
+
+        wr_raw = keep.tile([P, 4, N], F32)
         wr_v = wr.rearrange("(q t i) n -> t q i n", t=4, i=8)
         for t in range(4):
-            nc.sync.dma_start(raw[3][:, t, :], wr_v[t])
+            nc.sync.dma_start(wr_raw[:, t, :], wr_v[t])
 
         ident = keep.tile([P, P], F32)
         make_identity(nc, ident[:])
@@ -131,13 +128,9 @@ def tile_list_fm_rating_kernel(
         def quantize(words, scales, values):
             nc.vector.quantize_mx(words.bitcast(FP8X4), scales, values.rearrange("p e t -> p (e t)"))
 
-        def project(name, j):
+        def project(name, j, slot):
             ch, c0 = j // TPC, (j % TPC) * P
-            if name == "a":
-                slot = BANKS["a%d" % j]
-            else:
-                slot = (2 * BC_ORDER.index(j) + (name == "c")) % NPROD
-            bank = psum.tile([P, H], F32, tag="prod%d" % slot, name="bank")
+            bank = psum.tile([P, H], F32, tag="bank%d" % slot, name="bank")
             cols = slice(j * P, (j + 1) * P)
             for a in range(PASSES):
                 if name == "a":
@@ -158,65 +151,41 @@ def tile_list_fm_rating_kernel(
                 )
             return bank[:].rearrange("p (q t i) -> p t q i", t=4, i=8)
 
-        s_sb, p_sb, q_sb, h_bf, pooled = {}, {}, {}, {}, {}
+        b_sb, c_sb, c_ps, a_ps, q_sb, h_bf = {}, {}, {}, {}, {}, {}
 
-        def tag_of(key):
-            return REUSE.get(key, key)
+        def runs(ap):
+            return ap.rearrange("p t (q i) -> p t q i", i=8)
 
-        def runs(tile):
-            return tile[:].rearrange("p t (q i) -> p t q i", i=8)
-
-        def project_bc(j):
-            b_ps = project("b", j)
-            c_ps = project("c", j)
-            b_sb = keep.tile([P, 4, P], F32, name="b%d" % j)
-            nc.scalar.copy(runs(b_sb), b_ps)
-            return b_sb, c_ps
-
-        def sum_and_product_tiles(j):
-            s_sb[j] = keep.tile([P, 4, P], F32, name="s%d" % j, tag=tag_of("s%d" % j), align_bytes=64)
-            p_sb[j] = keep.tile([P, 4, P], F32, name="p%d" % j, tag=tag_of("p%d" % j), align_bytes=64)
-
-        def pair_bc(j):
-            b_sb, c_ps = project_bc(j)
-            c_sb = keep.tile([P, 4, P], F32, name="c%d" % j)
-            nc.scalar.copy(runs(c_sb), c_ps)
-            sum_and_product_tiles(j)
-            nc.gpsimd.tensor_tensor(s_sb[j][:], c_sb[:], b_sb[:], ADD)
-            pooled[j] = b_sb, c_sb
-
-        def combine_on_vector(j, b_sb, c_ps):
-            sum_and_product_tiles(j)
-            nc.vector.tensor_tensor(runs(s_sb[j]), c_ps, runs(b_sb), ADD)
-            nc.vector.tensor_tensor(runs(p_sb[j]), c_ps, runs(b_sb), MULT)
+        def copy_out(name, j, slot, sb):
+            nc.scalar.copy(runs(sb), project(name, j, slot))
+            return sb
 
         out_v = out.rearrange("(h p) j -> p h j", p=P)
 
         def times_a(j):
-            a_ps = project("a", j)
-            q_sb[j] = keep.tile([P, 4, P], F32, name="q%d" % j, tag=tag_of("q%d" % j), align_bytes=64)
-            nc.vector.tensor_tensor(runs(q_sb[j]), a_ps, runs(s_sb[j]), MULT)
+            q_sb[j] = keep.tile([P, 4, P], F32, name="q%d" % j)
+            nc.vector.tensor_tensor(runs(q_sb[j][:]), a_ps[j], runs(sp[:, j, 0]), MULT)
 
-        def turn(j, g):
-            h_ps = psum.tile([P, 4, P], F32, tag="h", bufs=NH, name="h_ps")
+        def turn(j, g, slot):
+            h_ps = psum.tile([P, 4, P], F32, tag="bank%d" % slot, name="h_ps")
             for t in range(4):
-                nc.tensor.matmul(h_ps[:, t, :], p_sb[j][:, t, :], ident[:], start=True, stop=False, is_transpose=True)
+                nc.tensor.matmul(h_ps[:, t, :], sp[:, j, 1, t, :], ident[:], start=True, stop=False, is_transpose=True)
                 nc.tensor.matmul(h_ps[:, t, :], q_sb[j][:, t, :], ident[:], start=False, stop=True, is_transpose=True)
             if g not in h_bf:
                 h_bf[g] = keep.tile([P, len(g) * P, 4], BF16, name="h_bf%d" % g[0], align_bytes=64)
             c0 = (j - g[0]) * P
             nc.scalar.copy(h_bf[g][:, c0 : c0 + P, :], h_ps[:].rearrange("p t j -> p j t"))
 
-        def rate(g):
+        def rate(g, slots, tag):
             w, j0 = len(g) * P, g[0] * P
-            h_w = keep.tile([P, w], U32, name="h_w%d" % g[0], tag=tag_of("h%d" % g[0]), align_bytes=64)
+            h_w = keep.tile([P, w], U32, name="h_w%d" % g[0], tag=tag, align_bytes=64)
             h_sc = keep.tile([P, w], U8, name="h_sc%d" % g[0], align_bytes=64)
-            nc.vector.quantize_mx(h_w[:].bitcast(FP8X4), h_sc[:], h_bf[g][:].rearrange("p j t -> p (j t)"))
-            y_ps = psum.tile([P, 2, w], F32, tag=Y_BANKS[g[0]], name="y_ps")
+            quantize(h_w[:], h_sc[:], h_bf[g][:])
             y_sb = keep.tile([P, 2, w], F32, name="y_sb%d" % g[0])
             for h in range(2):
+                y_ps = psum.tile([P, w], F32, tag="bank%d" % slots[h], name="y_ps")
                 nc.tensor.matmul_mx(
-                    y_ps[:, h, :],
+                    y_ps[:],
                     lhsT=wr_w[:, h * P : (h + 1) * P].bitcast(FP8X4),
                     lhsT_scale=wr_sc[:, h * P : (h + 1) * P],
                     rhs=h_w[:].bitcast(FP8X4),
@@ -224,46 +193,63 @@ def tile_list_fm_rating_kernel(
                     start=True,
                     stop=True,
                 )
-            for h in range(2):
-                nc.scalar.activation(y_sb[:, h, :], y_ps[:, h, :], IDENT, bias=bias_sb[:, h : h + 1])
+                if h == 0 or len(g) > 1:
+                    nc.scalar.activation(y_sb[:, h, :], y_ps[:], IDENT, bias=bias_sb[:, h : h + 1])
+                else:
+                    nc.vector.tensor_scalar_add(y_sb[:, h, :], y_ps[:], bias_sb[:, h : h + 1])
             nc.sync.dma_start(out_v[:, :, j0 : j0 + w], y_sb[:])
 
         gather_scales("c")
         nc.gpsimd.dma_start(c1_sc[0:100, :].bitcast(I32), sc["c"][4:104, :].bitcast(I32))
         gather_scales("b")
-        gather_words("b", 0, (0, 1))
-        gather_words("c", 0, (0, 1))
-        for ch in range(CHUNKS):
-            gather_words("b", 1, (ch,))
-            gather_words("c", 1, (ch,))
+        for a in range(PASSES):
+            gather_words("b", a, (0, 1))
+            gather_words("c", a, (0, 1))
         gather_scales("a")
-        gather_words("a", 0, (0,))
+        gather_words("a", 0, (0, 1))
         gather_words("a", 1, (0,))
-        for j in BC_ORDER[:2]:
-            pair_bc(j)
         for u in range(2):
             cast_weight(nc.scalar.copy, wu_bf[:, HALF * u : HALF * (u + 1), :], raw[u][:])
-        cast_weight(nc.vector.tensor_copy, wu_bf[:, H:, :], raw[2][:])
+        cast_weight(nc.scalar.copy, wu_bf[:, H:, :], raw[2][:])
         quantize(wu_w[:].rearrange("p a e -> p (a e)"), wu_sc[:].rearrange("p a e -> p (a e)"), wu_bf[:])
-        late = keep.tile([P, PASSES, CHUNK], U32, tag="wu_bf", align_bytes=64)
-        for a in range(PASSES):
-            gather_words("a", a, (1,), late[:, a, :])
-        for j in BC_ORDER[2:6]:
-            pair_bc(j)
-        held = {j: project_bc(j) for j in VECTOR_TILES}
-        for j in BC_ORDER[:6]:
-            nc.gpsimd.tensor_tensor(p_sb[j][:], pooled[j][1][:], pooled[j][0][:], MULT)
-        cast_weight(nc.scalar.copy, wr_bf[:], raw[3][:])
+        cast_weight(nc.scalar.copy, wr_bf[:], wr_raw[:])
         quantize(wr_w[:], wr_sc[:], wr_bf[:])
-        for j in range(3):
+        late = keep.tile([P, CHUNK], U32, tag="wu_bf", align_bytes=64)
+        gather_words("a", 1, (1,), late[:])
+
+        b_early = keep.tile([P, TPC, 4, P], F32)
+        for j in range(TPC):
+            b_sb[j] = copy_out("b", j, j, b_early[:, j])
+        for j in range(TPC):
+            c_ps[j] = project("c", j, j)
+        bc_late = keep.tile([P, TPC, 2, 4, P], F32, tag="raw2")
+        ring = {"b4": 4, "c4": 5, "b5": 6, "c5": 7, "a0": 4, "b6": 5, "c6": 6, "b7": 7, "c7": 5, "a1": 6, "a2": 7}
+        for key, slot in ring.items():
+            name, j = key[0], int(key[1])
+            if name == "a":
+                a_ps[j] = project("a", j, slot)
+            else:
+                (b_sb if name == "b" else c_sb)[j] = copy_out(name, j, slot, bc_late[:, j - TPC, int(name == "c")])
+
+        sp = keep.tile([P, TILES, 2, 4, P], F32, tag="tab_w1")
+        for j in range(TPC, TILES):
+            nc.gpsimd.tensor_tensor(sp[:, j, 0], c_sb[j], b_sb[j], ADD)
+            nc.gpsimd.tensor_tensor(sp[:, j, 1], c_sb[j], b_sb[j], MULT)
+        a_ps[4] = project("a", 4, 5)
+        for j in range(TPC):
+            nc.vector.tensor_tensor(runs(sp[:, j, 0]), c_ps[j], runs(b_sb[j]), ADD)
+            nc.vector.tensor_tensor(runs(sp[:, j, 1]), c_ps[j], runs(b_sb[j]), MULT)
             times_a(j)
-        turn(0, GROUPS[0])
-        for j in VECTOR_TILES:
-            combine_on_vector(j, *held[j])
-        for j in range(3, TILES):
+            follower, slot = ((3, 4), (5, 6), (6, 7), (7, 4))[j]
+            a_ps[follower] = project("a", follower, slot)
+            turn(j, GROUPS[0], j)
+        for j in range(TPC, TILES):
             times_a(j)
-        for g in GROUPS:
-            for j in g:
-                if j > 0:
-                    turn(j, g)
-            rate(g)
+        for j in (4, 5):
+            turn(j, GROUPS[1], j - TPC)
+        rate(GROUPS[0], (5, 6), "h_w0")
+        turn(6, GROUPS[2], 2)
+        turn(7, GROUPS[3], 3)
+        rate(GROUPS[1], (7, 4), "h_w4")
+        rate(GROUPS[2], (0, 1), "h_w6")
+        rate(GROUPS[3], (5, 6), "h_w7")

@@ -52,7 +52,7 @@ def tile_list_fm_rating_kernel(
         tab_w = [keep.tile([P, T], I32, name="tab_w%d" % a, tag="tab_w%d" % a) for a in range(PASSES)]
         wi_w = keep.tile([P, PASSES, H], I32, align_bytes=64)
         wc_w = keep.tile([P, PASSES, 2 * H], U8, align_bytes=64)
-        raw = [keep.tile([P, 4, w], F32, name="raw%d" % u, tag="raw%d" % u) for u, w in enumerate((HALF, HALF, H))]
+        raw = [keep.tile([P, 4, w], F32, name="raw%d" % u, tag="raw%d" % u, align_bytes=64) for u, w in enumerate((HALF, HALF, H))]
         bias_sb = keep.tile([P, 2], F32)
 
         def load_table(a, half):
@@ -60,13 +60,11 @@ def tile_list_fm_rating_kernel(
             nc.sync.dma_start(tab_w[a][:, cols], tab_words[a].rearrange("p t i -> p (t i)").bitcast(I32)[:, cols])
 
         nc.sync.dma_start(lists["c"][:], offs3)
-        for q in range(4):
-            nc.sync.dma_start(
-                tab_sc[32 * q : 32 * q + 8, :].bitcast(I32), tab_scales[:, 4 * q : 4 * q + 4, :].bitcast(I32)
-            )
         nc.sync.dma_start(lists["b"][:], offs2)
-        with nc.allow_non_contiguous_dma(reason="one bias value a partition"):
-            nc.sync.dma_start(bias_sb[:], bias.rearrange("(h p) -> p h", p=P))
+        nc.sync.dma_start(lists["a"][:], offs)
+        for r in range(4):
+            for a in range(PASSES):
+                nc.sync.dma_start(tab_sc[4 * a + r : P : 32, :].bitcast(I32), tab_scales[a, r:16:4, :].bitcast(I32))
         load_table(0, 0)
         for q in range(4):
             nc.sync.dma_start(
@@ -80,7 +78,6 @@ def tile_list_fm_rating_kernel(
             )
         load_table(1, 0)
         load_table(1, 1)
-        nc.sync.dma_start(lists["a"][:], offs)
         nc.sync.dma_start(wi_w[:], wi_words.rearrange("a p e i -> p a (e i)").bitcast(I32))
         nc.sync.dma_start(wc_w[:].bitcast(I32), wc_words.rearrange("a p e -> p a e").bitcast(I32))
         for u in range(2):
@@ -91,6 +88,8 @@ def tile_list_fm_rating_kernel(
         wr_v = wr.rearrange("(q t i) n -> t q i n", t=4, i=8)
         for t in range(4):
             nc.sync.dma_start(wr_raw[:, t, :], wr_v[t])
+        with nc.allow_non_contiguous_dma(reason="one bias value a partition"):
+            nc.sync.dma_start(bias_sb[:], bias.rearrange("(h p) -> p h", p=P))
 
         ident = keep.tile([P, P], F32)
         make_identity(nc, ident[:])
@@ -119,8 +118,8 @@ def tile_list_fm_rating_kernel(
         wr_w = keep.tile([P, N], U32, align_bytes=64)
         wr_sc = keep.tile([P, N], U8, align_bytes=64)
 
-        wu_bf = keep.tile([P, PASSES * H, 4], BF16, tag="wu_bf", align_bytes=64)
-        wr_bf = keep.tile([P, N, 4], BF16, align_bytes=64)
+        w_bf = keep.tile([P, PASSES * H + N, 4], BF16, tag="wu_bf", align_bytes=64)
+        wu_bf, wr_bf = w_bf[:, : PASSES * H, :], w_bf[:, PASSES * H :, :]
 
         def cast_weight(copy, dst, rows):
             copy(dst.rearrange("p (c i) t -> p c t i", i=4), rows.rearrange("p t (c i) -> p c t i", i=4))
@@ -202,27 +201,30 @@ def tile_list_fm_rating_kernel(
         gather_scales("c")
         nc.gpsimd.dma_start(c1_sc[0:100, :].bitcast(I32), sc["c"][4:104, :].bitcast(I32))
         gather_scales("b")
-        for a in range(PASSES):
-            gather_words("b", a, (0, 1))
-            gather_words("c", a, (0, 1))
         gather_scales("a")
-        gather_words("a", 0, (0, 1))
+        gather_words("b", 0, (0, 1))
+        gather_words("c", 0, (0, 1))
+        for ch in range(CHUNKS):
+            gather_words("b", 1, (ch,))
+            gather_words("c", 1, (ch,))
         gather_words("a", 1, (0,))
         for u in range(2):
             cast_weight(nc.scalar.copy, wu_bf[:, HALF * u : HALF * (u + 1), :], raw[u][:])
+        a_first = keep.tile([P, S], U32, tag="raw0", align_bytes=64)
+        gather_words("a", 0, (0, 1), a_first[:])
         cast_weight(nc.scalar.copy, wu_bf[:, H:, :], raw[2][:])
-        quantize(wu_w[:].rearrange("p a e -> p (a e)"), wu_sc[:].rearrange("p a e -> p (a e)"), wu_bf[:])
-        cast_weight(nc.scalar.copy, wr_bf[:], wr_raw[:])
-        quantize(wr_w[:], wr_sc[:], wr_bf[:])
+        quantize(wu_w[:].rearrange("p a e -> p (a e)"), wu_sc[:].rearrange("p a e -> p (a e)"), wu_bf)
+        cast_weight(nc.scalar.copy, wr_bf, wr_raw[:])
+        quantize(wr_w[:], wr_sc[:], wr_bf)
         late = keep.tile([P, CHUNK], U32, tag="wu_bf", align_bytes=64)
         gather_words("a", 1, (1,), late[:])
 
-        b_early = keep.tile([P, TPC, 4, P], F32)
+        b_early = keep.tile([P, 2, 4, P], F32, tag="raw1", align_bytes=64)
+        bc_late = keep.tile([P, TPC + 1, 2, 4, P], F32, tag="raw2", align_bytes=64)
         for j in range(TPC):
-            b_sb[j] = copy_out("b", j, j, b_early[:, j])
+            b_sb[j] = copy_out("b", j, j, b_early[:, j] if j < 2 else bc_late[:, TPC, j - 2])
         for j in range(TPC):
             c_ps[j] = project("c", j, j)
-        bc_late = keep.tile([P, TPC, 2, 4, P], F32, tag="raw2")
         ring = {"b4": 4, "c4": 5, "b5": 6, "c5": 7, "a0": 4, "b6": 5, "c6": 6, "b7": 7, "c7": 5, "a1": 6, "a2": 7}
         for key, slot in ring.items():
             name, j = key[0], int(key[1])

@@ -25,8 +25,8 @@ CHUNKS = S // CHUNK
 TILES = S // P
 TPC = CHUNK // P
 HALF = H // 2
-GROUPS = ((0, 1, 2, 3), (4, 5), (6,), (7,))
-BANKS = 8
+GROUPS = ((0, 1, 2, 3), (4, 5), (6, 7))
+WORD_TILES = (6, 7)
 
 
 def tile_list_fm_rating_kernel(
@@ -148,39 +148,68 @@ def tile_list_fm_rating_kernel(
                     start=(a == 0),
                     stop=(a == PASSES - 1),
                 )
+            if j in WORD_TILES:
+                return bank[:].rearrange("p (q u e i) -> p u q i e", u=2, e=2, i=8)
             return bank[:].rearrange("p (q t i) -> p t q i", t=4, i=8)
 
         b_sb, c_sb, c_ps, a_ps, q_sb, h_bf = {}, {}, {}, {}, {}, {}
 
-        def runs(ap):
+        def runs(ap, j):
+            if j in WORD_TILES:
+                return ap.rearrange("p t c -> p (t c)").rearrange("p (u q i e) -> p u q i e", u=2, e=2, i=8)
             return ap.rearrange("p t (q i) -> p t q i", i=8)
 
         def copy_out(name, j, slot, sb):
-            nc.scalar.copy(runs(sb), project(name, j, slot))
+            nc.scalar.copy(runs(sb, j), project(name, j, slot))
             return sb
 
         out_v = out.rearrange("(h p) j -> p h j", p=P)
 
+        q_early = keep.tile([P, TILES - 2, 4, P], F32)
+        q_last = keep.tile([P, 2, 4, P], F32, tag="q_last", align_bytes=64)
+
         def times_a(j):
-            q_sb[j] = keep.tile([P, 4, P], F32, name="q%d" % j)
-            nc.vector.tensor_tensor(runs(q_sb[j][:]), a_ps[j], runs(sp[:, j, 0]), MULT)
+            q_sb[j] = q_last[:, j - 6] if j in WORD_TILES else q_early[:, j]
+            q_v, a_v, s_v = runs(q_sb[j], j), a_ps[j], runs(s_sb[j], j)
+            if j in WORD_TILES:
+                for u in range(2):
+                    nc.vector.tensor_tensor(q_v[:, u], a_v[:, u], s_v[:, u], MULT)
+            else:
+                nc.vector.tensor_tensor(q_v, a_v, s_v, MULT)
 
         def turn(j, g, slot):
             h_ps = psum.tile([P, 4, P], F32, tag="bank%d" % slot, name="h_ps")
             for t in range(4):
-                nc.tensor.matmul(h_ps[:, t, :], sp[:, j, 1, t, :], ident[:], start=True, stop=False, is_transpose=True)
-                nc.tensor.matmul(h_ps[:, t, :], q_sb[j][:, t, :], ident[:], start=False, stop=True, is_transpose=True)
+                nc.tensor.matmul(h_ps[:, t, :], q_sb[j][:, t, :], ident[:], start=True, stop=False, is_transpose=True)
+                nc.tensor.matmul(h_ps[:, t, :], p_sb[j][:, t, :], ident[:], start=False, stop=True, is_transpose=True)
             if g not in h_bf:
-                h_bf[g] = keep.tile([P, len(g) * P, 4], BF16, name="h_bf%d" % g[0], align_bytes=64)
+                h_bf[g] = keep.tile([P, len(g) * P, 4], BF16, name="h_bf%d" % g[0], tag="h_bf%d" % g[0], align_bytes=64)
             c0 = (j - g[0]) * P
             nc.scalar.copy(h_bf[g][:, c0 : c0 + P, :], h_ps[:].rearrange("p t j -> p j t"))
 
-        def rate(g, slots, tag):
-            w, j0 = len(g) * P, g[0] * P
+        def add_and_turn_words(g, slot):
+            pairs = keep.tile([P, 2, 4, P], BF16)
+            nc.vector.tensor_tensor(pairs[:], q_last[:], room[:, 10:12], ADD)
+            words_in = pairs[:].rearrange("p n t c -> p (n t c)").bitcast(F32)
+            h_ps = psum.tile([P, 4, P], F32, tag="bank%d" % slot, name="h_ps")
+            for n in range(4):
+                nc.tensor.transpose(h_ps[:, n, :], words_in[:, n * P : (n + 1) * P], ident[:])
+            h_bf[g] = keep.tile([P, 2 * P, 4], BF16, name="h_bf6", tag="h_bf6", align_bytes=64)
+            nc.scalar.copy(
+                h_bf[g][:].bitcast(F32).rearrange("p (n j) u -> p n j u", n=2),
+                h_ps[:].rearrange("p (n u) j -> p n j u", u=2),
+            )
+
+        def quantize_h(g, tag):
+            w = len(g) * P
             h_w = keep.tile([P, w], U32, name="h_w%d" % g[0], tag=tag, align_bytes=64)
             h_sc = keep.tile([P, w], U8, name="h_sc%d" % g[0], align_bytes=64)
             quantize(h_w[:], h_sc[:], h_bf[g][:])
-            y_sb = keep.tile([P, 2, w], F32, name="y_sb%d" % g[0])
+            return h_w, h_sc
+
+        def rate(g, slots, tag, on_scalar, h_w, h_sc):
+            w, j0 = len(g) * P, g[0] * P
+            y_sb = keep.tile([P, 2, w], F32, name="y_sb%d" % g[0], tag=tag, align_bytes=64)
             for h in range(2):
                 y_ps = psum.tile([P, w], F32, tag="bank%d" % slots[h], name="y_ps")
                 nc.tensor.matmul_mx(
@@ -192,11 +221,11 @@ def tile_list_fm_rating_kernel(
                     start=True,
                     stop=True,
                 )
-                if h == 0 or len(g) > 1:
+                if h < on_scalar:
                     nc.scalar.activation(y_sb[:, h, :], y_ps[:], IDENT, bias=bias_sb[:, h : h + 1])
                 else:
                     nc.vector.tensor_scalar_add(y_sb[:, h, :], y_ps[:], bias_sb[:, h : h + 1])
-            nc.sync.dma_start(out_v[:, :, j0 : j0 + w], y_sb[:])
+                nc.sync.dma_start(out_v[:, h, j0 : j0 + w], y_sb[:, h, :])
 
         gather_scales("c")
         nc.gpsimd.dma_start(c1_sc[0:100, :].bitcast(I32), sc["c"][4:104, :].bitcast(I32))
@@ -207,7 +236,7 @@ def tile_list_fm_rating_kernel(
         for ch in range(CHUNKS):
             gather_words("b", 1, (ch,))
             gather_words("c", 1, (ch,))
-        gather_words("a", 1, (0,))
+        gather_words("a", 1, (0, 1))
         for u in range(2):
             cast_weight(nc.scalar.copy, wu_bf[:, HALF * u : HALF * (u + 1), :], raw[u][:])
         a_first = keep.tile([P, S], U32, tag="raw0", align_bytes=64)
@@ -216,8 +245,6 @@ def tile_list_fm_rating_kernel(
         quantize(wu_w[:].rearrange("p a e -> p (a e)"), wu_sc[:].rearrange("p a e -> p (a e)"), wu_bf)
         cast_weight(nc.scalar.copy, wr_bf, wr_raw[:])
         quantize(wr_w[:], wr_sc[:], wr_bf)
-        late = keep.tile([P, CHUNK], U32, tag="wu_bf", align_bytes=64)
-        gather_words("a", 1, (1,), late[:])
 
         b_early = keep.tile([P, 2, 4, P], F32, tag="raw1", align_bytes=64)
         bc_late = keep.tile([P, TPC + 1, 2, 4, P], F32, tag="raw2", align_bytes=64)
@@ -225,33 +252,34 @@ def tile_list_fm_rating_kernel(
             b_sb[j] = copy_out("b", j, j, b_early[:, j] if j < 2 else bc_late[:, TPC, j - 2])
         for j in range(TPC):
             c_ps[j] = project("c", j, j)
-        ring = {"b4": 4, "c4": 5, "b5": 6, "c5": 7, "a0": 4, "b6": 5, "c6": 6, "b7": 7, "c7": 5, "a1": 6, "a2": 7}
-        for key, slot in ring.items():
-            name, j = key[0], int(key[1])
-            if name == "a":
-                a_ps[j] = project("a", j, slot)
-            else:
-                (b_sb if name == "b" else c_sb)[j] = copy_out(name, j, slot, bc_late[:, j - TPC, int(name == "c")])
-
-        sp = keep.tile([P, TILES, 2, 4, P], F32, tag="tab_w1")
         for j in range(TPC, TILES):
-            nc.gpsimd.tensor_tensor(sp[:, j, 0], c_sb[j], b_sb[j], ADD)
-            nc.gpsimd.tensor_tensor(sp[:, j, 1], c_sb[j], b_sb[j], MULT)
-        a_ps[4] = project("a", 4, 5)
+            b_sb[j] = copy_out("b", j, TPC + 2 * (j % 2), bc_late[:, j - TPC, 0])
+            c_sb[j] = copy_out("c", j, TPC + 2 * (j % 2) + 1, bc_late[:, j - TPC, 1])
         for j in range(TPC):
-            nc.vector.tensor_tensor(runs(sp[:, j, 0]), c_ps[j], runs(b_sb[j]), ADD)
-            nc.vector.tensor_tensor(runs(sp[:, j, 1]), c_ps[j], runs(b_sb[j]), MULT)
+            a_ps[j] = project("a", j, TPC + j)
+
+        room = keep.tile([P, 12, 4, P], F32, tag="wu_bf", align_bytes=64)
+        s_sb = [room[:, n] for n in (0, 1, 0, 0, 4, 5, 6, 7)]
+        p_sb = [room[:, n] for n in (2, 3, 1, 2, 8, 9, 10, 11)]
+
+        def combine_on_gpsimd(j):
+            nc.gpsimd.tensor_tensor(s_sb[j], c_sb[j], b_sb[j], ADD)
+            nc.gpsimd.tensor_tensor(p_sb[j], c_sb[j], b_sb[j], MULT)
+
+        for j in range(TPC, TILES):
+            combine_on_gpsimd(j)
+        for j in range(TPC):
+            nc.vector.tensor_tensor(runs(s_sb[j], j), c_ps[j], runs(b_sb[j], j), ADD)
+            nc.vector.tensor_tensor(runs(p_sb[j], j), c_ps[j], runs(b_sb[j], j), MULT)
             times_a(j)
-            follower, slot = ((3, 4), (5, 6), (6, 7), (7, 4))[j]
-            a_ps[follower] = project("a", follower, slot)
+            a_ps[TPC + j] = project("a", TPC + j, TPC + j)
             turn(j, GROUPS[0], j)
         for j in range(TPC, TILES):
             times_a(j)
         for j in (4, 5):
             turn(j, GROUPS[1], j - TPC)
-        rate(GROUPS[0], (5, 6), "h_w0")
-        turn(6, GROUPS[2], 2)
-        turn(7, GROUPS[3], 3)
-        rate(GROUPS[1], (7, 4), "h_w4")
-        rate(GROUPS[2], (0, 1), "h_w6")
-        rate(GROUPS[3], (5, 6), "h_w7")
+        add_and_turn_words(GROUPS[2], 2)
+        codes = [quantize_h(g, tag) for g, tag in zip(GROUPS, ("q_last", "h_bf0", "h_w6"))]
+        rate(GROUPS[0], (4, 5), "y_sb0", 2, *codes[0])
+        rate(GROUPS[1], (6, 7), "h_bf6", 0, *codes[1])
+        rate(GROUPS[2], (0, 1), "y_sb6", 1, *codes[2])

@@ -21,12 +21,9 @@ IDENT = mybir.ActivationFunctionType.Identity
 P = 128
 PASSES = K // 512
 CHUNK = 512
-CHUNKS = S // CHUNK
 TILES = S // P
 TPC = CHUNK // P
 HALF = H // 2
-GROUPS = ((0, 1, 2, 3), (4, 5), (6, 7))
-WORD_TILES = (6, 7)
 
 
 def tile_list_fm_rating_kernel(
@@ -37,27 +34,38 @@ def tile_list_fm_rating_kernel(
         keep = ctx.enter_context(tc.tile_pool(name="keep", bufs=1))
         psum = ctx.enter_context(tc.psum_pool(name="psum", bufs=1))
 
+        def sbuf(shape, dtype, name, tag=None):
+            return keep.tile([P] + shape, dtype, name=name, tag=tag or name, align_bytes=64)
+
+        def rows_of(count, name, tag=None):
+            tile = sbuf([count * H], F32, name, tag)
+            return [tile[:, n * H : (n + 1) * H] for n in range(count)]
+
         lists = {}
         for name in ("c", "b", "a"):
             lists[name] = keep.tile([P, S // 16], U16, name="list_" + name)
-        tab_sc = keep.tile([P, T], U8, align_bytes=64)
-        wi_sc = keep.tile([P, H], U8, align_bytes=64)
-        wc_sc = keep.tile([P, PASSES, H], U8, align_bytes=64)
-        c1_sc = keep.tile([P, S], U8, align_bytes=64)
+        tab_sc = sbuf([T], U8, "tab_sc")
+        wi_sc = sbuf([H], U8, "wi_sc")
+        wc_sc = sbuf([PASSES, H], U8, "wc_sc")
+        c1_sc = sbuf([S], U8, "c1_sc")
         nc.vector.memset(tab_sc[:].bitcast(I32), 0)
         nc.vector.memset(wi_sc[:].bitcast(I32), 0)
         nc.vector.memset(wc_sc[:].rearrange("p a e -> p (a e)").bitcast(I32), 0)
         nc.vector.memset(c1_sc[:].bitcast(I32), 0)
 
-        tab_w = [keep.tile([P, T], I32, name="tab_w%d" % a, tag="tab_w%d" % a) for a in range(PASSES)]
-        wi_w = keep.tile([P, PASSES, H], I32, align_bytes=64)
-        wc_w = keep.tile([P, PASSES, 2 * H], U8, align_bytes=64)
-        raw = [keep.tile([P, 4, w], F32, name="raw%d" % u, tag="raw%d" % u, align_bytes=64) for u, w in enumerate((HALF, HALF, H))]
+        tab_w = [sbuf([T], I32, "tab_w%d" % a) for a in range(PASSES)]
+        wi_w = sbuf([PASSES, H], I32, "wi_w")
+        wc_w = sbuf([PASSES, 2 * H], U8, "wc_w")
+        raw = [sbuf([4, HALF], F32, "raw%d" % u) for u in range(4)]
         bias_sb = keep.tile([P, 2], F32)
 
-        def load_table(a, half):
-            cols = slice(half * T // 2, (half + 1) * T // 2)
-            nc.sync.dma_start(tab_w[a][:, cols], tab_words[a].rearrange("p t i -> p (t i)").bitcast(I32)[:, cols])
+        def load_table(a):
+            nc.sync.dma_start(tab_w[a][:], tab_words[a].rearrange("p t i -> p (t i)").bitcast(I32))
+
+        def load_wu(u):
+            rows = slice(512 * (u // 2), 512 * (u // 2 + 1))
+            cols = slice(HALF * (u % 2), HALF * (u % 2 + 1))
+            nc.sync.dma_start(raw[u][:], wu[rows, cols].rearrange("(p j) e -> p j e", j=4))
 
         nc.sync.dma_start(lists["c"][:], offs3)
         nc.sync.dma_start(lists["b"][:], offs2)
@@ -65,24 +73,23 @@ def tile_list_fm_rating_kernel(
         for r in range(4):
             for a in range(PASSES):
                 nc.sync.dma_start(tab_sc[4 * a + r : P : 32, :].bitcast(I32), tab_scales[a, r:16:4, :].bitcast(I32))
-        load_table(0, 0)
         for q in range(4):
             nc.sync.dma_start(
                 wi_sc[32 * q : 32 * q + 8, :].bitcast(I32), wi_scales[:, 4 * q : 4 * q + 4, :].bitcast(I32)
             )
-        load_table(0, 1)
+        load_table(0)
+        nc.sync.dma_start(wi_w[:], wi_words.rearrange("a p e i -> p a (e i)").bitcast(I32))
+        nc.sync.dma_start(wc_w[:].bitcast(I32), wc_words.rearrange("a p e -> p a e").bitcast(I32))
         for q in range(4):
             nc.sync.dma_start(
                 wc_sc[32 * q : 32 * q + 4, :, :].bitcast(I32),
                 wc_scales[:, 4 * q : 4 * q + 4, :].rearrange("a r e -> r a e").bitcast(I32),
             )
-        load_table(1, 0)
-        load_table(1, 1)
-        nc.sync.dma_start(wi_w[:], wi_words.rearrange("a p e i -> p a (e i)").bitcast(I32))
-        nc.sync.dma_start(wc_w[:].bitcast(I32), wc_words.rearrange("a p e -> p a e").bitcast(I32))
-        for u in range(2):
-            nc.sync.dma_start(raw[u][:], wu[0:512, HALF * u : HALF * (u + 1)].rearrange("(p j) e -> p j e", j=4))
-        nc.sync.dma_start(raw[2][:], wu[512:1024, :].rearrange("(p j) e -> p j e", j=4))
+        load_wu(0)
+        load_wu(1)
+        load_table(1)
+        load_wu(2)
+        load_wu(3)
 
         wr_raw = keep.tile([P, 4, N], F32)
         wr_v = wr.rearrange("(q t i) n -> t q i n", t=4, i=8)
@@ -100,186 +107,228 @@ def tile_list_fm_rating_kernel(
         words = {}
 
         def gather_scales(name):
-            sc[name] = keep.tile([P, S], U8, name="sc_" + name, align_bytes=64)
+            sc[name] = sbuf([S], U8, "sc_" + name)
             nc.vector.tensor_copy(sc[name][:], tab_sc[:].indirect(lists[name][:]))
 
-        def gather_words(name, a, chunks, tile=None):
-            width = CHUNK * len(chunks)
-            if tile is None:
-                own = keep.tile([P, width], U32, name="w_%s%d%d" % (name, a, chunks[0]), align_bytes=64)
-                tile = own[:]
+        def gather_words(name, a, chunks, dst):
             for n, ch in enumerate(chunks):
-                words[name, a, ch] = tile[:, n * CHUNK : (n + 1) * CHUNK]
+                words[name, a, ch] = dst[:, n * CHUNK : (n + 1) * CHUNK]
             c0 = CHUNK // 16 * chunks[0]
-            nc.vector.tensor_copy(tile, tab_w[a][:].bitcast(U32).indirect(lists[name][:, c0 : c0 + width // 16]))
+            cols = slice(c0, c0 + len(chunks) * CHUNK // 16)
+            nc.vector.tensor_copy(dst, tab_w[a][:].bitcast(U32).indirect(lists[name][:, cols]))
 
-        wu_w = keep.tile([P, PASSES, H], U32, align_bytes=64)
-        wu_sc = keep.tile([P, PASSES, H], U8, align_bytes=64)
-        wr_w = keep.tile([P, N], U32, align_bytes=64)
-        wr_sc = keep.tile([P, N], U8, align_bytes=64)
+        wu_w = sbuf([PASSES, H], U32, "wu_w")
+        wu_sc = sbuf([PASSES, H], U8, "wu_sc")
+        wu_bf = sbuf([PASSES * H, 4], BF16, "wu_bf")
 
-        w_bf = keep.tile([P, PASSES * H + N, 4], BF16, tag="wu_bf", align_bytes=64)
-        wu_bf, wr_bf = w_bf[:, : PASSES * H, :], w_bf[:, PASSES * H :, :]
+        def cast_weight(dst, rows):
+            nc.scalar.copy(dst.rearrange("p (c i) t -> p c t i", i=4), rows.rearrange("p t (c i) -> p c t i", i=4))
 
-        def cast_weight(copy, dst, rows):
-            copy(dst.rearrange("p (c i) t -> p c t i", i=4), rows.rearrange("p t (c i) -> p c t i", i=4))
+        def quantize(codes, scales, values):
+            nc.vector.quantize_mx(codes.bitcast(FP8X4), scales, values.rearrange("p e t -> p (e t)"))
 
-        def quantize(words, scales, values):
-            nc.vector.quantize_mx(words.bitcast(FP8X4), scales, values.rearrange("p e t -> p (e t)"))
+        banks = {}
+
+        def open_bank(key, slot):
+            banks[key] = psum.tile([P, H], F32, tag="bank%d" % slot, name="bank")
+
+        def project_pass(name, j, a):
+            ch, c0 = j // TPC, (j % TPC) * P
+            cols = slice(j * P, (j + 1) * P)
+            if name == "a":
+                rhs, rhs_sc, lhs_sc = wu_w[:, a, :].bitcast(FP8X4), wu_sc[:, a, :], sc[name][4 * a :, cols]
+            elif name == "b":
+                rhs, rhs_sc, lhs_sc = wi_w[:, a, :].bitcast(FP8X4), wi_sc[4 * a :, :], sc[name][4 * a :, cols]
+            else:
+                rhs, rhs_sc = wc_w[:, a, :].bitcast(FP4X4), wc_sc[:, a, :]
+                lhs_sc = (sc["c"], c1_sc)[a][:, cols]
+            nc.tensor.matmul_mx(
+                banks[name, j][:],
+                lhsT=words[name, a, ch][:, c0 : c0 + P].bitcast(FP8X4),
+                lhsT_scale=lhs_sc,
+                rhs=rhs,
+                rhs_scale=rhs_sc,
+                start=(a == 0),
+                stop=(a == PASSES - 1),
+            )
 
         def project(name, j, slot):
-            ch, c0 = j // TPC, (j % TPC) * P
-            bank = psum.tile([P, H], F32, tag="bank%d" % slot, name="bank")
-            cols = slice(j * P, (j + 1) * P)
+            open_bank((name, j), slot)
             for a in range(PASSES):
-                if name == "a":
-                    rhs, rhs_sc, lhs_sc = wu_w[:, a, :].bitcast(FP8X4), wu_sc[:, a, :], sc[name][4 * a :, cols]
-                elif name == "b":
-                    rhs, rhs_sc, lhs_sc = wi_w[:, a, :].bitcast(FP8X4), wi_sc[4 * a :, :], sc[name][4 * a :, cols]
-                else:
-                    rhs, rhs_sc = wc_w[:, a, :].bitcast(FP4X4), wc_sc[:, a, :]
-                    lhs_sc = (sc["c"], c1_sc)[a][:, cols]
-                nc.tensor.matmul_mx(
-                    bank[:],
-                    lhsT=words[name, a, ch][:, c0 : c0 + P].bitcast(FP8X4),
-                    lhsT_scale=lhs_sc,
-                    rhs=rhs,
-                    rhs_scale=rhs_sc,
-                    start=(a == 0),
-                    stop=(a == PASSES - 1),
+                project_pass(name, j, a)
+
+        def in_psum(name, j):
+            return banks[name, j][:].rearrange("p (q t i) -> p t q i", t=4, i=8)
+
+        def runs(ap):
+            return ap.rearrange("p (t q i) -> p t q i", t=4, i=8)
+
+        held = {}
+
+        def copy_out(name, j, dst):
+            held[name, j] = dst
+            nc.scalar.copy(runs(dst), in_psum(name, j))
+
+        def on_vector(key, j, op, dst):
+            held[key, j] = dst
+            nc.vector.tensor_tensor(runs(dst), in_psum("c", j), runs(held["b", j]), op)
+
+        def on_gpsimd(key, j, op, dst):
+            held[key, j] = dst
+            nc.gpsimd.tensor_tensor(dst, held["c", j], held["b", j], op)
+
+        q_sb = rows_of(TILES, "q_sb")
+
+        def times_a(j):
+            held["q", j] = q_sb[j]
+            nc.vector.tensor_tensor(runs(q_sb[j]), in_psum("a", j), runs(held["s", j]), MULT)
+
+        def turn(key, j, first):
+            for t in range(4):
+                cols = slice(t * P, (t + 1) * P)
+                nc.tensor.matmul(
+                    banks["h", j][:, cols],
+                    held[key, j][:, cols],
+                    ident[:],
+                    start=(first and t == 0),
+                    stop=(not first and t == 3),
+                    is_transpose=True,
                 )
-            if j in WORD_TILES:
-                return bank[:].rearrange("p (q u e i) -> p u q i e", u=2, e=2, i=8)
-            return bank[:].rearrange("p (q t i) -> p t q i", t=4, i=8)
 
-        b_sb, c_sb, c_ps, a_ps, q_sb, h_bf = {}, {}, {}, {}, {}, {}
-
-        def runs(ap, j):
-            if j in WORD_TILES:
-                return ap.rearrange("p t c -> p (t c)").rearrange("p (u q i e) -> p u q i e", u=2, e=2, i=8)
-            return ap.rearrange("p t (q i) -> p t q i", i=8)
-
-        def copy_out(name, j, slot, sb):
-            nc.scalar.copy(runs(sb, j), project(name, j, slot))
-            return sb
+        def round_h(j, dst):
+            copy = nc.vector.tensor_copy if j == 6 else nc.scalar.copy
+            copy(dst, banks["h", j][:].rearrange("p (t j) -> p j t", t=4))
 
         out_v = out.rearrange("(h p) j -> p h j", p=P)
 
-        q_early = keep.tile([P, TILES - 2, 4, P], F32)
-        q_last = keep.tile([P, 2, 4, P], F32, tag="q_last", align_bytes=64)
-
-        def times_a(j):
-            q_sb[j] = q_last[:, j - 6] if j in WORD_TILES else q_early[:, j]
-            q_v, a_v, s_v = runs(q_sb[j], j), a_ps[j], runs(s_sb[j], j)
-            if j in WORD_TILES:
-                for u in range(2):
-                    nc.vector.tensor_tensor(q_v[:, u], a_v[:, u], s_v[:, u], MULT)
-            else:
-                nc.vector.tensor_tensor(q_v, a_v, s_v, MULT)
-
-        def turn(j, g, slot):
-            h_ps = psum.tile([P, 4, P], F32, tag="bank%d" % slot, name="h_ps")
-            for t in range(4):
-                nc.tensor.matmul(h_ps[:, t, :], q_sb[j][:, t, :], ident[:], start=True, stop=False, is_transpose=True)
-                nc.tensor.matmul(h_ps[:, t, :], p_sb[j][:, t, :], ident[:], start=False, stop=True, is_transpose=True)
-            if g not in h_bf:
-                h_bf[g] = keep.tile([P, len(g) * P, 4], BF16, name="h_bf%d" % g[0], tag="h_bf%d" % g[0], align_bytes=64)
-            c0 = (j - g[0]) * P
-            nc.scalar.copy(h_bf[g][:, c0 : c0 + P, :], h_ps[:].rearrange("p t j -> p j t"))
-
-        def add_and_turn_words(g, slot):
-            pairs = keep.tile([P, 2, 4, P], BF16)
-            nc.vector.tensor_tensor(pairs[:], q_last[:], room[:, 10:12], ADD)
-            words_in = pairs[:].rearrange("p n t c -> p (n t c)").bitcast(F32)
-            h_ps = psum.tile([P, 4, P], F32, tag="bank%d" % slot, name="h_ps")
-            for n in range(4):
-                nc.tensor.transpose(h_ps[:, n, :], words_in[:, n * P : (n + 1) * P], ident[:])
-            h_bf[g] = keep.tile([P, 2 * P, 4], BF16, name="h_bf6", tag="h_bf6", align_bytes=64)
-            nc.scalar.copy(
-                h_bf[g][:].bitcast(F32).rearrange("p (n j) u -> p n j u", n=2),
-                h_ps[:].rearrange("p (n u) j -> p n j u", u=2),
+        def rate(j0, tiles, h, slot, on_scalar):
+            w = tiles * P
+            y_ps = psum.tile([P, w], F32, tag="bank%d" % slot, name="y_ps")
+            y_sb = sbuf([w], F32, "y_sb%d%d" % (j0, h))
+            cols = slice(N + j0 * P, N + j0 * P + w)
+            nc.tensor.matmul_mx(
+                y_ps[:],
+                lhsT=end_w[:, h * P : (h + 1) * P].bitcast(FP8X4),
+                lhsT_scale=end_sc[:, h * P : (h + 1) * P],
+                rhs=end_w[:, cols].bitcast(FP8X4),
+                rhs_scale=end_sc[:, cols],
+                start=True,
+                stop=True,
             )
-
-        def quantize_h(g, tag):
-            w = len(g) * P
-            h_w = keep.tile([P, w], U32, name="h_w%d" % g[0], tag=tag, align_bytes=64)
-            h_sc = keep.tile([P, w], U8, name="h_sc%d" % g[0], align_bytes=64)
-            quantize(h_w[:], h_sc[:], h_bf[g][:])
-            return h_w, h_sc
-
-        def rate(g, slots, tag, on_scalar, h_w, h_sc):
-            w, j0 = len(g) * P, g[0] * P
-            y_sb = keep.tile([P, 2, w], F32, name="y_sb%d" % g[0], tag=tag, align_bytes=64)
-            for h in range(2):
-                y_ps = psum.tile([P, w], F32, tag="bank%d" % slots[h], name="y_ps")
-                nc.tensor.matmul_mx(
-                    y_ps[:],
-                    lhsT=wr_w[:, h * P : (h + 1) * P].bitcast(FP8X4),
-                    lhsT_scale=wr_sc[:, h * P : (h + 1) * P],
-                    rhs=h_w[:].bitcast(FP8X4),
-                    rhs_scale=h_sc[:],
-                    start=True,
-                    stop=True,
-                )
-                if h < on_scalar:
-                    nc.scalar.activation(y_sb[:, h, :], y_ps[:], IDENT, bias=bias_sb[:, h : h + 1])
-                else:
-                    nc.vector.tensor_scalar_add(y_sb[:, h, :], y_ps[:], bias_sb[:, h : h + 1])
-                nc.sync.dma_start(out_v[:, h, j0 : j0 + w], y_sb[:, h, :])
+            if on_scalar:
+                nc.scalar.activation(y_sb[:], y_ps[:], IDENT, bias=bias_sb[:, h : h + 1])
+            else:
+                nc.vector.tensor_scalar_add(y_sb[:], y_ps[:], bias_sb[:, h : h + 1])
+            nc.sync.dma_start(out_v[:, h, j0 * P : j0 * P + w], y_sb[:])
 
         gather_scales("c")
         nc.gpsimd.dma_start(c1_sc[0:100, :].bitcast(I32), sc["c"][4:104, :].bitcast(I32))
         gather_scales("b")
         gather_scales("a")
-        gather_words("b", 0, (0, 1))
-        gather_words("c", 0, (0, 1))
-        for ch in range(CHUNKS):
-            gather_words("b", 1, (ch,))
-            gather_words("c", 1, (ch,))
-        gather_words("a", 1, (0, 1))
-        for u in range(2):
-            cast_weight(nc.scalar.copy, wu_bf[:, HALF * u : HALF * (u + 1), :], raw[u][:])
-        a_first = keep.tile([P, S], U32, tag="raw0", align_bytes=64)
-        gather_words("a", 0, (0, 1), a_first[:])
-        cast_weight(nc.scalar.copy, wu_bf[:, H:, :], raw[2][:])
-        quantize(wu_w[:].rearrange("p a e -> p (a e)"), wu_sc[:].rearrange("p a e -> p (a e)"), wu_bf)
-        cast_weight(nc.scalar.copy, wr_bf, wr_raw[:])
-        quantize(wr_w[:], wr_sc[:], wr_bf)
+        for name in ("a", "b", "c"):
+            gather_words(name, 0, (0, 1), sbuf([S], U32, "w0_" + name)[:])
+        for n, name in enumerate(("b", "c")):
+            for j in range(TPC):
+                open_bank((name, j), TPC * n + j)
+                project_pass(name, j, 0)
+        for ch in range(2):
+            for name in ("b", "c"):
+                gather_words(name, 1, (ch,), sbuf([CHUNK], U32, "w1_%s%d" % (name, ch))[:])
+        for name in ("b", "c"):
+            for j in range(TPC):
+                project_pass(name, j, 1)
 
-        b_early = keep.tile([P, 2, 4, P], F32, tag="raw1", align_bytes=64)
-        bc_late = keep.tile([P, TPC + 1, 2, 4, P], F32, tag="raw2", align_bytes=64)
-        for j in range(TPC):
-            b_sb[j] = copy_out("b", j, j, b_early[:, j] if j < 2 else bc_late[:, TPC, j - 2])
-        for j in range(TPC):
-            c_ps[j] = project("c", j, j)
-        for j in range(TPC, TILES):
-            b_sb[j] = copy_out("b", j, TPC + 2 * (j % 2), bc_late[:, j - TPC, 0])
-            c_sb[j] = copy_out("c", j, TPC + 2 * (j % 2) + 1, bc_late[:, j - TPC, 1])
-        for j in range(TPC):
-            a_ps[j] = project("a", j, TPC + j)
+        def cast_wu(u):
+            cast_weight(wu_bf[:, HALF * u : HALF * (u + 1), :], raw[u][:])
 
-        room = keep.tile([P, 12, 4, P], F32, tag="wu_bf", align_bytes=64)
-        s_sb = [room[:, n] for n in (0, 1, 0, 0, 4, 5, 6, 7)]
-        p_sb = [room[:, n] for n in (2, 3, 1, 2, 8, 9, 10, 11)]
+        cast_wu(0)
+        cast_wu(1)
+        b_two = sbuf([H], F32, "b_two")
+        early = rows_of(5, "early")
+        for name, j, dst in (
+            ("b", 0, early[0]),
+            ("b", 1, early[1]),
+            ("b", 2, b_two[:]),
+            ("b", 3, early[2]),
+            ("c", 0, early[3]),
+            ("c", 1, early[4]),
+        ):
+            copy_out(name, j, dst)
+        for slot, (name, j) in enumerate((("b", 4), ("b", 5), ("c", 4), ("c", 5), ("b", 6), ("c", 6))):
+            project(name, j, slot)
+        s_zero = sbuf([H], F32, "s_zero", "w1_c0")
+        first_room = rows_of(5, "first_room")
+        on_gpsimd("s", 0, ADD, s_zero[:])
+        on_gpsimd("s", 1, ADD, first_room[4])
+        for j in (2, 3):
+            on_vector("s", j, ADD, first_room[2 * j - 4])
+            on_vector("p", j, MULT, first_room[2 * j - 3])
+        project("b", 7, 6)
+        project("c", 7, 7)
+        gather_words("a", 1, (0,), sbuf([CHUNK], U32, "a_early", "b_two")[:])
+        cast_wu(2)
+        cast_wu(3)
+        quantize(wu_w[:].rearrange("p a e -> p (a e)"), wu_sc[:].rearrange("p a e -> p (a e)"), wu_bf[:])
+        late = rows_of(6, "late", "raw3")
+        for n, (name, j) in enumerate((("b", 4), ("b", 6), ("c", 6), ("b", 5), ("b", 7), ("c", 7))):
+            copy_out(name, j, late[n])
+        for j, slot in ((2, 4), (3, 5), (0, 6), (1, 7)):
+            project("a", j, slot)
+        for j in (2, 3):
+            open_bank(("h", j), j - 2)
+            turn("p", j, True)
+        mid_bf = sbuf([N + CHUNK, 4], BF16, "mid_bf")
+        cast_weight(mid_bf[:, :N, :], wr_raw[:])
 
-        def combine_on_gpsimd(j):
-            nc.gpsimd.tensor_tensor(s_sb[j], c_sb[j], b_sb[j], ADD)
-            nc.gpsimd.tensor_tensor(p_sb[j], c_sb[j], b_sb[j], MULT)
-
-        for j in range(TPC, TILES):
-            combine_on_gpsimd(j)
-        for j in range(TPC):
-            nc.vector.tensor_tensor(runs(s_sb[j], j), c_ps[j], runs(b_sb[j], j), ADD)
-            nc.vector.tensor_tensor(runs(p_sb[j], j), c_ps[j], runs(b_sb[j], j), MULT)
-            times_a(j)
-            a_ps[TPC + j] = project("a", TPC + j, TPC + j)
-            turn(j, GROUPS[0], j)
-        for j in range(TPC, TILES):
-            times_a(j)
+        room = rows_of(8, "room", "wu_bf")
+        for j in (0, 1):
+            on_gpsimd("p", j, MULT, room[j])
+        for j in (6, 7):
+            on_gpsimd("s", j, ADD, room[j - 4])
         for j in (4, 5):
-            turn(j, GROUPS[1], j - TPC)
-        add_and_turn_words(GROUPS[2], 2)
-        codes = [quantize_h(g, tag) for g, tag in zip(GROUPS, ("q_last", "h_bf0", "h_w6"))]
-        rate(GROUPS[0], (4, 5), "y_sb0", 2, *codes[0])
-        rate(GROUPS[1], (6, 7), "h_bf6", 0, *codes[1])
-        rate(GROUPS[2], (0, 1), "y_sb6", 1, *codes[2])
+            on_vector("s", j, ADD, room[2 * j - 4])
+            on_vector("p", j, MULT, room[2 * j - 3])
+        for j in (2, 3, 0, 1):
+            times_a(j)
+            if j < 2:
+                open_bank(("h", j), j + 2)
+                turn("p", j, True)
+            turn("q", j, False)
+            round_h(j, mid_bf[:, N + j * P : N + (j + 1) * P, :])
+
+        gather_words("a", 1, (1,), sbuf([CHUNK], U32, "a_late", "w1_c0")[:])
+        for j, slot in ((4, 4), (5, 5), (6, 0), (7, 1)):
+            project("a", j, slot)
+        for j in (4, 5):
+            open_bank(("h", j), j + 2)
+            turn("p", j, True)
+
+        end_w = sbuf([N + S], U32, "end_w", "tab_w1")
+        end_sc = sbuf([N + S], U8, "end_sc")
+        quantize(end_w[:, 512:768], end_sc[:, 512:768], mid_bf[:, 512:, :])
+        quantize(end_w[:, :512], end_sc[:, :512], mid_bf[:, :512, :])
+        last_room = rows_of(2, "last_room", "mid_bf")
+        for j in (6, 7):
+            on_gpsimd("p", j, MULT, last_room[j - 6])
+        rate(0, TPC, 0, 2, True)
+        rate(0, TPC, 1, 3, False)
+
+        end_bf = sbuf([CHUNK, 4], BF16, "end_bf")
+        for j in range(TPC, TILES):
+            times_a(j)
+            if j in (4, 5):
+                turn("q", j, False)
+            if j == 6:
+                open_bank(("h", 6), 4)
+                turn("p", 6, True)
+                turn("q", 6, False)
+            if j == 7:
+                open_bank(("h", 7), 5)
+                turn("q", 7, True)
+                turn("p", 7, False)
+            round_h(j, end_bf[:, (j - TPC) * P : (j - TPC + 1) * P, :])
+        for j0, slots in ((4, (2, 3)), (6, (0, 1))):
+            cols = slice(N + j0 * P, N + (j0 + 2) * P)
+            quantize(end_w[:, cols], end_sc[:, cols], end_bf[:, (j0 - TPC) * P : (j0 - TPC + 2) * P, :])
+            rate(j0, 2, 0, slots[0], True)
+            rate(j0, 2, 1, slots[1], j0 == 4)

@@ -32,6 +32,7 @@ def tile_list_fm_rating_kernel(
     nc = tc.nc
     with ExitStack() as ctx:
         keep = ctx.enter_context(tc.tile_pool(name="keep", bufs=1))
+        placed = ctx.enter_context(tc.tile_pool(name="placed", bufs=1))
         psum = ctx.enter_context(tc.psum_pool(name="psum", bufs=1))
 
         def sbuf(shape, dtype, name, tag=None):
@@ -56,7 +57,8 @@ def tile_list_fm_rating_kernel(
         tab_w = [sbuf([T], I32, "tab_w%d" % a) for a in range(PASSES)]
         wi_w = sbuf([PASSES, H], I32, "wi_w")
         wc_w = sbuf([PASSES, 2 * H], U8, "wc_w")
-        raw = [sbuf([4, HALF], F32, "raw%d" % u) for u in range(4)]
+        raw = {u: sbuf([4, HALF], F32, "raw%d" % u) for u in (0, 2, 3)}
+        raw[1] = placed.tile([P, 4, HALF], F32, name="raw1", align_bytes=64, offset=0)
         bias_sb = keep.tile([P, 2], F32)
 
         def load_table(a):
@@ -86,15 +88,10 @@ def tile_list_fm_rating_kernel(
                 wc_scales[:, 4 * q : 4 * q + 4, :].rearrange("a r e -> r a e").bitcast(I32),
             )
         load_wu(0)
-        load_wu(1)
         load_table(1)
-        load_wu(2)
-        load_wu(3)
+        for u in range(1, 4):
+            load_wu(u)
 
-        wr_raw = keep.tile([P, 4, N], F32)
-        wr_v = wr.rearrange("(q t i) n -> t q i n", t=4, i=8)
-        for t in range(4):
-            nc.sync.dma_start(wr_raw[:, t, :], wr_v[t])
         with nc.allow_non_contiguous_dma(reason="one bias value a partition"):
             nc.sync.dma_start(bias_sb[:], bias.rearrange("(h p) -> p h", p=P))
 
@@ -177,11 +174,9 @@ def tile_list_fm_rating_kernel(
             held[key, j] = dst
             nc.gpsimd.tensor_tensor(dst, held["c", j], held["b", j], op)
 
-        q_sb = rows_of(TILES, "q_sb")
-
-        def times_a(j):
-            held["q", j] = q_sb[j]
-            nc.vector.tensor_tensor(runs(q_sb[j]), in_psum("a", j), runs(held["s", j]), MULT)
+        def times_a(j, dst):
+            held["q", j] = dst
+            nc.vector.tensor_tensor(runs(dst), in_psum("a", j), runs(held["s", j]), MULT)
 
         def turn(key, j, first):
             for t in range(4):
@@ -243,18 +238,19 @@ def tile_list_fm_rating_kernel(
 
         cast_wu(0)
         cast_wu(1)
-        b_two = sbuf([H], F32, "b_two")
-        early = rows_of(5, "early")
+        b_two = placed.tile([P, H], F32, name="b_two", align_bytes=64, offset=0)
+        early_tile = placed.tile([P, 5 * H], F32, name="early", align_bytes=64, offset=4 * H)
+        early = [early_tile[:, n * H : (n + 1) * H] for n in range(5)]
         for name, j, dst in (
             ("b", 0, early[0]),
-            ("b", 1, early[1]),
             ("b", 2, b_two[:]),
-            ("b", 3, early[2]),
-            ("c", 0, early[3]),
-            ("c", 1, early[4]),
+            ("b", 3, early[4]),
+            ("c", 0, early[1]),
+            ("b", 1, early[2]),
+            ("c", 1, early[3]),
         ):
             copy_out(name, j, dst)
-        for slot, (name, j) in enumerate((("b", 4), ("b", 5), ("c", 4), ("c", 5), ("b", 6), ("c", 6))):
+        for name, j, slot in (("b", 4, 0), ("b", 5, 2), ("c", 4, 3), ("c", 5, 4), ("b", 6, 1), ("c", 6, 5)):
             project(name, j, slot)
         s_zero = sbuf([H], F32, "s_zero", "w1_c0")
         first_room = rows_of(5, "first_room")
@@ -265,69 +261,67 @@ def tile_list_fm_rating_kernel(
             on_vector("p", j, MULT, first_room[2 * j - 3])
         project("b", 7, 6)
         project("c", 7, 7)
-        gather_words("a", 1, (0,), sbuf([CHUNK], U32, "a_early", "b_two")[:])
+        a_early = placed.tile([P, CHUNK], U32, name="a_early", align_bytes=64, offset=0)
+        gather_words("a", 1, (0,), a_early[:])
         cast_wu(2)
+        wr_raw = sbuf([4, N], F32, "wr_raw", "raw2")
+        wr_v = wr.rearrange("(q t i) n -> t q i n", t=4, i=8)
+        for t in range(4):
+            nc.sync.dma_start(wr_raw[:, t, :], wr_v[t])
         cast_wu(3)
         quantize(wu_w[:].rearrange("p a e -> p (a e)"), wu_sc[:].rearrange("p a e -> p (a e)"), wu_bf[:])
         late = rows_of(6, "late", "raw3")
-        for n, (name, j) in enumerate((("b", 4), ("b", 6), ("c", 6), ("b", 5), ("b", 7), ("c", 7))):
+        for n, (name, j) in enumerate((("b", 6), ("b", 4), ("c", 6), ("b", 5), ("b", 7), ("c", 7))):
             copy_out(name, j, late[n])
-        for j, slot in ((2, 4), (3, 5), (0, 6), (1, 7)):
-            project("a", j, slot)
-        for j in (2, 3):
-            open_bank(("h", j), j - 2)
-            turn("p", j, True)
         mid_bf = sbuf([N + CHUNK, 4], BF16, "mid_bf")
         cast_weight(mid_bf[:, :N, :], wr_raw[:])
 
-        room = rows_of(8, "room", "wu_bf")
+        room = rows_of(4, "room", "wu_bf")
         for j in (0, 1):
             on_gpsimd("p", j, MULT, room[j])
         for j in (6, 7):
             on_gpsimd("s", j, ADD, room[j - 4])
-        for j in (4, 5):
-            on_vector("s", j, ADD, room[2 * j - 4])
-            on_vector("p", j, MULT, room[2 * j - 3])
+        second_room = rows_of(9, "second_room")
+        on_vector("s", 4, ADD, second_room[0])
+        on_vector("p", 4, MULT, second_room[1])
+        on_vector("p", 6, MULT, second_room[8])
+        on_vector("s", 5, ADD, second_room[2])
+        on_vector("p", 5, MULT, second_room[3])
+        for j, slot in ((2, 1), (3, 5), (0, 6), (1, 7)):
+            project("a", j, slot)
+        for j, slot in ((2, 0), (3, 2), (0, 3), (1, 4)):
+            open_bank(("h", j), slot)
+            turn("p", j, True)
         for j in (2, 3, 0, 1):
-            times_a(j)
-            if j < 2:
-                open_bank(("h", j), j + 2)
-                turn("p", j, True)
+            times_a(j, second_room[4 + j])
             turn("q", j, False)
             round_h(j, mid_bf[:, N + j * P : N + (j + 1) * P, :])
+        for j in (4, 5):
+            open_bank(("h", j), (1, 5)[j - 4])
+            turn("p", j, True)
 
         gather_words("a", 1, (1,), sbuf([CHUNK], U32, "a_late", "w1_c0")[:])
-        for j, slot in ((4, 4), (5, 5), (6, 0), (7, 1)):
+        for j, slot in ((4, 6), (5, 7), (6, 0), (7, 2)):
             project("a", j, slot)
-        for j in (4, 5):
-            open_bank(("h", j), j + 2)
-            turn("p", j, True)
 
         end_w = sbuf([N + S], U32, "end_w", "tab_w1")
         end_sc = sbuf([N + S], U8, "end_sc")
         quantize(end_w[:, 512:768], end_sc[:, 512:768], mid_bf[:, 512:, :])
         quantize(end_w[:, :512], end_sc[:, :512], mid_bf[:, :512, :])
-        last_room = rows_of(2, "last_room", "mid_bf")
-        for j in (6, 7):
-            on_gpsimd("p", j, MULT, last_room[j - 6])
-        rate(0, TPC, 0, 2, True)
-        rate(0, TPC, 1, 3, False)
+        last_room = rows_of(5, "last_room", "mid_bf")
+        on_gpsimd("p", 7, MULT, last_room[4])
+        rate(0, TPC, 0, 3, True)
+        rate(0, TPC, 1, 4, True)
 
         end_bf = sbuf([CHUNK, 4], BF16, "end_bf")
         for j in range(TPC, TILES):
-            times_a(j)
+            times_a(j, last_room[j - TPC])
+            turn("q", j, False)
             if j in (4, 5):
-                turn("q", j, False)
-            if j == 6:
-                open_bank(("h", 6), 4)
-                turn("p", 6, True)
-                turn("q", 6, False)
-            if j == 7:
-                open_bank(("h", 7), 5)
-                turn("q", 7, True)
-                turn("p", 7, False)
+                open_bank(("h", j + 2), j + 2)
+                turn("p", j + 2, True)
             round_h(j, end_bf[:, (j - TPC) * P : (j - TPC + 1) * P, :])
-        for j0, slots in ((4, (2, 3)), (6, (0, 1))):
+        for j0, slots in ((4, (3, 4)), (6, (0, 2))):
             cols = slice(N + j0 * P, N + (j0 + 2) * P)
             quantize(end_w[:, cols], end_sc[:, cols], end_bf[:, (j0 - TPC) * P : (j0 - TPC + 2) * P, :])
             rate(j0, 2, 0, slots[0], True)

@@ -55,19 +55,23 @@ def tile_list_fm_rating_kernel(
         nc.vector.memset(c1_sc[:].bitcast(I32), 0)
 
         tab_w = [sbuf([T], I32, "tab_w%d" % a) for a in range(PASSES)]
-        wi_w = sbuf([PASSES, H], I32, "wi_w")
-        wc_w = sbuf([PASSES, 2 * H], U8, "wc_w")
-        raw = {u: sbuf([4, HALF], F32, "raw%d" % u) for u in (0, 2, 3)}
-        raw[1] = placed.tile([P, 4, HALF], F32, name="raw1", align_bytes=64, offset=0)
+        wi_w = [sbuf([H], I32, "wi_w%d" % a) for a in range(PASSES)]
+        wc_w = [sbuf([2 * H], U8, "wc_w%d" % a) for a in range(PASSES)]
+        def at(offset, shape, dtype, name):
+            return placed.tile([P] + shape, dtype, name=name, align_bytes=64, offset=offset)
+
+        raw = [sbuf([4, H], F32, "raw0"), at(2048, [4, H], F32, "raw1")]
         bias_sb = keep.tile([P, 2], F32)
 
         def load_table(a):
             nc.sync.dma_start(tab_w[a][:], tab_words[a].rearrange("p t i -> p (t i)").bitcast(I32))
 
-        def load_wu(u):
-            rows = slice(512 * (u // 2), 512 * (u // 2 + 1))
-            cols = slice(HALF * (u % 2), HALF * (u % 2 + 1))
-            nc.sync.dma_start(raw[u][:], wu[rows, cols].rearrange("(p j) e -> p j e", j=4))
+        def load_weight_words(a):
+            nc.sync.dma_start(wi_w[a][:], wi_words[a].rearrange("p e i -> p (e i)").bitcast(I32))
+            nc.sync.dma_start(wc_w[a][:].bitcast(I32), wc_words[a].bitcast(I32))
+
+        def load_wu(a):
+            nc.sync.dma_start(raw[a][:], wu[512 * a : 512 * (a + 1), :].rearrange("(p j) e -> p j e", j=4))
 
         nc.sync.dma_start(lists["c"][:], offs3)
         nc.sync.dma_start(lists["b"][:], offs2)
@@ -80,8 +84,7 @@ def tile_list_fm_rating_kernel(
                 wi_sc[32 * q : 32 * q + 8, :].bitcast(I32), wi_scales[:, 4 * q : 4 * q + 4, :].bitcast(I32)
             )
         load_table(0)
-        nc.sync.dma_start(wi_w[:], wi_words.rearrange("a p e i -> p a (e i)").bitcast(I32))
-        nc.sync.dma_start(wc_w[:].bitcast(I32), wc_words.rearrange("a p e -> p a e").bitcast(I32))
+        load_weight_words(0)
         for q in range(4):
             nc.sync.dma_start(
                 wc_sc[32 * q : 32 * q + 4, :, :].bitcast(I32),
@@ -89,8 +92,12 @@ def tile_list_fm_rating_kernel(
             )
         load_wu(0)
         load_table(1)
-        for u in range(1, 4):
-            load_wu(u)
+        load_weight_words(1)
+        load_wu(1)
+        wr_raw = sbuf([4, N], F32, "wr_raw")
+        wr_v = wr.rearrange("(q t i) n -> t q i n", t=4, i=8)
+        for t in range(4):
+            nc.sync.dma_start(wr_raw[:, t, :], wr_v[t])
 
         with nc.allow_non_contiguous_dma(reason="one bias value a partition"):
             nc.sync.dma_start(bias_sb[:], bias.rearrange("(h p) -> p h", p=P))
@@ -135,9 +142,9 @@ def tile_list_fm_rating_kernel(
             if name == "a":
                 rhs, rhs_sc, lhs_sc = wu_w[:, a, :].bitcast(FP8X4), wu_sc[:, a, :], sc[name][4 * a :, cols]
             elif name == "b":
-                rhs, rhs_sc, lhs_sc = wi_w[:, a, :].bitcast(FP8X4), wi_sc[4 * a :, :], sc[name][4 * a :, cols]
+                rhs, rhs_sc, lhs_sc = wi_w[a][:].bitcast(FP8X4), wi_sc[4 * a :, :], sc[name][4 * a :, cols]
             else:
-                rhs, rhs_sc = wc_w[:, a, :].bitcast(FP4X4), wc_sc[:, a, :]
+                rhs, rhs_sc = wc_w[a][:].bitcast(FP4X4), wc_sc[:, a, :]
                 lhs_sc = (sc["c"], c1_sc)[a][:, cols]
             nc.tensor.matmul_mx(
                 banks[name, j][:],
@@ -233,14 +240,9 @@ def tile_list_fm_rating_kernel(
             for j in range(TPC):
                 project_pass(name, j, 1)
 
-        def cast_wu(u):
-            cast_weight(wu_bf[:, HALF * u : HALF * (u + 1), :], raw[u][:])
-
-        cast_wu(0)
-        cast_wu(1)
-        b_two = placed.tile([P, H], F32, name="b_two", align_bytes=64, offset=0)
-        early_tile = placed.tile([P, 5 * H], F32, name="early", align_bytes=64, offset=4 * H)
-        early = [early_tile[:, n * H : (n + 1) * H] for n in range(5)]
+        cast_weight(wu_bf[:, :H, :], raw[0][:])
+        b_two = sbuf([H], F32, "b_two")
+        early = rows_of(5, "early")
         for name, j, dst in (
             ("b", 0, early[0]),
             ("b", 2, b_two[:]),
@@ -253,28 +255,31 @@ def tile_list_fm_rating_kernel(
         for name, j, slot in (("b", 4, 0), ("b", 5, 2), ("c", 4, 3), ("c", 5, 4), ("b", 6, 1), ("c", 6, 5)):
             project(name, j, slot)
         s_zero = sbuf([H], F32, "s_zero", "w1_c0")
-        first_room = rows_of(5, "first_room")
+        first_room = rows_of(4, "first_room")
         on_gpsimd("s", 0, ADD, s_zero[:])
-        on_gpsimd("s", 1, ADD, first_room[4])
+        on_gpsimd("s", 1, ADD, sbuf([H], F32, "s_one")[:])
         for j in (2, 3):
             on_vector("s", j, ADD, first_room[2 * j - 4])
             on_vector("p", j, MULT, first_room[2 * j - 3])
-        project("b", 7, 6)
-        project("c", 7, 7)
-        a_early = placed.tile([P, CHUNK], U32, name="a_early", align_bytes=64, offset=0)
+        for j in (2, 3):
+            open_bank(("h", j), j + 4)
+            turn("p", j, True)
+        a_early = sbuf([CHUNK], U32, "a_early", "b_two")
         gather_words("a", 1, (0,), a_early[:])
-        cast_wu(2)
-        wr_raw = sbuf([4, N], F32, "wr_raw", "raw2")
-        wr_v = wr.rearrange("(q t i) n -> t q i n", t=4, i=8)
-        for t in range(4):
-            nc.sync.dma_start(wr_raw[:, t, :], wr_v[t])
-        cast_wu(3)
+        cast_weight(wu_bf[:, H:, :], raw[1][:])
         quantize(wu_w[:].rearrange("p a e -> p (a e)"), wu_sc[:].rearrange("p a e -> p (a e)"), wu_bf[:])
-        late = rows_of(6, "late", "raw3")
-        for n, (name, j) in enumerate((("b", 6), ("b", 4), ("c", 6), ("b", 5), ("b", 7), ("c", 7))):
-            copy_out(name, j, late[n])
-        mid_bf = sbuf([N + CHUNK, 4], BF16, "mid_bf")
-        cast_weight(mid_bf[:, :N, :], wr_raw[:])
+        b_four = at(2048, [H], F32, "b_four")
+        late_tile = at(4096, [5 * H], F32, "late")
+        late = [late_tile[:, n * H : (n + 1) * H] for n in range(5)]
+        for name, j, dst in (("b", 4, b_four[:]), ("b", 5, late[2]), ("b", 6, late[0]), ("c", 6, late[1])):
+            copy_out(name, j, dst)
+        for name, slot, dst in (("b", 0, late[3]), ("c", 2, late[4])):
+            project(name, 7, slot)
+            copy_out(name, 7, dst)
+        pair_bf = {j0: sbuf([2 * P, 4], BF16, "pair_bf%d" % j0) for j0 in (0, 2, 4, 6)}
+
+        def pair_slot(j):
+            return pair_bf[j - j % 2][:, (j % 2) * P : (j % 2 + 1) * P, :]
 
         room = rows_of(4, "room", "wu_bf")
         for j in (0, 1):
@@ -284,45 +289,54 @@ def tile_list_fm_rating_kernel(
         second_room = rows_of(9, "second_room")
         on_vector("s", 4, ADD, second_room[0])
         on_vector("p", 4, MULT, second_room[1])
-        on_vector("p", 6, MULT, second_room[8])
+        wr_bf = at(1024, [N, 4], BF16, "wr_bf")
+        cast_weight(wr_bf[:], wr_raw[:])
         on_vector("s", 5, ADD, second_room[2])
         on_vector("p", 5, MULT, second_room[3])
-        for j, slot in ((2, 1), (3, 5), (0, 6), (1, 7)):
+        on_vector("p", 6, MULT, second_room[8])
+        for j, slot in ((2, 1), (3, 3), (0, 0), (1, 4)):
             project("a", j, slot)
-        for j, slot in ((2, 0), (3, 2), (0, 3), (1, 4)):
+        for j, slot in ((0, 2), (1, 5)):
             open_bank(("h", j), slot)
             turn("p", j, True)
         for j in (2, 3, 0, 1):
             times_a(j, second_room[4 + j])
             turn("q", j, False)
-            round_h(j, mid_bf[:, N + j * P : N + (j + 1) * P, :])
+            round_h(j, pair_slot(j))
         for j in (4, 5):
-            open_bank(("h", j), (1, 5)[j - 4])
+            open_bank(("h", j), (0, 4)[j - 4])
             turn("p", j, True)
+        for j, slot in ((4, 1), (5, 3), (6, 6), (7, 7)):
+            open_bank(("a", j), slot)
+            project_pass("a", j, 0)
 
         gather_words("a", 1, (1,), sbuf([CHUNK], U32, "a_late", "w1_c0")[:])
-        for j, slot in ((4, 6), (5, 7), (6, 0), (7, 2)):
-            project("a", j, slot)
+        for j in range(TPC, TILES):
+            project_pass("a", j, 1)
 
-        end_w = sbuf([N + S], U32, "end_w", "tab_w1")
+        end_w = sbuf([N + S], U32, "end_w", "s_one")
         end_sc = sbuf([N + S], U8, "end_sc")
-        quantize(end_w[:, 512:768], end_sc[:, 512:768], mid_bf[:, 512:, :])
-        quantize(end_w[:, :512], end_sc[:, :512], mid_bf[:, :512, :])
-        last_room = rows_of(5, "last_room", "mid_bf")
-        on_gpsimd("p", 7, MULT, last_room[4])
-        rate(0, TPC, 0, 3, True)
-        rate(0, TPC, 1, 4, True)
 
-        end_bf = sbuf([CHUNK, 4], BF16, "end_bf")
+        def quantize_pair(j0):
+            cols = slice(N + j0 * P, N + (j0 + 2) * P)
+            quantize(end_w[:, cols], end_sc[:, cols], pair_bf[j0][:])
+
+        quantize(end_w[:, :N], end_sc[:, :N], wr_bf[:])
+        quantize_pair(2)
+        quantize_pair(0)
+        last_room = rows_of(5, "last_room", "pair_bf0")
+        on_gpsimd("p", 7, MULT, last_room[4])
+        rate(0, TPC, 0, 2, True)
+        rate(0, TPC, 1, 5, True)
+
         for j in range(TPC, TILES):
             times_a(j, last_room[j - TPC])
             turn("q", j, False)
             if j in (4, 5):
-                open_bank(("h", j + 2), j + 2)
+                open_bank(("h", j + 2), (1, 3)[j - 4])
                 turn("p", j + 2, True)
-            round_h(j, end_bf[:, (j - TPC) * P : (j - TPC + 1) * P, :])
-        for j0, slots in ((4, (3, 4)), (6, (0, 2))):
-            cols = slice(N + j0 * P, N + (j0 + 2) * P)
-            quantize(end_w[:, cols], end_sc[:, cols], end_bf[:, (j0 - TPC) * P : (j0 - TPC + 2) * P, :])
+            round_h(j, pair_slot(j))
+        for j0, slots in ((4, (2, 5)), (6, (6, 7))):
+            quantize_pair(j0)
             rate(j0, 2, 0, slots[0], True)
-            rate(j0, 2, 1, slots[1], j0 == 4)
+            rate(j0, 2, 1, slots[1], False)

@@ -24,6 +24,7 @@ CHUNK = 512
 TILES = S // P
 TPC = CHUNK // P
 HALF = H // 2
+WORD_TILES = (7,)
 
 
 def tile_list_fm_rating_kernel(
@@ -162,20 +163,32 @@ def tile_list_fm_rating_kernel(
                 project_pass(name, j, a)
 
         def in_psum(name, j):
+            if j in WORD_TILES:
+                return banks[name, j][:].rearrange("p (q u e i) -> p u q i e", u=2, e=2, i=8)
             return banks[name, j][:].rearrange("p (q t i) -> p t q i", t=4, i=8)
 
-        def runs(ap):
+        def runs(ap, j):
+            if j in WORD_TILES:
+                return ap.rearrange("p (u q i e) -> p u q i e", u=2, e=2, i=8)
             return ap.rearrange("p (t q i) -> p t q i", t=4, i=8)
+
+        def from_psum(dst, name, j, other, op):
+            views = runs(dst, j), in_psum(name, j), runs(other, j)
+            if j in WORD_TILES:
+                for u in range(2):
+                    nc.vector.tensor_tensor(views[0][:, u], views[1][:, u], views[2][:, u], op)
+            else:
+                nc.vector.tensor_tensor(views[0], views[1], views[2], op)
 
         held = {}
 
         def copy_out(name, j, dst):
             held[name, j] = dst
-            nc.scalar.copy(runs(dst), in_psum(name, j))
+            nc.scalar.copy(runs(dst, j), in_psum(name, j))
 
         def on_vector(key, j, op, dst):
             held[key, j] = dst
-            nc.vector.tensor_tensor(runs(dst), in_psum("c", j), runs(held["b", j]), op)
+            from_psum(dst, "c", j, held["b", j], op)
 
         def on_gpsimd(key, j, op, dst):
             held[key, j] = dst
@@ -183,7 +196,7 @@ def tile_list_fm_rating_kernel(
 
         def times_a(j, dst):
             held["q", j] = dst
-            nc.vector.tensor_tensor(runs(dst), in_psum("a", j), runs(held["s", j]), MULT)
+            from_psum(dst, "a", j, held["s", j], MULT)
 
         def turn(key, j, first):
             for t in range(4):
@@ -200,6 +213,15 @@ def tile_list_fm_rating_kernel(
         def round_h(j, dst):
             copy = nc.vector.tensor_copy if j == 6 else nc.scalar.copy
             copy(dst, banks["h", j][:].rearrange("p (t j) -> p j t", t=4))
+
+        def add_and_turn_words(j, slot, dst):
+            pairs = sbuf([H], BF16, "pairs%d" % j)
+            nc.vector.tensor_tensor(pairs[:], held["q", j], held["p", j], ADD)
+            open_bank(("h", j), slot)
+            for u in range(2):
+                cols = slice(u * P, (u + 1) * P)
+                nc.tensor.transpose(banks["h", j][:, cols], pairs[:].bitcast(F32)[:, cols], ident[:])
+            nc.scalar.copy(dst.bitcast(F32), banks["h", j][:, : 2 * P].rearrange("p (u j) -> p j u", u=2))
 
         out_v = out.rearrange("(h p) j -> p h j", p=P)
 
@@ -331,10 +353,14 @@ def tile_list_fm_rating_kernel(
 
         for j in range(TPC, TILES):
             times_a(j, last_room[j - TPC])
+        add_and_turn_words_later = 7
+        for j in (4, 5, 6):
             turn("q", j, False)
-            if j in (4, 5):
-                open_bank(("h", j + 2), (1, 3)[j - 4])
-                turn("p", j + 2, True)
+            if j == 4:
+                open_bank(("h", 6), 1)
+                turn("p", 6, True)
+            if j == 6:
+                add_and_turn_words(add_and_turn_words_later, 3, pair_slot(7))
             round_h(j, pair_slot(j))
         for j0, slots in ((4, (2, 5)), (6, (6, 7))):
             quantize_pair(j0)

@@ -20,11 +20,10 @@ IDENT = mybir.ActivationFunctionType.Identity
 
 P = 128
 PASSES = K // 512
-CHUNK = 512
-TILES = S // P
-TPC = CHUNK // P
-HALF = H // 2
-WORD_TILES = (7,)
+HALF = S // 2
+HALF_TILES = HALF // P
+ROW_BYTES = 4 * H
+PAIR_TILE = 7
 
 
 def tile_list_fm_rating_kernel(
@@ -36,12 +35,17 @@ def tile_list_fm_rating_kernel(
         placed = ctx.enter_context(tc.tile_pool(name="placed", bufs=1))
         psum = ctx.enter_context(tc.psum_pool(name="psum", bufs=1))
 
-        def sbuf(shape, dtype, name, tag=None):
-            return keep.tile([P] + shape, dtype, name=name, tag=tag or name, align_bytes=64)
+        def sbuf(shape, dtype, name, after=None):
+            return keep.tile([P] + shape, dtype, name=name, tag=after or name, align_bytes=64)
 
-        def rows_of(count, name, tag=None):
-            tile = sbuf([count * H], F32, name, tag)
+        def at(offset, shape, dtype, name):
+            return placed.tile([P] + shape, dtype, name=name, align_bytes=64, offset=offset)
+
+        def rows(tile, count):
             return [tile[:, n * H : (n + 1) * H] for n in range(count)]
+
+        def rows_of(count, name, after=None):
+            return rows(sbuf([count * H], F32, name, after), count)
 
         lists = {}
         for name in ("c", "b", "a"):
@@ -55,31 +59,29 @@ def tile_list_fm_rating_kernel(
         nc.vector.memset(wc_sc[:].rearrange("p a e -> p (a e)").bitcast(I32), 0)
         nc.vector.memset(c1_sc[:].bitcast(I32), 0)
 
-        tab_w = [sbuf([T], I32, "tab_w%d" % a) for a in range(PASSES)]
-        wi_w = [sbuf([H], I32, "wi_w%d" % a) for a in range(PASSES)]
-        wc_w = [sbuf([2 * H], U8, "wc_w%d" % a) for a in range(PASSES)]
-        def at(offset, shape, dtype, name):
-            return placed.tile([P] + shape, dtype, name=name, align_bytes=64, offset=offset)
-
-        raw = [sbuf([4, H], F32, "raw0"), at(2048, [4, H], F32, "raw1")]
+        tab_w = [sbuf([T], I32, "tab_w%d" % ps) for ps in range(PASSES)]
+        wi_w = [sbuf([H], I32, "wi_w%d" % ps) for ps in range(PASSES)]
+        wc_w = [sbuf([2 * H], U8, "wc_w%d" % ps) for ps in range(PASSES)]
+        wu_raw = [sbuf([4, H], F32, "wu_raw0"), at(ROW_BYTES, [4, H], F32, "wu_raw1")]
         bias_sb = keep.tile([P, 2], F32)
 
-        def load_table(a):
-            nc.sync.dma_start(tab_w[a][:], tab_words[a].rearrange("p t i -> p (t i)").bitcast(I32))
+        def load_table(ps):
+            nc.sync.dma_start(tab_w[ps][:], tab_words[ps].rearrange("p t i -> p (t i)").bitcast(I32))
 
-        def load_weight_words(a):
-            nc.sync.dma_start(wi_w[a][:], wi_words[a].rearrange("p e i -> p (e i)").bitcast(I32))
-            nc.sync.dma_start(wc_w[a][:].bitcast(I32), wc_words[a].bitcast(I32))
+        def load_weight_words(ps):
+            nc.sync.dma_start(wi_w[ps][:], wi_words[ps].rearrange("p e i -> p (e i)").bitcast(I32))
+            nc.sync.dma_start(wc_w[ps][:].bitcast(I32), wc_words[ps].bitcast(I32))
 
-        def load_wu(a):
-            nc.sync.dma_start(raw[a][:], wu[512 * a : 512 * (a + 1), :].rearrange("(p j) e -> p j e", j=4))
+        def load_wu(ps):
+            nc.sync.dma_start(wu_raw[ps][:], wu[512 * ps : 512 * (ps + 1), :].rearrange("(p t) e -> p t e", t=4))
 
         nc.sync.dma_start(lists["c"][:], offs3)
         nc.sync.dma_start(lists["b"][:], offs2)
         nc.sync.dma_start(lists["a"][:], offs)
-        for r in range(4):
-            for a in range(PASSES):
-                nc.sync.dma_start(tab_sc[4 * a + r : P : 32, :].bitcast(I32), tab_scales[a, r:16:4, :].bitcast(I32))
+        for m in range(4):
+            for ps in range(PASSES):
+                queue = (nc.sync, nc.scalar)[ps]
+                queue.dma_start(tab_sc[4 * ps + m : P : 32, :].bitcast(I32), tab_scales[ps, m:16:4, :].bitcast(I32))
         for q in range(4):
             nc.sync.dma_start(
                 wi_sc[32 * q : 32 * q + 8, :].bitcast(I32), wi_scales[:, 4 * q : 4 * q + 4, :].bitcast(I32)
@@ -96,273 +98,284 @@ def tile_list_fm_rating_kernel(
         load_weight_words(1)
         load_wu(1)
         wr_raw = sbuf([4, N], F32, "wr_raw")
-        wr_v = wr.rearrange("(q t i) n -> t q i n", t=4, i=8)
+        wr_rows = wr.rearrange("(g t i) n -> t g i n", t=4, i=8)
         for t in range(4):
-            nc.sync.dma_start(wr_raw[:, t, :], wr_v[t])
-
+            nc.sync.dma_start(wr_raw[:, t, :], wr_rows[t])
         with nc.allow_non_contiguous_dma(reason="one bias value a partition"):
             nc.sync.dma_start(bias_sb[:], bias.rearrange("(h p) -> p h", p=P))
 
         ident = keep.tile([P, P], F32)
         make_identity(nc, ident[:])
-        warm = keep.tile([P, 1], F32)
-        nc.scalar.activation(warm[:], ident[:, 0:1], IDENT)
 
-        sc = {}
-        words = {}
+        picked_sc = {}
+        picked_w = {}
 
         def gather_scales(name):
-            sc[name] = sbuf([S], U8, "sc_" + name)
-            nc.vector.tensor_copy(sc[name][:], tab_sc[:].indirect(lists[name][:]))
+            picked_sc[name] = sbuf([S], U8, "sc_" + name)
+            nc.vector.tensor_copy(picked_sc[name][:], tab_sc[:].indirect(lists[name][:]))
 
-        def gather_words(name, a, chunks, dst):
-            for n, ch in enumerate(chunks):
-                words[name, a, ch] = dst[:, n * CHUNK : (n + 1) * CHUNK]
-            c0 = CHUNK // 16 * chunks[0]
-            cols = slice(c0, c0 + len(chunks) * CHUNK // 16)
-            nc.vector.tensor_copy(dst, tab_w[a][:].bitcast(U32).indirect(lists[name][:, cols]))
+        def gather_words(name, ps, halves, dst):
+            for n, half in enumerate(halves):
+                picked_w[name, ps, half] = dst[:, n * HALF : (n + 1) * HALF]
+            first = HALF // 16 * halves[0]
+            cols = slice(first, first + len(halves) * HALF // 16)
+            nc.vector.tensor_copy(dst, tab_w[ps][:].bitcast(U32).indirect(lists[name][:, cols]))
 
         wu_w = sbuf([PASSES, H], U32, "wu_w")
         wu_sc = sbuf([PASSES, H], U8, "wu_sc")
         wu_bf = sbuf([PASSES * H, 4], BF16, "wu_bf")
 
-        def cast_weight(dst, rows):
-            nc.scalar.copy(dst.rearrange("p (c i) t -> p c t i", i=4), rows.rearrange("p t (c i) -> p c t i", i=4))
+        def cast_weight(dst, src):
+            nc.scalar.copy(dst.rearrange("p (c i) t -> p c t i", i=4), src.rearrange("p t (c i) -> p c t i", i=4))
 
         def quantize(codes, scales, values):
             nc.vector.quantize_mx(codes.bitcast(FP8X4), scales, values.rearrange("p e t -> p (e t)"))
 
         banks = {}
+        bank_tag = {}
 
-        def open_bank(key, slot):
-            banks[key] = psum.tile([P, H], F32, tag="bank%d" % slot, name="bank")
+        def open_bank(key, after, width=H):
+            bank_tag[key] = bank_tag.get(after, after)
+            banks[key] = psum.tile([P, width], F32, tag=bank_tag[key], name="bank")
 
-        def project_pass(name, j, a):
-            ch, c0 = j // TPC, (j % TPC) * P
+        def project_pass(name, j, ps):
+            half, first = j // HALF_TILES, (j % HALF_TILES) * P
             cols = slice(j * P, (j + 1) * P)
             if name == "a":
-                rhs, rhs_sc, lhs_sc = wu_w[:, a, :].bitcast(FP8X4), wu_sc[:, a, :], sc[name][4 * a :, cols]
+                rhs, rhs_sc = wu_w[:, ps, :].bitcast(FP8X4), wu_sc[:, ps, :]
+                lhs_sc = picked_sc[name][4 * ps :, cols]
             elif name == "b":
-                rhs, rhs_sc, lhs_sc = wi_w[a][:].bitcast(FP8X4), wi_sc[4 * a :, :], sc[name][4 * a :, cols]
+                rhs, rhs_sc = wi_w[ps][:].bitcast(FP8X4), wi_sc[4 * ps :, :]
+                lhs_sc = picked_sc[name][4 * ps :, cols]
             else:
-                rhs, rhs_sc = wc_w[a][:].bitcast(FP4X4), wc_sc[:, a, :]
-                lhs_sc = (sc["c"], c1_sc)[a][:, cols]
+                rhs, rhs_sc = wc_w[ps][:].bitcast(FP4X4), wc_sc[:, ps, :]
+                lhs_sc = (picked_sc["c"], c1_sc)[ps][:, cols]
             nc.tensor.matmul_mx(
                 banks[name, j][:],
-                lhsT=words[name, a, ch][:, c0 : c0 + P].bitcast(FP8X4),
+                lhsT=picked_w[name, ps, half][:, first : first + P].bitcast(FP8X4),
                 lhsT_scale=lhs_sc,
                 rhs=rhs,
                 rhs_scale=rhs_sc,
-                start=(a == 0),
-                stop=(a == PASSES - 1),
+                start=(ps == 0),
+                stop=(ps == PASSES - 1),
             )
 
-        def project(name, j, slot):
-            open_bank((name, j), slot)
-            for a in range(PASSES):
-                project_pass(name, j, a)
+        def project(name, j, after):
+            open_bank((name, j), after)
+            for ps in range(PASSES):
+                project_pass(name, j, ps)
 
         def in_psum(name, j):
-            if j in WORD_TILES:
-                return banks[name, j][:].rearrange("p (q u e i) -> p u q i e", u=2, e=2, i=8)
-            return banks[name, j][:].rearrange("p (q t i) -> p t q i", t=4, i=8)
+            if j == PAIR_TILE:
+                return banks[name, j][:].rearrange("p (g u e i) -> p u g i e", u=2, e=2, i=8)
+            return banks[name, j][:].rearrange("p (g t i) -> p t g i", t=4, i=8)
 
-        def runs(ap, j):
-            if j in WORD_TILES:
-                return ap.rearrange("p (u q i e) -> p u q i e", u=2, e=2, i=8)
-            return ap.rearrange("p (t q i) -> p t q i", t=4, i=8)
-
-        def from_psum(dst, name, j, other, op):
-            views = runs(dst, j), in_psum(name, j), runs(other, j)
-            if j in WORD_TILES:
-                for u in range(2):
-                    nc.vector.tensor_tensor(views[0][:, u], views[1][:, u], views[2][:, u], op)
-            else:
-                nc.vector.tensor_tensor(views[0], views[1], views[2], op)
+        def in_sbuf(row, j):
+            if j == PAIR_TILE:
+                return row.rearrange("p (u g i e) -> p u g i e", u=2, e=2, i=8)
+            return row.rearrange("p (t g i) -> p t g i", t=4, i=8)
 
         held = {}
 
         def copy_out(name, j, dst):
             held[name, j] = dst
-            nc.scalar.copy(runs(dst, j), in_psum(name, j))
+            nc.scalar.copy(in_sbuf(dst, j), in_psum(name, j))
 
-        def on_vector(key, j, op, dst):
-            held[key, j] = dst
-            from_psum(dst, "c", j, held["b", j], op)
+        def on_vector(name, j, op, dst):
+            held[name, j] = dst
+            nc.vector.tensor_tensor(in_sbuf(dst, j), in_psum("c", j), in_sbuf(held["b", j], j), op)
 
-        def on_gpsimd(key, j, op, dst):
-            held[key, j] = dst
+        def on_gpsimd(name, j, op, dst):
+            held[name, j] = dst
             nc.gpsimd.tensor_tensor(dst, held["c", j], held["b", j], op)
 
         def times_a(j, dst):
             held["q", j] = dst
-            from_psum(dst, "a", j, held["s", j], MULT)
+            q_view, a_view, s_view = in_sbuf(dst, j), in_psum("a", j), in_sbuf(held["s", j], j)
+            if j == PAIR_TILE:
+                for u in range(2):
+                    nc.vector.tensor_tensor(q_view[:, u], a_view[:, u], s_view[:, u], MULT)
+            else:
+                nc.vector.tensor_tensor(q_view, a_view, s_view, MULT)
 
-        def turn(key, j, first):
+        def turn(name, j):
             for t in range(4):
                 cols = slice(t * P, (t + 1) * P)
                 nc.tensor.matmul(
                     banks["h", j][:, cols],
-                    held[key, j][:, cols],
+                    held[name, j][:, cols],
                     ident[:],
-                    start=(first and t == 0),
-                    stop=(not first and t == 3),
+                    start=(name == "m" and t == 0),
+                    stop=(name == "q" and t == 3),
                     is_transpose=True,
                 )
 
-        def round_h(j, dst):
-            copy = nc.vector.tensor_copy if j == 6 else nc.scalar.copy
-            copy(dst, banks["h", j][:].rearrange("p (t j) -> p j t", t=4))
+        def turn_product(j, after):
+            open_bank(("h", j), after)
+            turn("m", j)
 
-        def add_and_turn_words(j, slot, dst):
-            pairs = sbuf([H], BF16, "pairs%d" % j)
-            nc.vector.tensor_tensor(pairs[:], held["q", j], held["p", j], ADD)
-            open_bank(("h", j), slot)
-            for u in range(2):
-                cols = slice(u * P, (u + 1) * P)
-                nc.tensor.transpose(banks["h", j][:, cols], pairs[:].bitcast(F32)[:, cols], ident[:])
-            nc.scalar.copy(dst.bitcast(F32), banks["h", j][:, : 2 * P].rearrange("p (u j) -> p j u", u=2))
+        def round_h(j):
+            nc.scalar.copy(h_slot(j), banks["h", j][:].rearrange("p (t j) -> p j t", t=4))
 
-        out_v = out.rearrange("(h p) j -> p h j", p=P)
+        out_halves = out.rearrange("(h p) j -> p h j", p=P)
 
-        def rate(j0, tiles, h, slot, on_scalar):
-            w = tiles * P
-            y_ps = psum.tile([P, w], F32, tag="bank%d" % slot, name="y_ps")
-            y_sb = sbuf([w], F32, "y_sb%d%d" % (j0, h))
-            cols = slice(N + j0 * P, N + j0 * P + w)
+        def rate(j0, tiles, half, after):
+            open_bank(("y", j0, half), after, tiles * P)
+            cols = slice(N + j0 * P, N + (j0 + tiles) * P)
             nc.tensor.matmul_mx(
-                y_ps[:],
-                lhsT=end_w[:, h * P : (h + 1) * P].bitcast(FP8X4),
-                lhsT_scale=end_sc[:, h * P : (h + 1) * P],
+                banks["y", j0, half][:],
+                lhsT=end_w[:, half * P : (half + 1) * P].bitcast(FP8X4),
+                lhsT_scale=end_sc[:, half * P : (half + 1) * P],
                 rhs=end_w[:, cols].bitcast(FP8X4),
                 rhs_scale=end_sc[:, cols],
                 start=True,
                 stop=True,
             )
+
+        def add_bias_and_store(j0, tiles, half, on_scalar, after=None):
+            y_sb = sbuf([tiles * P], F32, "y_sb%d%d" % (j0, half), after)
+            y_ps, bias_col = banks["y", j0, half][:], bias_sb[:, half : half + 1]
             if on_scalar:
-                nc.scalar.activation(y_sb[:], y_ps[:], IDENT, bias=bias_sb[:, h : h + 1])
+                nc.scalar.activation(y_sb[:], y_ps, IDENT, bias=bias_col)
             else:
-                nc.vector.tensor_scalar_add(y_sb[:], y_ps[:], bias_sb[:, h : h + 1])
-            nc.sync.dma_start(out_v[:, h, j0 * P : j0 * P + w], y_sb[:])
+                nc.vector.tensor_scalar_add(y_sb[:], y_ps, bias_col)
+            nc.sync.dma_start(out_halves[:, half, j0 * P : (j0 + tiles) * P], y_sb[:])
 
         gather_scales("c")
-        nc.gpsimd.dma_start(c1_sc[0:100, :].bitcast(I32), sc["c"][4:104, :].bitcast(I32))
+        nc.gpsimd.dma_start(c1_sc[0:100, :].bitcast(I32), picked_sc["c"][4:104, :].bitcast(I32))
         gather_scales("b")
         gather_scales("a")
         for name in ("a", "b", "c"):
             gather_words(name, 0, (0, 1), sbuf([S], U32, "w0_" + name)[:])
-        for n, name in enumerate(("b", "c")):
-            for j in range(TPC):
-                open_bank((name, j), TPC * n + j)
-                project_pass(name, j, 0)
-        for ch in range(2):
-            for name in ("b", "c"):
-                gather_words(name, 1, (ch,), sbuf([CHUNK], U32, "w1_%s%d" % (name, ch))[:])
         for name in ("b", "c"):
-            for j in range(TPC):
+            for j in range(HALF_TILES):
+                open_bank((name, j), "bank_%s%d" % (name, j))
+                project_pass(name, j, 0)
+        for half in range(2):
+            for name in ("b", "c"):
+                gather_words(name, 1, (half,), sbuf([HALF], U32, "w1_%s%d" % (name, half))[:])
+        for name in ("b", "c"):
+            for j in range(HALF_TILES):
                 project_pass(name, j, 1)
 
-        cast_weight(wu_bf[:, :H, :], raw[0][:])
+        cast_weight(wu_bf[:, :H, :], wu_raw[0][:])
         b_two = sbuf([H], F32, "b_two")
         early = rows_of(5, "early")
-        for name, j, dst in (
-            ("b", 0, early[0]),
-            ("b", 2, b_two[:]),
-            ("b", 3, early[4]),
-            ("c", 0, early[1]),
-            ("b", 1, early[2]),
-            ("c", 1, early[3]),
-        ):
-            copy_out(name, j, dst)
-        for name, j, slot in (("b", 4, 0), ("b", 5, 2), ("c", 4, 3), ("c", 5, 4), ("b", 6, 1), ("c", 6, 5)):
-            project(name, j, slot)
+        copy_out("b", 0, early[0])
+        copy_out("b", 2, b_two[:])
+        copy_out("b", 3, early[4])
+        copy_out("c", 0, early[1])
+        copy_out("b", 1, early[2])
+        copy_out("c", 1, early[3])
+        project("b", 4, ("b", 0))
+        project("b", 5, ("b", 2))
+        project("c", 4, ("b", 3))
+        project("c", 5, ("c", 0))
+        project("b", 6, ("b", 1))
+        project("c", 6, ("c", 1))
         s_zero = sbuf([H], F32, "s_zero", "w1_c0")
-        first_room = rows_of(4, "first_room")
+        first_rows = rows_of(4, "first_rows")
         on_gpsimd("s", 0, ADD, s_zero[:])
         on_gpsimd("s", 1, ADD, sbuf([H], F32, "s_one")[:])
         for j in (2, 3):
-            on_vector("s", j, ADD, first_room[2 * j - 4])
-            on_vector("p", j, MULT, first_room[2 * j - 3])
+            on_vector("s", j, ADD, first_rows[2 * j - 4])
+            on_vector("m", j, MULT, first_rows[2 * j - 3])
         for j in (2, 3):
-            open_bank(("h", j), j + 4)
-            turn("p", j, True)
-        a_early = sbuf([CHUNK], U32, "a_early", "b_two")
-        gather_words("a", 1, (0,), a_early[:])
-        cast_weight(wu_bf[:, H:, :], raw[1][:])
+            turn_product(j, ("c", j))
+
+        gather_words("a", 1, (0,), sbuf([HALF], U32, "w1_a0", "b_two")[:])
+        cast_weight(wu_bf[:, H:, :], wu_raw[1][:])
         quantize(wu_w[:].rearrange("p a e -> p (a e)"), wu_sc[:].rearrange("p a e -> p (a e)"), wu_bf[:])
-        b_four = at(2048, [H], F32, "b_four")
-        late_tile = at(4096, [5 * H], F32, "late")
-        late = [late_tile[:, n * H : (n + 1) * H] for n in range(5)]
-        for name, j, dst in (("b", 4, b_four[:]), ("b", 5, late[2]), ("b", 6, late[0]), ("c", 6, late[1])):
-            copy_out(name, j, dst)
-        for name, slot, dst in (("b", 0, late[3]), ("c", 2, late[4])):
-            project(name, 7, slot)
-            copy_out(name, 7, dst)
-        pair_bf = {j0: sbuf([2 * P, 4], BF16, "pair_bf%d" % j0) for j0 in (0, 2, 4, 6)}
+        b_four = at(ROW_BYTES, [H], F32, "b_four")
+        late = rows(at(2 * ROW_BYTES, [5 * H], F32, "late"), 5)
+        copy_out("b", 4, b_four[:])
+        copy_out("b", 5, late[2])
+        copy_out("b", 6, late[0])
+        copy_out("c", 6, late[1])
+        project("b", 7, ("b", 4))
+        copy_out("b", 7, late[3])
+        project("c", 7, ("b", 5))
+        copy_out("c", 7, late[4])
+        h_bf = {j0: sbuf([2 * P, 4], BF16, "h_bf%d" % j0) for j0 in (0, 2, 4, 6)}
 
-        def pair_slot(j):
-            return pair_bf[j - j % 2][:, (j % 2) * P : (j % 2 + 1) * P, :]
+        def h_slot(j):
+            return h_bf[j - j % 2][:, (j % 2) * P : (j % 2 + 1) * P, :]
 
-        room = rows_of(4, "room", "wu_bf")
+        gpsimd_rows = rows_of(4, "gpsimd_rows", "wu_bf")
         for j in (0, 1):
-            on_gpsimd("p", j, MULT, room[j])
+            on_gpsimd("m", j, MULT, gpsimd_rows[j])
         for j in (6, 7):
-            on_gpsimd("s", j, ADD, room[j - 4])
-        second_room = rows_of(9, "second_room")
-        on_vector("s", 4, ADD, second_room[0])
-        on_vector("p", 4, MULT, second_room[1])
-        wr_bf = at(1024, [N, 4], BF16, "wr_bf")
+            on_gpsimd("s", j, ADD, gpsimd_rows[j - 4])
+        second_rows = rows_of(9, "second_rows")
+        on_vector("s", 4, ADD, second_rows[0])
+        on_vector("m", 4, MULT, second_rows[1])
+        wr_bf = at(ROW_BYTES // 2, [N, 4], BF16, "wr_bf")
         cast_weight(wr_bf[:], wr_raw[:])
-        on_vector("s", 5, ADD, second_room[2])
-        on_vector("p", 5, MULT, second_room[3])
-        on_vector("p", 6, MULT, second_room[8])
-        for j, slot in ((2, 1), (3, 3), (0, 0), (1, 4)):
-            project("a", j, slot)
-        for j, slot in ((0, 2), (1, 5)):
-            open_bank(("h", j), slot)
-            turn("p", j, True)
+        on_vector("s", 5, ADD, second_rows[2])
+        on_vector("m", 5, MULT, second_rows[3])
+        on_vector("m", 6, MULT, second_rows[8])
+        project("a", 2, ("b", 6))
+        project("a", 3, ("c", 4))
+        project("a", 0, ("b", 7))
+        project("a", 1, ("c", 5))
+        turn_product(0, ("c", 7))
+        turn_product(1, ("c", 6))
         for j in (2, 3, 0, 1):
-            times_a(j, second_room[4 + j])
-            turn("q", j, False)
-            round_h(j, pair_slot(j))
-        for j in (4, 5):
-            open_bank(("h", j), (0, 4)[j - 4])
-            turn("p", j, True)
-        for j, slot in ((4, 1), (5, 3), (6, 6), (7, 7)):
-            open_bank(("a", j), slot)
+            times_a(j, second_rows[4 + j])
+            turn("q", j)
+            round_h(j)
+        turn_product(4, ("a", 0))
+        turn_product(5, ("a", 1))
+        last_tiles = (4, 5, PAIR_TILE, 6)
+        for j, after in zip(last_tiles, (("a", 2), ("a", 3), ("h", 2), ("h", 3))):
+            open_bank(("a", j), after)
             project_pass("a", j, 0)
 
-        gather_words("a", 1, (1,), sbuf([CHUNK], U32, "a_late", "w1_c0")[:])
-        for j in range(TPC, TILES):
+        gather_words("a", 1, (1,), sbuf([HALF], U32, "w1_a1", "w1_c0")[:])
+        for j in last_tiles:
             project_pass("a", j, 1)
 
         end_w = sbuf([N + S], U32, "end_w", "s_one")
         end_sc = sbuf([N + S], U8, "end_sc")
 
-        def quantize_pair(j0):
+        def quantize_h(j0):
             cols = slice(N + j0 * P, N + (j0 + 2) * P)
-            quantize(end_w[:, cols], end_sc[:, cols], pair_bf[j0][:])
+            quantize(end_w[:, cols], end_sc[:, cols], h_bf[j0][:])
 
         quantize(end_w[:, :N], end_sc[:, :N], wr_bf[:])
-        quantize_pair(2)
-        quantize_pair(0)
-        last_room = rows_of(5, "last_room", "pair_bf0")
-        on_gpsimd("p", 7, MULT, last_room[4])
-        rate(0, TPC, 0, 2, True)
-        rate(0, TPC, 1, 5, True)
+        quantize_h(2)
+        quantize_h(0)
 
-        for j in range(TPC, TILES):
-            times_a(j, last_room[j - TPC])
-        add_and_turn_words_later = 7
-        for j in (4, 5, 6):
-            turn("q", j, False)
-            if j == 4:
-                open_bank(("h", 6), 1)
-                turn("p", 6, True)
-            if j == 6:
-                add_and_turn_words(add_and_turn_words_later, 3, pair_slot(7))
-            round_h(j, pair_slot(j))
-        for j0, slots in ((4, (2, 5)), (6, (6, 7))):
-            quantize_pair(j0)
-            rate(j0, 2, 0, slots[0], True)
-            rate(j0, 2, 1, slots[1], False)
+        last_rows = rows_of(5, "last_rows", "h_bf0")
+        on_gpsimd("m", 7, MULT, last_rows[4])
+        rate(0, HALF_TILES, 0, ("h", 0))
+        rate(0, HALF_TILES, 1, ("h", 1))
+        add_bias_and_store(0, HALF_TILES, 0, True)
+        for j in last_tiles:
+            times_a(j, last_rows[j - HALF_TILES])
+        turn("q", 4)
+        turn_product(6, ("a", 4))
+        round_h(4)
+        turn("q", 5)
+        round_h(5)
+        turn("q", 6)
+        pairs = sbuf([H], BF16, "pairs")
+        nc.vector.tensor_tensor(pairs[:], held["q", PAIR_TILE], held["m", PAIR_TILE], ADD)
+        open_bank(("h", PAIR_TILE), ("a", 5))
+        for u in range(2):
+            cols = slice(u * P, (u + 1) * P)
+            nc.tensor.transpose(banks["h", PAIR_TILE][:, cols], pairs[:].bitcast(F32)[:, cols], ident[:])
+        round_h(6)
+        add_bias_and_store(0, HALF_TILES, 1, True, "pairs")
+        quantize_h(4)
+        rate(4, 2, 0, ("h", 4))
+        rate(4, 2, 1, ("h", 5))
+        nc.vector.tensor_copy(
+            h_slot(PAIR_TILE).bitcast(F32), banks["h", PAIR_TILE][:, : 2 * P].rearrange("p (u j) -> p j u", u=2)
+        )
+        quantize_h(6)
+        rate(6, 2, 0, ("a", PAIR_TILE))
+        rate(6, 2, 1, ("a", 6))
+        for j0 in (4, 6):
+            add_bias_and_store(j0, 2, 0, True)
+            add_bias_and_store(j0, 2, 1, False)

@@ -23,6 +23,7 @@ PASSES = K // 512
 HALF = S // 2
 HALF_TILES = HALF // P
 ROW_BYTES = 4 * H
+STAGE = 96
 PAIR_TILE = 7
 
 
@@ -51,13 +52,14 @@ def tile_list_fm_rating_kernel(
         for name in ("c", "b", "a"):
             lists[name] = keep.tile([P, S // 16], U16, name="list_" + name)
         tab_sc = sbuf([T], U8, "tab_sc")
+        planes = [sbuf([3 * S], U8, "planes%d" % ps) for ps in range(PASSES)]
         wi_sc = sbuf([H], U8, "wi_sc")
         wc_sc = sbuf([PASSES, H], U8, "wc_sc")
-        c1_sc = sbuf([S], U8, "c1_sc")
-        nc.vector.memset(tab_sc[:].bitcast(I32), 0)
         nc.vector.memset(wi_sc[:].bitcast(I32), 0)
         nc.vector.memset(wc_sc[:].rearrange("p a e -> p (a e)").bitcast(I32), 0)
-        nc.vector.memset(c1_sc[:].bitcast(I32), 0)
+        nc.vector.memset(tab_sc[0:STAGE, :].bitcast(I32), 0)
+        nc.vector.memset(planes[0][:].bitcast(I32), 0)
+        nc.gpsimd.memset(planes[1][:].bitcast(I32), 0)
 
         tab_w = [sbuf([T], I32, "tab_w%d" % ps) for ps in range(PASSES)]
         wi_w = [sbuf([H], I32, "wi_w%d" % ps) for ps in range(PASSES)]
@@ -75,26 +77,50 @@ def tile_list_fm_rating_kernel(
         def load_wu(ps):
             nc.sync.dma_start(wu_raw[ps][:], wu[512 * ps : 512 * (ps + 1), :].rearrange("(p t) e -> p t e", t=4))
 
-        nc.sync.dma_start(lists["c"][:], offs3)
-        nc.sync.dma_start(lists["b"][:], offs2)
-        nc.sync.dma_start(lists["a"][:], offs)
-        for m in range(4):
-            for ps in range(PASSES):
-                queue = (nc.sync, nc.scalar)[ps]
-                queue.dma_start(tab_sc[4 * ps + m : P : 32, :].bitcast(I32), tab_scales[ps, m:16:4, :].bitcast(I32))
-        for q in range(4):
+        def load_wi_scales(q):
             nc.sync.dma_start(
                 wi_sc[32 * q : 32 * q + 8, :].bitcast(I32), wi_scales[:, 4 * q : 4 * q + 4, :].bitcast(I32)
             )
-        load_table(0)
-        load_weight_words(0)
-        for q in range(4):
+
+        def load_wc_scales(q):
             nc.sync.dma_start(
                 wc_sc[32 * q : 32 * q + 4, :, :].bitcast(I32),
                 wc_scales[:, 4 * q : 4 * q + 4, :].rearrange("a r e -> r a e").bitcast(I32),
             )
+
+        nc.sync.dma_start(lists["c"][:], offs3)
+        nc.sync.dma_start(tab_sc[STAGE:P, :].bitcast(I32), tab_scales.rearrange("a q t -> (a q) t").bitcast(I32))
+        nc.sync.dma_start(lists["b"][:], offs2)
+        nc.sync.dma_start(lists["a"][:], offs)
+        for q in range(3):
+            load_wi_scales(q)
+        load_table(0)
+        load_wi_scales(3)
+        for q in range(4):
+            load_wc_scales(q)
+        load_weight_words(0)
         load_wu(0)
+
+        picked_rows = sbuf([3 * S], U8, "picked_rows")
+        for n, name in enumerate(("c", "b", "a")):
+            nc.vector.tensor_copy(picked_rows[:, n * S : (n + 1) * S], tab_sc[:].indirect(lists[name][:]))
+        picked_sc = {}
+        for n, name in enumerate(("c", "b", "a")):
+            for ps in range(PASSES):
+                first_row = 0 if name == "c" else 4 * ps
+                picked_sc[name, ps] = planes[ps][first_row:, n * S : (n + 1) * S]
+
+        def move_rows(ps, dst, first_row, cols):
+            for m in range(4):
+                first = STAGE + 16 * ps + m
+                nc.sync.dma_start(
+                    dst[first_row + m : P : 32, :].bitcast(I32), picked_rows[first : first + 13 : 4, cols].bitcast(I32)
+                )
+
+        move_rows(0, planes[0][:], 0, slice(0, 3 * S))
+        move_rows(1, planes[1][:, :S], 0, slice(0, S))
         load_table(1)
+        move_rows(1, planes[1][:, S:], 4, slice(S, 3 * S))
         load_weight_words(1)
         load_wu(1)
         wr_raw = sbuf([4, N], F32, "wr_raw")
@@ -107,12 +133,7 @@ def tile_list_fm_rating_kernel(
         ident = keep.tile([P, P], F32)
         make_identity(nc, ident[:])
 
-        picked_sc = {}
         picked_w = {}
-
-        def gather_scales(name):
-            picked_sc[name] = sbuf([S], U8, "sc_" + name)
-            nc.vector.tensor_copy(picked_sc[name][:], tab_sc[:].indirect(lists[name][:]))
 
         def gather_words(name, ps, halves, dst):
             for n, half in enumerate(halves):
@@ -123,7 +144,7 @@ def tile_list_fm_rating_kernel(
 
         wu_w = sbuf([PASSES, H], U32, "wu_w")
         wu_sc = sbuf([PASSES, H], U8, "wu_sc")
-        wu_bf = sbuf([PASSES * H, 4], BF16, "wu_bf")
+        wu_bf = [sbuf([H, 4], BF16, "wu_bf%d" % ps) for ps in range(PASSES)]
 
         def cast_weight(dst, src):
             nc.scalar.copy(dst.rearrange("p (c i) t -> p c t i", i=4), src.rearrange("p t (c i) -> p c t i", i=4))
@@ -143,13 +164,13 @@ def tile_list_fm_rating_kernel(
             cols = slice(j * P, (j + 1) * P)
             if name == "a":
                 rhs, rhs_sc = wu_w[:, ps, :].bitcast(FP8X4), wu_sc[:, ps, :]
-                lhs_sc = picked_sc[name][4 * ps :, cols]
+                lhs_sc = picked_sc[name, ps][:, cols]
             elif name == "b":
                 rhs, rhs_sc = wi_w[ps][:].bitcast(FP8X4), wi_sc[4 * ps :, :]
-                lhs_sc = picked_sc[name][4 * ps :, cols]
+                lhs_sc = picked_sc[name, ps][:, cols]
             else:
                 rhs, rhs_sc = wc_w[ps][:].bitcast(FP4X4), wc_sc[:, ps, :]
-                lhs_sc = (picked_sc["c"], c1_sc)[ps][:, cols]
+                lhs_sc = picked_sc[name, ps][:, cols]
             nc.tensor.matmul_mx(
                 banks[name, j][:],
                 lhsT=picked_w[name, ps, half][:, first : first + P].bitcast(FP8X4),
@@ -241,12 +262,10 @@ def tile_list_fm_rating_kernel(
                 nc.vector.tensor_scalar_add(y_sb[:], y_ps, bias_col)
             nc.sync.dma_start(out_halves[:, half, j0 * P : (j0 + tiles) * P], y_sb[:])
 
-        gather_scales("c")
-        nc.gpsimd.dma_start(c1_sc[0:100, :].bitcast(I32), picked_sc["c"][4:104, :].bitcast(I32))
-        gather_scales("b")
-        gather_scales("a")
         for name in ("a", "b", "c"):
             gather_words(name, 0, (0, 1), sbuf([S], U32, "w0_" + name)[:])
+        cast_weight(wu_bf[0][:], wu_raw[0][:])
+        quantize(wu_w[:, 0, :], wu_sc[:, 0, :], wu_bf[0][:])
         for name in ("b", "c"):
             for j in range(HALF_TILES):
                 open_bank((name, j), "bank_%s%d" % (name, j))
@@ -258,7 +277,6 @@ def tile_list_fm_rating_kernel(
             for j in range(HALF_TILES):
                 project_pass(name, j, 1)
 
-        cast_weight(wu_bf[:, :H, :], wu_raw[0][:])
         b_two = sbuf([H], F32, "b_two")
         early = rows_of(5, "early")
         copy_out("b", 0, early[0])
@@ -284,8 +302,8 @@ def tile_list_fm_rating_kernel(
             turn_product(j, ("c", j))
 
         gather_words("a", 1, (0,), sbuf([HALF], U32, "w1_a0", "b_two")[:])
-        cast_weight(wu_bf[:, H:, :], wu_raw[1][:])
-        quantize(wu_w[:].rearrange("p a e -> p (a e)"), wu_sc[:].rearrange("p a e -> p (a e)"), wu_bf[:])
+        cast_weight(wu_bf[1][:], wu_raw[1][:])
+        quantize(wu_w[:, 1, :], wu_sc[:, 1, :], wu_bf[1][:])
         b_four = at(ROW_BYTES, [H], F32, "b_four")
         late = rows(at(2 * ROW_BYTES, [5 * H], F32, "late"), 5)
         copy_out("b", 4, b_four[:])
@@ -301,7 +319,7 @@ def tile_list_fm_rating_kernel(
         def h_slot(j):
             return h_bf[j - j % 2][:, (j % 2) * P : (j % 2 + 1) * P, :]
 
-        gpsimd_rows = rows_of(4, "gpsimd_rows", "wu_bf")
+        gpsimd_rows = rows_of(4, "gpsimd_rows", "wu_bf1")
         for j in (0, 1):
             on_gpsimd("m", j, MULT, gpsimd_rows[j])
         for j in (6, 7):

@@ -52,27 +52,28 @@ def tile_list_fm_rating_kernel(
         for name in ("c", "b", "a"):
             lists[name] = keep.tile([P, S // 16], U16, name="list_" + name)
         tab_sc = sbuf([T], U8, "tab_sc")
-        planes = [sbuf([3 * S], U8, "planes%d" % ps) for ps in range(PASSES)]
+        cb_sc = [sbuf([2 * S], U8, "cb_sc%d" % ps) for ps in range(PASSES)]
+        a_sc = sbuf([S], U8, "a_sc")
         wi_sc = sbuf([H], U8, "wi_sc")
         wc_sc = sbuf([PASSES, H], U8, "wc_sc")
         nc.vector.memset(wi_sc[:].bitcast(I32), 0)
         nc.vector.memset(wc_sc[:].rearrange("p a e -> p (a e)").bitcast(I32), 0)
         nc.vector.memset(tab_sc[0:STAGE, :].bitcast(I32), 0)
-        nc.vector.memset(planes[0][:].bitcast(I32), 0)
-        nc.gpsimd.memset(planes[1][:].bitcast(I32), 0)
+        nc.vector.memset(cb_sc[0][:].bitcast(I32), 0)
+        nc.gpsimd.memset(cb_sc[1][:].bitcast(I32), 0)
+        nc.gpsimd.memset(a_sc[:].bitcast(I32), 0)
 
         tab_w = [sbuf([T], I32, "tab_w%d" % ps) for ps in range(PASSES)]
         wi_w = [sbuf([H], I32, "wi_w%d" % ps) for ps in range(PASSES)]
-        wc_w = [sbuf([2 * H], U8, "wc_w%d" % ps) for ps in range(PASSES)]
+        wc_w = sbuf([PASSES, 2 * H], U8, "wc_w")
         wu_raw = [sbuf([4, H], F32, "wu_raw0"), at(ROW_BYTES, [4, H], F32, "wu_raw1")]
         bias_sb = keep.tile([P, 2], F32)
 
         def load_table(ps):
             nc.sync.dma_start(tab_w[ps][:], tab_words[ps].rearrange("p t i -> p (t i)").bitcast(I32))
 
-        def load_weight_words(ps):
+        def load_wi_words(ps):
             nc.sync.dma_start(wi_w[ps][:], wi_words[ps].rearrange("p e i -> p (e i)").bitcast(I32))
-            nc.sync.dma_start(wc_w[ps][:].bitcast(I32), wc_words[ps].bitcast(I32))
 
         def load_wu(ps):
             nc.sync.dma_start(wu_raw[ps][:], wu[512 * ps : 512 * (ps + 1), :].rearrange("(p t) e -> p t e", t=4))
@@ -98,17 +99,17 @@ def tile_list_fm_rating_kernel(
         load_wi_scales(3)
         for q in range(4):
             load_wc_scales(q)
-        load_weight_words(0)
+        load_wi_words(0)
+        nc.sync.dma_start(wc_w[:].bitcast(I32), wc_words.rearrange("a p e -> p a e").bitcast(I32))
         load_wu(0)
 
         picked_rows = sbuf([3 * S], U8, "picked_rows")
         for n, name in enumerate(("c", "b", "a")):
             nc.vector.tensor_copy(picked_rows[:, n * S : (n + 1) * S], tab_sc[:].indirect(lists[name][:]))
         picked_sc = {}
-        for n, name in enumerate(("c", "b", "a")):
-            for ps in range(PASSES):
-                first_row = 0 if name == "c" else 4 * ps
-                picked_sc[name, ps] = planes[ps][first_row:, n * S : (n + 1) * S]
+        for ps in range(PASSES):
+            picked_sc["c", ps], picked_sc["b", ps] = cb_sc[ps][:, :S], cb_sc[ps][:, S:]
+            picked_sc["a", ps] = a_sc[4 * ps :, :]
 
         def move_rows(ps, dst, first_row, cols):
             for m in range(4):
@@ -117,12 +118,13 @@ def tile_list_fm_rating_kernel(
                     dst[first_row + m : P : 32, :].bitcast(I32), picked_rows[first : first + 13 : 4, cols].bitcast(I32)
                 )
 
-        move_rows(0, planes[0][:], 0, slice(0, 3 * S))
-        move_rows(1, planes[1][:, :S], 0, slice(0, S))
+        move_rows(0, cb_sc[0], 0, slice(0, 2 * S))
         load_table(1)
-        move_rows(1, planes[1][:, S:], 4, slice(S, 3 * S))
-        load_weight_words(1)
+        load_wi_words(1)
+        move_rows(1, cb_sc[1], 0, slice(0, 2 * S))
         load_wu(1)
+        for ps in range(PASSES):
+            move_rows(ps, a_sc, 4 * ps, slice(2 * S, 3 * S))
         wr_raw = sbuf([4, N], F32, "wr_raw")
         wr_rows = wr.rearrange("(g t i) n -> t g i n", t=4, i=8)
         for t in range(4):
@@ -169,7 +171,7 @@ def tile_list_fm_rating_kernel(
                 rhs, rhs_sc = wi_w[ps][:].bitcast(FP8X4), wi_sc[4 * ps :, :]
                 lhs_sc = picked_sc[name, ps][:, cols]
             else:
-                rhs, rhs_sc = wc_w[ps][:].bitcast(FP4X4), wc_sc[:, ps, :]
+                rhs, rhs_sc = wc_w[:, ps, :].bitcast(FP4X4), wc_sc[:, ps, :]
                 lhs_sc = picked_sc[name, ps][:, cols]
             nc.tensor.matmul_mx(
                 banks[name, j][:],

@@ -83,10 +83,9 @@ def tile_list_fm_rating_kernel(
                 wi_sc[32 * q : 32 * q + 8, :].bitcast(I32), wi_scales[:, 4 * q : 4 * q + 4, :].bitcast(I32)
             )
 
-        def load_wc_scales(q):
+        def load_wc_scales(m):
             nc.sync.dma_start(
-                wc_sc[32 * q : 32 * q + 4, :, :].bitcast(I32),
-                wc_scales[:, 4 * q : 4 * q + 4, :].rearrange("a r e -> r a e").bitcast(I32),
+                wc_sc[m:P:32, :, :].bitcast(I32), wc_scales[:, m:16:4, :].rearrange("a q e -> q a e").bitcast(I32)
             )
 
         nc.sync.dma_start(lists["c"][:], offs3)
@@ -100,31 +99,32 @@ def tile_list_fm_rating_kernel(
         for q in range(4):
             load_wc_scales(q)
         load_wi_words(0)
-        nc.sync.dma_start(wc_w[:].bitcast(I32), wc_words.rearrange("a p e -> p a e").bitcast(I32))
         load_wu(0)
+        nc.sync.dma_start(wc_w[:].bitcast(I32), wc_words.rearrange("a p e -> p a e").bitcast(I32))
 
-        picked_rows = sbuf([3 * S], U8, "picked_rows")
-        for n, name in enumerate(("c", "b", "a")):
-            nc.vector.tensor_copy(picked_rows[:, n * S : (n + 1) * S], tab_sc[:].indirect(lists[name][:]))
+        cb_rows = sbuf([2 * S], U8, "cb_rows")
+        a_rows = sbuf([S], U8, "a_rows")
+        for name, dst in (("c", cb_rows[:, :S]), ("b", cb_rows[:, S:]), ("a", a_rows[:])):
+            nc.vector.tensor_copy(dst, tab_sc[:].indirect(lists[name][:]))
         picked_sc = {}
         for ps in range(PASSES):
             picked_sc["c", ps], picked_sc["b", ps] = cb_sc[ps][:, :S], cb_sc[ps][:, S:]
             picked_sc["a", ps] = a_sc[4 * ps :, :]
 
-        def move_rows(ps, dst, first_row, cols):
+        def move_rows(ps, dst, first_row, picked):
             for m in range(4):
                 first = STAGE + 16 * ps + m
                 nc.sync.dma_start(
-                    dst[first_row + m : P : 32, :].bitcast(I32), picked_rows[first : first + 13 : 4, cols].bitcast(I32)
+                    dst[first_row + m : P : 32, :].bitcast(I32), picked[first : first + 13 : 4, :].bitcast(I32)
                 )
 
-        move_rows(0, cb_sc[0], 0, slice(0, 2 * S))
+        move_rows(0, cb_sc[0], 0, cb_rows)
         load_table(1)
         load_wi_words(1)
-        move_rows(1, cb_sc[1], 0, slice(0, 2 * S))
+        move_rows(1, cb_sc[1], 0, cb_rows)
         load_wu(1)
         for ps in range(PASSES):
-            move_rows(ps, a_sc, 4 * ps, slice(2 * S, 3 * S))
+            move_rows(ps, a_sc, 4 * ps, a_rows)
         wr_raw = sbuf([4, N], F32, "wr_raw")
         wr_rows = wr.rearrange("(g t i) n -> t g i n", t=4, i=8)
         for t in range(4):

@@ -188,38 +188,48 @@ def tile_list_fm_rating_kernel(
             for ps in range(PASSES):
                 project_pass(name, j, ps)
 
-        def in_psum(name, j):
-            if j == PAIR_TILE:
-                return banks[name, j][:].rearrange("p (g u e i) -> p u g i e", u=2, e=2, i=8)
-            return banks[name, j][:].rearrange("p (g t i) -> p t g i", t=4, i=8)
+        def by_r(row):
+            return row.rearrange("p (g t i) -> p g t i", t=4, i=8)
 
-        def in_sbuf(row, j):
-            if j == PAIR_TILE:
-                return row.rearrange("p (u g i e) -> p u g i e", u=2, e=2, i=8)
-            return row.rearrange("p (t g i) -> p t g i", t=4, i=8)
+        def by_t(row):
+            return row.rearrange("p (t g i) -> p g t i", t=4, i=8)
+
+        def by_pair(row):
+            return row.rearrange("p (u g i e) -> p u g i e", u=2, e=2, i=8)
+
+        def pairs_in(bank):
+            return bank.rearrange("p (g u e i) -> p u g i e", u=2, e=2, i=8)
 
         held = {}
 
+        def combine(engine, name, j, op, dst, left, right):
+            held[name, j] = dst
+            if name == "s" or j == PAIR_TILE:
+                engine.tensor_tensor(dst, left, right, op)
+            else:
+                engine.tensor_tensor(by_t(dst), by_r(left), by_r(right), op)
+
         def copy_out(name, j, dst):
             held[name, j] = dst
-            nc.scalar.copy(in_sbuf(dst, j), in_psum(name, j))
-
-        def on_vector(name, j, op, dst):
-            held[name, j] = dst
-            nc.vector.tensor_tensor(in_sbuf(dst, j), in_psum("c", j), in_sbuf(held["b", j], j), op)
+            if j == PAIR_TILE:
+                nc.scalar.copy(by_pair(dst), pairs_in(banks[name, j][:]))
+            else:
+                nc.scalar.copy(dst, banks[name, j][:])
 
         def on_gpsimd(name, j, op, dst):
-            held[name, j] = dst
-            nc.gpsimd.tensor_tensor(dst, held["c", j], held["b", j], op)
+            combine(nc.gpsimd, name, j, op, dst, held["c", j], held["b", j])
+
+        def on_vector(name, j, op, dst):
+            combine(nc.vector, name, j, op, dst, banks["c", j][:], held["b", j])
 
         def times_a(j, dst):
-            held["q", j] = dst
-            q_view, a_view, s_view = in_sbuf(dst, j), in_psum("a", j), in_sbuf(held["s", j], j)
             if j == PAIR_TILE:
+                held["q", j] = dst
+                a_view = pairs_in(banks["a", j][:])
                 for u in range(2):
-                    nc.vector.tensor_tensor(q_view[:, u], a_view[:, u], s_view[:, u], MULT)
+                    nc.vector.tensor_tensor(by_pair(dst)[:, u], a_view[:, u], by_pair(held["s", j])[:, u], MULT)
             else:
-                nc.vector.tensor_tensor(q_view, a_view, s_view, MULT)
+                combine(nc.vector, "q", j, MULT, dst, banks["a", j][:], held["s", j])
 
         def turn(name, j):
             for t in range(4):

@@ -60,8 +60,8 @@ def tile_list_fm_rating_kernel(
         nc.vector.memset(wc_sc[:].rearrange("p a e -> p (a e)").bitcast(I32), 0)
         nc.vector.memset(tab_sc[0:STAGE, :].bitcast(I32), 0)
         nc.vector.memset(cb_sc[0][:].bitcast(I32), 0)
-        nc.gpsimd.memset(cb_sc[1][:].bitcast(I32), 0)
-        nc.gpsimd.memset(a_sc[:].bitcast(I32), 0)
+        nc.vector.memset(cb_sc[1][:].bitcast(I32), 0)
+        nc.vector.memset(a_sc[:].bitcast(I32), 0)
 
         tab_w = [sbuf([T], I32, "tab_w%d" % ps) for ps in range(PASSES)]
         wi_w = [sbuf([H], I32, "wi_w%d" % ps) for ps in range(PASSES)]

@@ -310,8 +310,8 @@ def tile_list_fm_rating_kernel(
         for j in (2, 3):
             on_vector("s", j, ADD, first_rows[2 * j - 4])
             on_vector("m", j, MULT, first_rows[2 * j - 3])
-        for j in (2, 3):
-            turn_product(j, ("c", j))
+        project("b", 7, ("c", 2))
+        project("c", 7, ("c", 3))
 
         gather_words("a", 1, (0,), sbuf([HALF], U32, "w1_a0", "b_two")[:])
         cast_weight(wu_bf[1][:], wu_raw[1][:])
@@ -322,9 +322,7 @@ def tile_list_fm_rating_kernel(
         copy_out("b", 5, late[2])
         copy_out("b", 6, late[0])
         copy_out("c", 6, late[1])
-        project("b", 7, ("b", 4))
         copy_out("b", 7, late[3])
-        project("c", 7, ("b", 5))
         copy_out("c", 7, late[4])
         h_bf = {j0: sbuf([2 * P, 4], BF16, "h_bf%d" % j0) for j0 in (0, 2, 4, 6)}
 
@@ -344,12 +342,14 @@ def tile_list_fm_rating_kernel(
         on_vector("s", 5, ADD, second_rows[2])
         on_vector("m", 5, MULT, second_rows[3])
         on_vector("m", 6, MULT, second_rows[8])
-        project("a", 2, ("b", 6))
-        project("a", 3, ("c", 4))
-        project("a", 0, ("b", 7))
-        project("a", 1, ("c", 5))
-        turn_product(0, ("c", 7))
-        turn_product(1, ("c", 6))
+        project("a", 2, ("b", 4))
+        project("a", 3, ("b", 5))
+        project("a", 0, ("b", 6))
+        project("a", 1, ("c", 4))
+        turn_product(2, ("c", 5))
+        turn_product(3, ("b", 7))
+        turn_product(0, ("c", 6))
+        turn_product(1, ("c", 7))
         for j in (2, 3, 0, 1):
             times_a(j, second_rows[4 + j])
             turn("q", j)

from contextlib import ExitStack

import concourse.mybir as mybir
from concourse.masks import make_identity

K, T, S, H, N = 1024, 4096, 1024, 512, 256
FLOPS = 2 * (3 * K * H * S + H * N * S)

F32 = mybir.dt.float32
BF16 = mybir.dt.bfloat16
I32 = mybir.dt.int32
U32 = mybir.dt.uint32
U16 = mybir.dt.uint16
U8 = mybir.dt.uint8
FP8X4 = mybir.dt.float8_e4m3fn_x4
FP4X4 = mybir.dt.float4_e2m1fn_x4
ADD = mybir.AluOpType.add
MULT = mybir.AluOpType.mult
IDENT = mybir.ActivationFunctionType.Identity

P = 128
PASSES = K // 512
HALF = S // 2
HALF_TILES = HALF // P
ROW_BYTES = 4 * H
STAGE = 96
PAIR_TILE = 7


def tile_list_fm_rating_kernel(
    tc, tab_words, tab_scales, offs, offs2, offs3, wu, wi_words, wi_scales, wc_words, wc_scales, wr, bias, out
):
    nc = tc.nc
    with ExitStack() as ctx:
        keep = ctx.enter_context(tc.tile_pool(name="keep", bufs=1))
        placed = ctx.enter_context(tc.tile_pool(name="placed", bufs=1))
        psum = ctx.enter_context(tc.psum_pool(name="psum", bufs=1))

        def sbuf(shape, dtype, name, after=None):
            return keep.tile([P] + shape, dtype, name=name, tag=after or name, align_bytes=64)

        def at(offset, shape, dtype, name):
            return placed.tile([P] + shape, dtype, name=name, align_bytes=64, offset=offset)

        def rows(tile, count):
            return [tile[:, n * H : (n + 1) * H] for n in range(count)]

        def rows_of(count, name, after=None):
            return rows(sbuf([count * H], F32, name, after), count)

        lists = {}
        for name in ("c", "b", "a"):
            lists[name] = keep.tile([P, S // 16], U16, name="list_" + name)
        tab_sc = sbuf([T], U8, "tab_sc")
        cb_sc = [sbuf([2 * S], U8, "cb_sc%d" % ps) for ps in range(PASSES)]
        a_sc = sbuf([S], U8, "a_sc")
        wi_sc = sbuf([H], U8, "wi_sc")
        wc_sc = sbuf([PASSES, H], U8, "wc_sc")
        nc.vector.memset(wi_sc[:].bitcast(I32), 0)
        nc.vector.memset(wc_sc[:].rearrange("p a e -> p (a e)").bitcast(I32), 0)
        nc.vector.memset(tab_sc[0:STAGE, :].bitcast(I32), 0)
        nc.vector.memset(cb_sc[0][:].bitcast(I32), 0)
        nc.vector.memset(cb_sc[1][:].bitcast(I32), 0)
        nc.vector.memset(a_sc[:].bitcast(I32), 0)

        tab_w = [sbuf([T], I32, "tab_w%d" % ps) for ps in range(PASSES)]
        wi_w = [sbuf([H], I32, "wi_w%d" % ps) for ps in range(PASSES)]
        wc_w = sbuf([PASSES, 2 * H], U8, "wc_w")
        wu_raw = [sbuf([4, H], F32, "wu_raw0"), at(ROW_BYTES, [4, H], F32, "wu_raw1")]
        bias_sb = keep.tile([P, 2], F32)

        def load_table(ps):
            nc.sync.dma_start(tab_w[ps][:], tab_words[ps].rearrange("p t i -> p (t i)").bitcast(I32))

        def load_wi_words(ps):
            nc.sync.dma_start(wi_w[ps][:], wi_words[ps].rearrange("p e i -> p (e i)").bitcast(I32))

        def load_wu(ps):
            nc.sync.dma_start(wu_raw[ps][:], wu[512 * ps : 512 * (ps + 1), :].rearrange("(p t) e -> p t e", t=4))

        def load_wi_scales(q):
            nc.sync.dma_start(
                wi_sc[32 * q : 32 * q + 8, :].bitcast(I32), wi_scales[:, 4 * q : 4 * q + 4, :].bitcast(I32)
            )

        def load_wc_scales(m):
            nc.sync.dma_start(
                wc_sc[m:P:32, :, :].bitcast(I32), wc_scales[:, m:16:4, :].rearrange("a q e -> q a e").bitcast(I32)
            )

        nc.sync.dma_start(lists["c"][:], offs3)
        nc.sync.dma_start(tab_sc[STAGE:P, :].bitcast(I32), tab_scales.rearrange("a q t -> (a q) t").bitcast(I32))
        nc.sync.dma_start(lists["b"][:], offs2)
        nc.sync.dma_start(lists["a"][:], offs)
        for q in range(3):
            load_wi_scales(q)
        load_table(0)
        load_wi_scales(3)
        for q in range(4):
            load_wc_scales(q)
        load_wi_words(0)
        load_wu(0)
        nc.sync.dma_start(wc_w[:].bitcast(I32), wc_words.rearrange("a p e -> p a e").bitcast(I32))

        cb_rows = sbuf([2 * S], U8, "cb_rows")
        a_rows = sbuf([S], U8, "a_rows")
        for name, dst in (("c", cb_rows[:, :S]), ("b", cb_rows[:, S:]), ("a", a_rows[:])):
            nc.vector.tensor_copy(dst, tab_sc[:].indirect(lists[name][:]))
        picked_sc = {}
        for ps in range(PASSES):
            picked_sc["c", ps], picked_sc["b", ps] = cb_sc[ps][:, :S], cb_sc[ps][:, S:]
            picked_sc["a", ps] = a_sc[4 * ps :, :]

        def move_rows(ps, dst, first_row, picked):
            for m in range(4):
                first = STAGE + 16 * ps + m
                nc.sync.dma_start(
                    dst[first_row + m : P : 32, :].bitcast(I32), picked[first : first + 13 : 4, :].bitcast(I32)
                )

        move_rows(0, cb_sc[0], 0, cb_rows)
        load_table(1)
        load_wi_words(1)
        move_rows(1, cb_sc[1], 0, cb_rows)
        load_wu(1)
        for ps in range(PASSES):
            move_rows(ps, a_sc, 4 * ps, a_rows)
        wr_raw = sbuf([4, N], F32, "wr_raw")
        wr_rows = wr.rearrange("(g t i) n -> t g i n", t=4, i=8)
        for t in range(4):
            nc.sync.dma_start(wr_raw[:, t, :], wr_rows[t])
        with nc.allow_non_contiguous_dma(reason="one bias value a partition"):
            nc.sync.dma_start(bias_sb[:], bias.rearrange("(h p) -> p h", p=P))

        ident = keep.tile([P, P], F32)
        make_identity(nc, ident[:])

        picked_w = {}

        def gather_words(name, ps, halves, dst):
            for n, half in enumerate(halves):
                picked_w[name, ps, half] = dst[:, n * HALF : (n + 1) * HALF]
            first = HALF // 16 * halves[0]
            cols = slice(first, first + len(halves) * HALF // 16)
            nc.vector.tensor_copy(dst, tab_w[ps][:].bitcast(U32).indirect(lists[name][:, cols]))

        wu_w = sbuf([PASSES, H], U32, "wu_w")
        wu_sc = sbuf([PASSES, H], U8, "wu_sc")
        wu_bf = [sbuf([H, 4], BF16, "wu_bf%d" % ps) for ps in range(PASSES)]

        def cast_weight(dst, src):
            nc.scalar.copy(dst.rearrange("p (c i) t -> p c t i", i=4), src.rearrange("p t (c i) -> p c t i", i=4))

        def quantize(codes, scales, values):
            nc.vector.quantize_mx(codes.bitcast(FP8X4), scales, values.rearrange("p e t -> p (e t)"))

        banks = {}
        bank_tag = {}

        def open_bank(key, after, width=H):
            bank_tag[key] = bank_tag.get(after, after)
            banks[key] = psum.tile([P, width], F32, tag=bank_tag[key], name="bank")

        def project_pass(name, j, ps):
            half, first = j // HALF_TILES, (j % HALF_TILES) * P
            cols = slice(j * P, (j + 1) * P)
            if name == "a":
                rhs, rhs_sc = wu_w[:, ps, :].bitcast(FP8X4), wu_sc[:, ps, :]
                lhs_sc = picked_sc[name, ps][:, cols]
            elif name == "b":
                rhs, rhs_sc = wi_w[ps][:].bitcast(FP8X4), wi_sc[4 * ps :, :]
                lhs_sc = picked_sc[name, ps][:, cols]
            else:
                rhs, rhs_sc = wc_w[:, ps, :].bitcast(FP4X4), wc_sc[:, ps, :]
                lhs_sc = picked_sc[name, ps][:, cols]
            nc.tensor.matmul_mx(
                banks[name, j][:],
                lhsT=picked_w[name, ps, half][:, first : first + P].bitcast(FP8X4),
                lhsT_scale=lhs_sc,
                rhs=rhs,
                rhs_scale=rhs_sc,
                start=(ps == 0),
                stop=(ps == PASSES - 1),
            )

        def project(name, j, after):
            open_bank((name, j), after)
            for ps in range(PASSES):
                project_pass(name, j, ps)

        def by_r(row):
            return row.rearrange("p (g t i) -> p g t i", t=4, i=8)

        def by_t(row):
            return row.rearrange("p (t g i) -> p g t i", t=4, i=8)

        def by_pair(row):
            return row.rearrange("p (u g i e) -> p u g i e", u=2, e=2, i=8)

        def pairs_in(bank):
            return bank.rearrange("p (g u e i) -> p u g i e", u=2, e=2, i=8)

        held = {}

        def combine(engine, name, j, op, dst, left, right):
            held[name, j] = dst
            if name == "s" or j == PAIR_TILE:
                engine.tensor_tensor(dst, left, right, op)
            else:
                engine.tensor_tensor(by_t(dst), by_r(left), by_r(right), op)

        def copy_out(name, j, dst):
            held[name, j] = dst
            if j == PAIR_TILE:
                nc.scalar.copy(by_pair(dst), pairs_in(banks[name, j][:]))
            else:
                nc.scalar.copy(dst, banks[name, j][:])

        def on_gpsimd(name, j, op, dst):
            combine(nc.gpsimd, name, j, op, dst, held["c", j], held["b", j])

        def on_vector(name, j, op, dst):
            combine(nc.vector, name, j, op, dst, banks["c", j][:], held["b", j])

        def times_a(j, dst):
            if j == PAIR_TILE:
                held["q", j] = dst
                a_view = pairs_in(banks["a", j][:])
                for u in range(2):
                    nc.vector.tensor_tensor(by_pair(dst)[:, u], a_view[:, u], by_pair(held["s", j])[:, u], MULT)
            else:
                combine(nc.vector, "q", j, MULT, dst, banks["a", j][:], held["s", j])

        def turn(name, j):
            for t in range(4):
                cols = slice(t * P, (t + 1) * P)
                nc.tensor.matmul(
                    banks["h", j][:, cols],
                    held[name, j][:, cols],
                    ident[:],
                    start=(name == "m" and t == 0),
                    stop=(name == "q" and t == 3),
                    is_transpose=True,
                )

        def turn_product(j, after):
            open_bank(("h", j), after)
            turn("m", j)

        def round_h(j):
            nc.scalar.copy(h_slot(j), banks["h", j][:].rearrange("p (t j) -> p j t", t=4))

        out_halves = out.rearrange("(h p) j -> p h j", p=P)

        def rate(j0, tiles, half, after):
            open_bank(("y", j0, half), after, tiles * P)
            cols = slice(N + j0 * P, N + (j0 + tiles) * P)
            nc.tensor.matmul_mx(
                banks["y", j0, half][:],
                lhsT=end_w[:, half * P : (half + 1) * P].bitcast(FP8X4),
                lhsT_scale=end_sc[:, half * P : (half + 1) * P],
                rhs=end_w[:, cols].bitcast(FP8X4),
                rhs_scale=end_sc[:, cols],
                start=True,
                stop=True,
            )

        def add_bias_and_store(j0, tiles, half, on_scalar, after=None):
            y_sb = sbuf([tiles * P], F32, "y_sb%d%d" % (j0, half), after)
            y_ps, bias_col = banks["y", j0, half][:], bias_sb[:, half : half + 1]
            if on_scalar:
                nc.scalar.activation(y_sb[:], y_ps, IDENT, bias=bias_col)
            else:
                nc.vector.tensor_scalar_add(y_sb[:], y_ps, bias_col)
            nc.sync.dma_start(out_halves[:, half, j0 * P : (j0 + tiles) * P], y_sb[:])

        for name in ("a", "b", "c"):
            gather_words(name, 0, (0, 1), sbuf([S], U32, "w0_" + name)[:])
        cast_weight(wu_bf[0][:], wu_raw[0][:])
        quantize(wu_w[:, 0, :], wu_sc[:, 0, :], wu_bf[0][:])
        for name in ("b", "c"):
            for j in range(HALF_TILES):
                open_bank((name, j), "bank_%s%d" % (name, j))
                project_pass(name, j, 0)
        for half in range(2):
            for name in ("b", "c"):
                gather_words(name, 1, (half,), sbuf([HALF], U32, "w1_%s%d" % (name, half))[:])
        for name in ("b", "c"):
            for j in range(HALF_TILES):
                project_pass(name, j, 1)

        b_two = sbuf([H], F32, "b_two")
        early = rows_of(5, "early")
        copy_out("b", 0, early[0])
        copy_out("b", 2, b_two[:])
        copy_out("b", 3, early[4])
        copy_out("c", 0, early[1])
        copy_out("b", 1, early[2])
        copy_out("c", 1, early[3])
        project("b", 4, ("b", 0))
        project("b", 5, ("b", 2))
        project("c", 4, ("b", 3))
        project("c", 5, ("c", 0))
        project("b", 6, ("b", 1))
        project("c", 6, ("c", 1))
        s_zero = sbuf([H], F32, "s_zero", "w1_c0")
        first_rows = rows_of(4, "first_rows")
        on_gpsimd("s", 0, ADD, s_zero[:])
        on_gpsimd("s", 1, ADD, sbuf([H], F32, "s_one")[:])
        for j in (2, 3):
            on_vector("s", j, ADD, first_rows[2 * j - 4])
            on_vector("m", j, MULT, first_rows[2 * j - 3])
        project("b", 7, ("c", 2))
        project("c", 7, ("c", 3))

        gather_words("a", 1, (0,), sbuf([HALF], U32, "w1_a0", "b_two")[:])
        cast_weight(wu_bf[1][:], wu_raw[1][:])
        quantize(wu_w[:, 1, :], wu_sc[:, 1, :], wu_bf[1][:])
        b_four = at(ROW_BYTES, [H], F32, "b_four")
        late = rows(at(2 * ROW_BYTES, [5 * H], F32, "late"), 5)
        copy_out("b", 4, b_four[:])
        copy_out("b", 5, late[2])
        copy_out("b", 6, late[0])
        copy_out("c", 6, late[1])
        copy_out("b", 7, late[3])
        copy_out("c", 7, late[4])
        h_bf = {j0: sbuf([2 * P, 4], BF16, "h_bf%d" % j0) for j0 in (0, 2, 4, 6)}

        def h_slot(j):
            return h_bf[j - j % 2][:, (j % 2) * P : (j % 2 + 1) * P, :]

        gpsimd_rows = rows_of(4, "gpsimd_rows", "wu_bf1")
        for j in (0, 1):
            on_gpsimd("m", j, MULT, gpsimd_rows[j])
        for j in (6, 7):
            on_gpsimd("s", j, ADD, gpsimd_rows[j - 4])
        second_rows = rows_of(9, "second_rows")
        on_vector("s", 4, ADD, second_rows[0])
        on_vector("m", 4, MULT, second_rows[1])
        wr_bf = at(ROW_BYTES // 2, [N, 4], BF16, "wr_bf")
        cast_weight(wr_bf[:], wr_raw[:])
        on_vector("s", 5, ADD, second_rows[2])
        on_vector("m", 5, MULT, second_rows[3])
        on_vector("m", 6, MULT, second_rows[8])
        project("a", 2, ("b", 4))
        project("a", 3, ("b", 5))
        project("a", 0, ("b", 6))
        project("a", 1, ("c", 4))
        turn_product(2, ("c", 5))
        turn_product(3, ("b", 7))
        turn_product(0, ("c", 6))
        turn_product(1, ("c", 7))
        for j in (2, 3, 0, 1):
            times_a(j, second_rows[4 + j])
            turn("q", j)
            round_h(j)
        turn_product(4, ("a", 0))
        turn_product(5, ("a", 1))
        last_tiles = (4, 5, PAIR_TILE, 6)
        for j, after in zip(last_tiles, (("a", 2), ("a", 3), ("h", 2), ("h", 3))):
            open_bank(("a", j), after)
            project_pass("a", j, 0)

        gather_words("a", 1, (1,), sbuf([HALF], U32, "w1_a1", "w1_c0")[:])
        for j in last_tiles:
            project_pass("a", j, 1)

        end_w = sbuf([N + S], U32, "end_w", "s_one")
        end_sc = sbuf([N + S], U8, "end_sc")

        def quantize_h(j0):
            cols = slice(N + j0 * P, N + (j0 + 2) * P)
            quantize(end_w[:, cols], end_sc[:, cols], h_bf[j0][:])

        quantize(end_w[:, :N], end_sc[:, :N], wr_bf[:])
        quantize_h(2)
        quantize_h(0)

        last_rows = rows_of(5, "last_rows", "h_bf0")
        on_gpsimd("m", 7, MULT, last_rows[4])
        rate(0, HALF_TILES, 0, ("h", 0))
        rate(0, HALF_TILES, 1, ("h", 1))
        add_bias_and_store(0, HALF_TILES, 0, True)
        for j in last_tiles:
            times_a(j, last_rows[j - HALF_TILES])
        turn("q", 4)
        turn_product(6, ("a", 4))
        round_h(4)
        turn("q", 5)
        round_h(5)
        turn("q", 6)
        pairs = sbuf([H], BF16, "pairs")
        nc.vector.tensor_tensor(pairs[:], held["q", PAIR_TILE], held["m", PAIR_TILE], ADD)
        open_bank(("h", PAIR_TILE), ("a", 5))
        for u in range(2):
            cols = slice(u * P, (u + 1) * P)
            nc.tensor.transpose(banks["h", PAIR_TILE][:, cols], pairs[:].bitcast(F32)[:, cols], ident[:])
        round_h(6)
        add_bias_and_store(0, HALF_TILES, 1, True, "pairs")
        quantize_h(4)
        rate(4, 2, 0, ("h", 4))
        rate(4, 2, 1, ("h", 5))
        nc.vector.tensor_copy(
            h_slot(PAIR_TILE).bitcast(F32), banks["h", PAIR_TILE][:, : 2 * P].rearrange("p (u j) -> p j u", u=2)
        )
        quantize_h(6)
        rate(6, 2, 0, ("a", PAIR_TILE))
        rate(6, 2, 1, ("a", 6))
        for j0 in (4, 6):
            add_bias_and_store(j0, 2, 0, True)
            add_bias_and_store(j0, 2, 1, False)
